import numpy as np
import ml_dtypes


def mxq(x, axis, fmt="e4m3"):
    dtype, down = {"e4m3": (ml_dtypes.float8_e4m3fn, 7), "e5m2": (ml_dtypes.float8_e5m2, 14)}[fmt]
    v = np.moveaxis(np.asarray(x, np.float32).astype(ml_dtypes.bfloat16).astype(np.float64), axis, -1)
    blocks = v.reshape(v.shape[:-1] + (-1, 32))
    amax = np.abs(blocks).max(-1, keepdims=True)
    byte = np.maximum(np.where(amax > 0, np.frexp(amax)[1] - 1 + 127, 0) - down, 1)
    scale = np.exp2(byte - 127.0)
    codes = (blocks / scale).astype(np.float32).astype(dtype).astype(np.float64)
    return np.moveaxis((codes * scale).reshape(v.shape), -1, axis)


WIDE = False


def mx_kscale(k):
    if not WIDE:
        return np.ones(k)
    levels = np.array([10, -10, 5, -5, 0])
    if k % 512:
        return np.exp2(np.random.permutation(np.resize(levels, k // 32))).repeat(32)
    a = np.empty((k // 512, 16))
    for p in range(k // 512):
        a[p, :8] = np.random.permutation(np.resize(levels, 8))
        for g in range(8):
            far = levels[np.abs(levels - a[p, g]) >= 10]
            a[p, g + 8] = far[np.random.randint(len(far))]
    return np.exp2(a.ravel()).repeat(32)


BF16 = ml_dtypes.bfloat16


def bf(x):
    return np.asarray(x, np.float32).astype(BF16)


def f64(x):
    return np.asarray(x).astype(np.float64)


E2M1 = np.array([0.0, 0.5, 1.0, 1.5, 2.0, 3.0, 4.0, 6.0, -0.0, -0.5, -1.0, -1.5, -2.0, -3.0, -4.0, -6.0])


def pack_weight(w, fmt):
    k, n = w.shape
    w = f64(bf(w)).reshape(k // 32, 32, n)
    amax = np.abs(w).max(1)
    if fmt == "e4m3":
        byte = np.frexp(amax)[1] - 1 + 127 - 7
    else:
        mant, ex = np.frexp(amax / 6.0)
        byte = np.where(mant > 0.5, ex, ex - 1) + 127
    byte = np.clip(np.where(amax > 0, byte, 1), 1, 254)
    scaled = (w * np.exp2(127.0 - byte)[:, None, :]).reshape(k, n).astype(np.float32)
    by_word = np.ascontiguousarray(scaled.reshape(k // 512, 128, 4, n).transpose(0, 1, 3, 2))
    if fmt == "e4m3":
        words = by_word.astype(ml_dtypes.float8_e4m3fn).view(np.uint8)
    else:
        c = by_word.astype(ml_dtypes.float4_e2m1fn).view(np.uint8) & 0xF
        words = c[..., 0::2] | (c[..., 1::2] << 4)
    return np.ascontiguousarray(words), np.ascontiguousarray(byte.astype(np.uint8).reshape(k // 512, 16, n))


def unpack_weight(words, scales, fmt):
    g, p, n, _ = words.shape
    if fmt == "e4m3":
        vals = np.ascontiguousarray(words).view(ml_dtypes.float8_e4m3fn).astype(np.float64)
    else:
        nib = np.empty((g, p, n, 4), np.uint8)
        nib[..., 0::2] = words & 0xF
        nib[..., 1::2] = words >> 4
        vals = E2M1[nib]
    vals = vals * np.repeat(np.exp2(scales.astype(np.float64) - 127.0), 8, axis=1)[..., None]
    return vals.transpose(0, 1, 3, 2).reshape(g * 512, n)
def pack4(w):
    words, scales = pack_weight(w, "e2m1")
    return words.reshape(words.shape[0], 128, -1), scales


def unpack4(words, scales):
    return unpack_weight(words.reshape(words.shape[0], 128, -1, 2), scales, "e2m1")


E4M3FN = np.array([(-1.0 if i & 128 else 1.0) * ((1.0 + (i & 7) / 8.0) * 2.0 ** (((i >> 3) & 15) - 7) if i & 120 else (i & 7) * 2.0 ** -9) for i in range(256)])


def e4m3fn_bytes(y):
    return np.clip(np.asarray(y, np.float64), -448.0, 448.0).astype(np.float32).astype(ml_dtypes.float8_e4m3fn).view(np.uint8)


def e4m3fn_values(b):
    return E4M3FN[b]


N, O, V, B = 2048, 512, 1536, 128
FMAX = 448.0


def setup_inputs():
    s = mx_kscale(N)
    c = np.random.standard_normal((O, N)) / np.sqrt(N) * s
    c_scale = (np.abs(c).reshape(O, N // B, B).max(axis=2) / FMAX).astype(np.float32)
    c_bytes = e4m3fn_bytes(c / np.repeat(f64(c_scale), B, axis=1))
    a = np.random.standard_normal((N, N))
    fock = (a + a.T) / np.sqrt(2.0)
    v = np.random.standard_normal((N, V)) / np.sqrt(N) * s[:, None]
    v_words, v_scales = pack4(v)
    return {"c_bytes": c_bytes,
            "c_scale": c_scale,
            "fock": bf(fock / s[:, None] / s),
            "occ": bf(np.random.uniform(0.5, 2.0, (O,))),
            "v_words": v_words,
            "v_scales": v_scales}


def reference(c_bytes, c_scale, fock, occ, v_words, v_scales):
    c = e4m3fn_values(c_bytes) * np.repeat(f64(c_scale), B, axis=1)
    cq = mxq(c, 1, "e4m3")
    half = (cq @ mxq(f64(fock), 0, "e4m3")) * f64(occ)[:, None]
    hq = mxq(half, 1, "e4m3")
    f_oo = hq @ cq.T
    f_ov = hq @ unpack4(v_words, v_scales)
    return f_oo, f_ov

@@ -1,0 +1,275 @@
+from contextlib import ExitStack
+
+import concourse.mybir as mybir
+from concourse.masks import make_identity
+
+F32 = mybir.dt.float32
+BF16 = mybir.dt.bfloat16
+I32 = mybir.dt.int32
+U32 = mybir.dt.uint32
+U8 = mybir.dt.uint8
+FP8 = mybir.dt.float8_e4m3fn
+FP8X4 = mybir.dt.float8_e4m3fn_x4
+FP4X4 = mybir.dt.float4_e2m1fn_x4
+COPY = mybir.ActivationFunctionType.Copy
+MULT = mybir.AluOpType.mult
+
+P = 128
+N, O, V = 2048, 512, 1536
+G = N // 512
+OT = O // P
+B = 128
+
+SPLIT = (64,) * 4 + (76,) * 4 + (92,) * 4 + (100,) * 4
+WIDEN_S = (6, 6, 6, 6)
+UNTANGLE_V = ((0, 0), (1, 0), (2, 0), (3, 0))
+
+FLOPS = 2 * O * N * N + 2 * O * N * (O + V)
+
+
+def tile_fock_orbital_blocks_d4_kernel(tc, c_bytes, c_scale, fock, occ, v_words, v_scales, f_oo, f_ov):
+    nc = tc.nc
+    with ExitStack() as ctx:
+        keep = ctx.enter_context(tc.tile_pool(name="keep", bufs=1))
+        raw_pool = ctx.enter_context(tc.tile_pool(name="raw", bufs=16))
+        grp_pool = ctx.enter_context(tc.tile_pool(name="grp", bufs=5))
+        code_pool = ctx.enter_context(tc.tile_pool(name="code", bufs=10))
+        half_pool = ctx.enter_context(tc.tile_pool(name="half", bufs=2))
+        out_pool = ctx.enter_context(tc.tile_pool(name="outs", bufs=8))
+        psum = ctx.enter_context(tc.psum_pool(name="psum", bufs=1))
+
+        def bank(i):
+            return psum.tile([P, 512], F32, name=f"bank{i}", tag=f"bank{i}")
+
+        ident = keep.tile([P, P], F32, name="ident")
+        scale_sb = keep.tile([P, OT, N // B], F32, name="scale_sb")
+        occ_sb = keep.tile([P, O], BF16, name="occ_sb")
+        c_raw = [keep.tile([P, N], U8, name=f"c_raw{a}") for a in range(OT)]
+        c_wide = keep.tile([P, OT, N], BF16, name="c_wide", align_bytes=64)
+        c_grp = keep.tile([P, G, O, 4], BF16, name="c_grp", align_bytes=64)
+        c_codes = keep.tile([P, G, O], U32, name="c_codes", align_bytes=64)
+        c_planes = keep.tile([P, G, O], U8, name="c_planes", align_bytes=64)
+        h_codes = keep.tile([P, G, O], U32, name="h_codes", align_bytes=64)
+        h_planes = keep.tile([P, G, O], U8, name="h_planes", align_bytes=64)
+        v_sb = keep.tile([P, G, 2 * V], U8, name="v_sb", align_bytes=64)
+        v_planes = keep.tile([P, G, V], U8, name="v_planes", align_bytes=64)
+
+        ctx.enter_context(tc.manual_schedule())
+
+        nc.scalar.dma_start(out=scale_sb[:], in_=c_scale.rearrange("(a p) b -> p a b", p=P))
+        for a in range(OT):
+            nc.sync.dma_start(out=c_raw[a][:], in_=c_bytes[a * P : (a + 1) * P, :])
+        make_identity(nc, ident[:])
+        nc.gpsimd.memset(v_planes[:].rearrange("p g n -> p (g n)").bitcast(U32), 0)
+        raws = {}
+
+        def load_fock(g):
+            for k in range(G):
+                raw = raw_pool.tile([P, 4, 512], BF16, name="raw")
+                nc.sync.dma_start(
+                    out=raw[:],
+                    in_=fock[k * 512 : (k + 1) * 512, g * 512 : (g + 1) * 512].rearrange("(p j) n -> p j n", j=4),
+                )
+                raws[g, k] = raw
+
+        load_fock(0)
+        nc.sync.dma_start(out=occ_sb[:], in_=occ.partition_broadcast(P))
+        load_fock(1)
+        for q in range(4):
+            nc.sync.dma_start(
+                out=v_planes[32 * q : 32 * q + 4, :, :].bitcast(I32),
+                in_=v_scales[:, 4 * q : 4 * q + 4, :].rearrange("g r n -> r g n").bitcast(I32),
+            )
+        nc.sync.dma_start(out=v_sb[:].bitcast(I32), in_=v_words.rearrange("g p n -> p g n").bitcast(I32))
+        load_fock(2)
+        load_fock(3)
+
+        def widen(a):
+            for b in range(N // B):
+                src = c_raw[a][:, b * B : (b + 1) * B].bitcast(FP8)
+                dst = c_wide[:, a, b * B : (b + 1) * B]
+                if b * WIDEN_S[a] // 16 != (b + 1) * WIDEN_S[a] // 16:
+                    nc.scalar.activation(dst, src, COPY, scale=scale_sb[:, a, b : b + 1])
+                else:
+                    nc.vector.tensor_scalar(dst, src, scale_sb[:, a, b : b + 1], None, MULT)
+
+        turned = {}
+
+        def turn(a):
+            words = c_wide[:, a, :].bitcast(F32)
+            for h in range(2):
+                xt = bank(2 * a + h)
+                for gi in range(2):
+                    for u in range(2):
+                        g = 2 * h + gi
+                        col = 256 * gi + 128 * u
+                        nc.tensor.transpose(xt[:, col : col + P], words[:, 256 * g + u : 256 * (g + 1) : 2], ident[:])
+                turned[a, h] = xt
+
+        def untangle(a):
+            for h in range(2):
+                out = c_grp[:, 2 * h : 2 * h + 2, a * P : (a + 1) * P, :].rearrange("p g r j -> p g (r j)").bitcast(F32)
+                out = out.rearrange("p g (r u) -> p g r u", u=2)
+                in_ = turned[a, h][:].rearrange("p (g u r) -> p g r u", g=2, u=2)
+                if (a, h) in UNTANGLE_V:
+                    nc.vector.tensor_copy(out=out, in_=in_)
+                else:
+                    nc.scalar.copy(out, in_)
+
+        def quantise_c(g):
+            nc.vector.quantize_mx(
+                out=c_codes[:, g, :].bitcast(FP8X4),
+                scales=c_planes[:, g, :],
+                in_=c_grp[:, g, :, :].rearrange("p o j -> p (o j)"),
+            )
+
+        grps, f_codes, f_planes = {}, {}, {}
+
+        def interleave(s):
+            g, k = divmod(s, 4)
+            grp = grp_pool.tile([P, 4, P, 4], BF16, name="grp", align_bytes=64)
+            src = raws[g, k][:].rearrange("p j (m t) -> p m j t", t=4)
+            dst = grp[:].rearrange("p t m j -> p m j t")
+            cut = SPLIT[s]
+            nc.scalar.copy(dst[:, :cut], src[:, :cut])
+            nc.vector.tensor_copy(out=dst[:, cut:], in_=src[:, cut:])
+            grps[s] = grp
+
+        def quantise_fock(s):
+            codes = code_pool.tile([P, 512], U32, name="f_codes", align_bytes=64)
+            planes = code_pool.tile([P, 512], U8, name="f_planes", align_bytes=64)
+            nc.vector.quantize_mx(
+                out=codes[:].bitcast(FP8X4), scales=planes[:], in_=grps[s][:].rearrange("p t m j -> p (t m j)")
+            )
+            f_codes[s], f_planes[s] = codes, planes
+
+        s1_banks, h_grp = {}, {}
+
+        def stage1(i):
+            g, a = divmod(i, OT)
+            acc = bank(i % 2)
+            for t in range(4):
+                for k in range(G):
+                    nc.tensor.matmul_mx(
+                        out=acc[:, t * P : (t + 1) * P],
+                        lhsT=f_codes[4 * g + k][:, t * P : (t + 1) * P].bitcast(FP8X4),
+                        lhsT_scale=f_planes[4 * g + k][:, t * P : (t + 1) * P],
+                        rhs=c_codes[:, k, a * P : (a + 1) * P].bitcast(FP8X4),
+                        rhs_scale=c_planes[:, k, a * P : (a + 1) * P],
+                        start=(k == 0),
+                        stop=(k == G - 1),
+                    )
+            s1_banks[i] = acc
+
+        def weigh(i):
+            g, a = divmod(i, OT)
+            if a == 0:
+                h_grp[g] = half_pool.tile([P, O, 4], BF16, name="h_grp", align_bytes=64)
+            nc.vector.tensor_tensor(
+                out=h_grp[g][:, a * P : (a + 1) * P, :].rearrange("p (b i) t -> p b t i", i=4),
+                in0=s1_banks[i][:].rearrange("p (t b i) -> p b t i", t=4, i=4),
+                in1=occ_sb[:, a * P : (a + 1) * P].rearrange("p (b i) -> p b i", i=4).unsqueeze(2).to_broadcast([P, 32, 4, 4]),
+                op=MULT,
+            )
+
+        def quantise_half(i):
+            g, a = divmod(i, OT)
+            cols = slice(a * P, (a + 1) * P)
+            nc.vector.quantize_mx(
+                out=h_codes[:, g, cols].bitcast(FP8X4),
+                scales=h_planes[:, g, cols],
+                in_=h_grp[g][:, cols, :].rearrange("p o j -> p (o j)"),
+            )
+
+        def pass2(acc, g, a, n, start, stop, cols=slice(0, 512)):
+            if n == 0:
+                rhs, rhs_scale = c_codes[:, g, cols].bitcast(FP8X4), c_planes[:, g, cols]
+            else:
+                rhs = v_sb[:, g, (n - 1) * 1024 : n * 1024].bitcast(FP4X4)
+                rhs_scale = v_planes[:, g, (n - 1) * 512 : n * 512]
+            nc.tensor.matmul_mx(
+                out=acc,
+                lhsT=h_codes[:, g, a * P : (a + 1) * P].bitcast(FP8X4),
+                lhsT_scale=h_planes[:, g, a * P : (a + 1) * P],
+                rhs=rhs,
+                rhs_scale=rhs_scale,
+                start=start,
+                stop=stop,
+            )
+
+        early = [(a, 0) for a in range(3)] + [(a, 1) for a in range(3)]
+        early_acc = {}
+
+        def stage2(i):
+            g, a = divmod(i, OT)
+            for e, (ea, en) in enumerate(early):
+                if ea == a:
+                    if g == 0:
+                        early_acc[e] = bank(2 + e)
+                    pass2(early_acc[e][:], g, ea, en, g == 0, g == G - 1)
+
+        flip = [0]
+
+        def store(acc, a, n, cols=slice(0, 512)):
+            res = out_pool.tile([P, 512], F32, name="res")[:, cols]
+            acc = acc[:, cols]
+            if flip[0] % 2 == 0:
+                nc.vector.tensor_copy(out=res, in_=acc)
+            else:
+                nc.scalar.copy(res, acc)
+            flip[0] += 1
+            rows = slice(a * P, (a + 1) * P)
+            dst = f_oo[rows, cols] if n == 0 else f_ov[rows, (n - 1) * 512 : n * 512]
+            nc.sync.dma_start(out=dst, in_=res)
+
+        widen(0)
+        turn(0)
+        widen(1)
+        turn(1)
+        untangle(0)
+        widen(2)
+        turn(2)
+        untangle(1)
+        widen(3)
+        turn(3)
+        untangle(2)
+        interleave(0)
+        untangle(3)
+        for g in range(G):
+            quantise_c(g)
+
+        last = 4 * G
+        for s in range(1, last + 6):
+            if 0 <= s - 6 < last:
+                weigh(s - 6)
+            if s < last:
+                interleave(s)
+            if s - 1 < last:
+                quantise_fock(s - 1)
+            if 0 <= s - 6 < last:
+                quantise_half(s - 6)
+            if 0 <= s - 5 < last:
+                stage1(s - 5)
+            if 0 <= s - 7 < last:
+                stage2(s - 7)
+        late = [(a, n) for n in (1, 2, 3) for a in range(OT) if (a, n) not in early]
+        acc = bank(0)
+        a, n = late[0]
+        for g in range(G - 1):
+            pass2(acc[:], g, a, n, g == 0, False)
+        stage2(last - 1)
+        pass2(acc[:], G - 1, a, n, False, True)
+        for e, (ea, en) in enumerate(early):
+            store(early_acc[e], ea, en)
+        store(acc, a, n)
+        for j, (a, n) in enumerate(late[1:]):
+            acc = bank((j + 1) % 8)
+            for g in range(G):
+                pass2(acc[:], g, a, n, g == 0, g == G - 1)
+            store(acc, a, n)
+        for h in range(2):
+            cols = slice(256 * h, 256 * h + 256)
+            acc = bank((len(late) + h) % 8)
+            for g in range(G):
+                pass2(acc[:, cols], g, OT - 1, 0, g == 0, g == G - 1, cols)
+            store(acc, OT - 1, 0, cols)

@@ -16,13 +16,16 @@ MULT = mybir.AluOpType.mult
 
 P = 128
 N, O, V = 2048, 512, 1536
-G = N // 512
+W = 512
+G = N // W
 OT = O // P
 B = 128
+STEPS = G * G
 
-SPLIT = (64,) * 4 + (76,) * 4 + (92,) * 4 + (100,) * 4
-WIDEN_S = (6, 6, 6, 6)
-UNTANGLE_V = ((0, 0), (1, 0), (2, 0), (3, 0))
+SHARE_HEAD = 36
+SHARE = 42
+SHARE_LAST = 10
+WIDEN_S = 6
 
 FLOPS = 2 * O * N * N + 2 * O * N * (O + V)
 
@@ -31,245 +34,293 @@ def tile_fock_orbital_blocks_d4_kernel(tc, c_bytes, c_scale, fock, occ, v_words,
     nc = tc.nc
     with ExitStack() as ctx:
         keep = ctx.enter_context(tc.tile_pool(name="keep", bufs=1))
-        raw_pool = ctx.enter_context(tc.tile_pool(name="raw", bufs=16))
-        grp_pool = ctx.enter_context(tc.tile_pool(name="grp", bufs=5))
-        code_pool = ctx.enter_context(tc.tile_pool(name="code", bufs=10))
-        half_pool = ctx.enter_context(tc.tile_pool(name="half", bufs=2))
+        raw_pool = ctx.enter_context(tc.tile_pool(name="raw", bufs=STEPS))
+        grp_pool = ctx.enter_context(tc.tile_pool(name="grp", bufs=6))
+        code_pool = ctx.enter_context(tc.tile_pool(name="code", bufs=6))
+        wide_pool = ctx.enter_context(tc.tile_pool(name="wide", bufs=8))
+        turn_pool = ctx.enter_context(tc.tile_pool(name="turn", bufs=2))
         out_pool = ctx.enter_context(tc.tile_pool(name="outs", bufs=8))
         psum = ctx.enter_context(tc.psum_pool(name="psum", bufs=1))
 
         def bank(i):
-            return psum.tile([P, 512], F32, name=f"bank{i}", tag=f"bank{i}")
+            return psum.tile([P, W], F32, name=f"bank{i}", tag=f"bank{i}")
 
         ident = keep.tile([P, P], F32, name="ident")
         scale_sb = keep.tile([P, OT, N // B], F32, name="scale_sb")
-        occ_sb = keep.tile([P, O], BF16, name="occ_sb")
-        c_raw = [keep.tile([P, N], U8, name=f"c_raw{a}") for a in range(OT)]
-        c_wide = keep.tile([P, OT, N], BF16, name="c_wide", align_bytes=64)
-        c_grp = keep.tile([P, G, O, 4], BF16, name="c_grp", align_bytes=64)
-        c_codes = keep.tile([P, G, O], U32, name="c_codes", align_bytes=64)
-        c_planes = keep.tile([P, G, O], U8, name="c_planes", align_bytes=64)
-        h_codes = keep.tile([P, G, O], U32, name="h_codes", align_bytes=64)
-        h_planes = keep.tile([P, G, O], U8, name="h_planes", align_bytes=64)
+        occ_sb = keep.tile([P, OT], BF16, name="occ_sb")
+        occ_f32 = keep.tile([P, OT], F32, name="occ_f32")
+        c_raw = [keep.tile([P, OT, W], U8, name=f"c_raw{g}") for g in range(G)]
+        c_codes = [keep.tile([P, O], U32, name=f"c_codes{g}", align_bytes=64) for g in range(G)]
+        c_planes = [keep.tile([P, O], U8, name=f"c_planes{g}", align_bytes=64) for g in range(G)]
+        h_codes = [keep.tile([P, O], U32, name=f"h_codes{g}", align_bytes=64) for g in range(G)]
+        h_planes = [keep.tile([P, O], U8, name=f"h_planes{g}", align_bytes=64) for g in range(G)]
         v_sb = keep.tile([P, G, 2 * V], U8, name="v_sb", align_bytes=64)
         v_planes = keep.tile([P, G, V], U8, name="v_planes", align_bytes=64)
 
         ctx.enter_context(tc.manual_schedule())
 
-        nc.scalar.dma_start(out=scale_sb[:], in_=c_scale.rearrange("(a p) b -> p a b", p=P))
-        for a in range(OT):
-            nc.sync.dma_start(out=c_raw[a][:], in_=c_bytes[a * P : (a + 1) * P, :])
-        make_identity(nc, ident[:])
-        nc.gpsimd.memset(v_planes[:].rearrange("p g n -> p (g n)").bitcast(U32), 0)
+        nc.scalar.dma_start(out=scale_sb[:], in_=c_scale.rearrange("(p a) b -> p a b", a=OT))
         raws = {}
 
-        def load_fock(g):
-            for k in range(G):
-                raw = raw_pool.tile([P, 4, 512], BF16, name="raw")
-                nc.sync.dma_start(
-                    out=raw[:],
-                    in_=fock[k * 512 : (k + 1) * 512, g * 512 : (g + 1) * 512].rearrange("(p j) n -> p j n", j=4),
-                )
-                raws[g, k] = raw
+        def load_fock(s):
+            g, k = divmod(s, G)
+            raw = raw_pool.tile([P, 4, W], BF16, name="raw")
+            nc.sync.dma_start(
+                out=raw[:], in_=fock[k * W : (k + 1) * W, g * W : (g + 1) * W].rearrange("(p j) n -> p j n", j=4)
+            )
+            raws[s] = raw
 
-        load_fock(0)
-        nc.sync.dma_start(out=occ_sb[:], in_=occ.partition_broadcast(P))
-        load_fock(1)
+        for k in range(G + 1):
+            if k < G:
+                nc.sync.dma_start(
+                    out=c_raw[k][:], in_=c_bytes[:, k * W : (k + 1) * W].rearrange("(p a) n -> p a n", a=OT)
+                )
+            if k > 0:
+                load_fock(k - 1)
+        make_identity(nc, ident[:])
+        nc.gpsimd.memset(v_planes[:].rearrange("p g n -> p (g n)").bitcast(U32), 0)
+        nc.sync.dma_start(out=occ_sb[:], in_=occ.rearrange("(p a) -> p a", a=OT))
+        for s in range(G, STEPS):
+            load_fock(s)
         for q in range(4):
             nc.sync.dma_start(
                 out=v_planes[32 * q : 32 * q + 4, :, :].bitcast(I32),
                 in_=v_scales[:, 4 * q : 4 * q + 4, :].rearrange("g r n -> r g n").bitcast(I32),
             )
         nc.sync.dma_start(out=v_sb[:].bitcast(I32), in_=v_words.rearrange("g p n -> p g n").bitcast(I32))
-        load_fock(2)
-        load_fock(3)
 
-        def widen(a):
-            for b in range(N // B):
-                src = c_raw[a][:, b * B : (b + 1) * B].bitcast(FP8)
-                dst = c_wide[:, a, b * B : (b + 1) * B]
-                if b * WIDEN_S[a] // 16 != (b + 1) * WIDEN_S[a] // 16:
-                    nc.scalar.activation(dst, src, COPY, scale=scale_sb[:, a, b : b + 1])
-                else:
-                    nc.vector.tensor_scalar(dst, src, scale_sb[:, a, b : b + 1], None, MULT)
+        c_wide, c_turned, c_grp = {}, {}, {}
 
-        turned = {}
+        def widen(g):
+            for a in range(OT):
+                wide = wide_pool.tile([P, W], BF16, name="c_wide")
+                for b in range(W // B):
+                    src = c_raw[g][:, a, b * B : (b + 1) * B].bitcast(FP8)
+                    dst = wide[:, b * B : (b + 1) * B]
+                    scale = scale_sb[:, a, 4 * g + b : 4 * g + b + 1]
+                    i = 4 * a + b
+                    if i * WIDEN_S // 16 != (i + 1) * WIDEN_S // 16:
+                        nc.scalar.activation(dst, src, COPY, scale=scale)
+                    else:
+                        nc.vector.tensor_scalar(dst, src, scale, None, MULT)
+                c_wide[g, a] = wide
 
-        def turn(a):
-            words = c_wide[:, a, :].bitcast(F32)
+        def turn_c(g):
             for h in range(2):
-                xt = bank(2 * a + h)
-                for gi in range(2):
+                xt = bank(4 + 2 * (g % 2) + h)
+                for a2 in range(2):
+                    words = c_wide[g, 2 * h + a2][:].bitcast(F32)
                     for u in range(2):
-                        g = 2 * h + gi
-                        col = 256 * gi + 128 * u
-                        nc.tensor.transpose(xt[:, col : col + P], words[:, 256 * g + u : 256 * (g + 1) : 2], ident[:])
-                turned[a, h] = xt
+                        col = 256 * a2 + P * u
+                        nc.tensor.transpose(xt[:, col : col + P], words[:, u : 256 : 2], ident[:])
+                c_turned[g, h] = xt
 
-        def untangle(a):
+        def untangle(dst, xt, on_vector):
+            out = dst.rearrange("p r j -> p (r j)").bitcast(F32).rearrange("p (a r u) -> p a r u", a=2, u=2)
+            in_ = xt[:].rearrange("p (a u r) -> p a r u", a=2, u=2)
+            if on_vector:
+                nc.vector.tensor_copy(out=out, in_=in_)
+            else:
+                nc.scalar.copy(out, in_)
+
+        def untangle_c(g):
+            grp = turn_pool.tile([P, O, 4], BF16, name="c_grp", align_bytes=64)
             for h in range(2):
-                out = c_grp[:, 2 * h : 2 * h + 2, a * P : (a + 1) * P, :].rearrange("p g r j -> p g (r j)").bitcast(F32)
-                out = out.rearrange("p g (r u) -> p g r u", u=2)
-                in_ = turned[a, h][:].rearrange("p (g u r) -> p g r u", g=2, u=2)
-                if (a, h) in UNTANGLE_V:
-                    nc.vector.tensor_copy(out=out, in_=in_)
-                else:
-                    nc.scalar.copy(out, in_)
+                untangle(grp[:, 256 * h : 256 * (h + 1), :], c_turned[g, h], False)
+            c_grp[g] = grp
 
         def quantise_c(g):
             nc.vector.quantize_mx(
-                out=c_codes[:, g, :].bitcast(FP8X4),
-                scales=c_planes[:, g, :],
-                in_=c_grp[:, g, :, :].rearrange("p o j -> p (o j)"),
+                out=c_codes[g][:].bitcast(FP8X4), scales=c_planes[g][:], in_=c_grp[g][:].rearrange("p o j -> p (o j)")
             )
 
         grps, f_codes, f_planes = {}, {}, {}
 
-        def interleave(s):
-            g, k = divmod(s, 4)
-            grp = grp_pool.tile([P, 4, P, 4], BF16, name="grp", align_bytes=64)
-            src = raws[g, k][:].rearrange("p j (m t) -> p m j t", t=4)
-            dst = grp[:].rearrange("p t m j -> p m j t")
-            cut = SPLIT[s]
-            nc.scalar.copy(dst[:, :cut], src[:, :cut])
-            nc.vector.tensor_copy(out=dst[:, cut:], in_=src[:, cut:])
-            grps[s] = grp
+        def interleave(s, on_vector):
+            if s >= STEPS:
+                return
+            if s not in grps:
+                grps[s] = grp_pool.tile([P, W, 4], BF16, name="grp", align_bytes=64)
+            cut = SHARE_HEAD if s < G else SHARE if s < STEPS - 1 else SHARE_LAST
+            src = raws[s][:].rearrange("p j (c i) -> p c j i", i=4)
+            dst = grps[s][:].rearrange("p (c i) j -> p c j i", i=4)
+            if on_vector:
+                nc.vector.tensor_copy(out=dst[:, cut:], in_=src[:, cut:])
+            else:
+                nc.scalar.copy(dst[:, :cut], src[:, :cut])
 
         def quantise_fock(s):
-            codes = code_pool.tile([P, 512], U32, name="f_codes", align_bytes=64)
-            planes = code_pool.tile([P, 512], U8, name="f_planes", align_bytes=64)
+            codes = code_pool.tile([P, W], U32, name="f_codes", align_bytes=64)
+            planes = code_pool.tile([P, W], U8, name="f_planes", align_bytes=64)
             nc.vector.quantize_mx(
-                out=codes[:].bitcast(FP8X4), scales=planes[:], in_=grps[s][:].rearrange("p t m j -> p (t m j)")
+                out=codes[:].bitcast(FP8X4), scales=planes[:], in_=grps[s][:].rearrange("p n j -> p (n j)")
             )
             f_codes[s], f_planes[s] = codes, planes
 
-        s1_banks, h_grp = {}, {}
+        s1_banks, h_wide, h_turned, h_grp = {}, {}, {}, {}
 
-        def stage1(i):
-            g, a = divmod(i, OT)
-            acc = bank(i % 2)
-            for t in range(4):
-                for k in range(G):
-                    nc.tensor.matmul_mx(
-                        out=acc[:, t * P : (t + 1) * P],
-                        lhsT=f_codes[4 * g + k][:, t * P : (t + 1) * P].bitcast(FP8X4),
-                        lhsT_scale=f_planes[4 * g + k][:, t * P : (t + 1) * P],
-                        rhs=c_codes[:, k, a * P : (a + 1) * P].bitcast(FP8X4),
-                        rhs_scale=c_planes[:, k, a * P : (a + 1) * P],
-                        start=(k == 0),
-                        stop=(k == G - 1),
-                    )
-            s1_banks[i] = acc
+        def stage1(s, tiles):
+            g, k = divmod(s, G)
+            for a in tiles:
+                if k == 0:
+                    s1_banks[g, a] = bank(a)
+                nc.tensor.matmul_mx(
+                    out=s1_banks[g, a][:],
+                    lhsT=c_codes[k][:, a * P : (a + 1) * P].bitcast(FP8X4),
+                    lhsT_scale=c_planes[k][:, a * P : (a + 1) * P],
+                    rhs=f_codes[s][:].bitcast(FP8X4),
+                    rhs_scale=f_planes[s][:],
+                    start=(k == 0),
+                    stop=(k == G - 1),
+                )
 
-        def weigh(i):
-            g, a = divmod(i, OT)
-            if a == 0:
-                h_grp[g] = half_pool.tile([P, O, 4], BF16, name="h_grp", align_bytes=64)
-            nc.vector.tensor_tensor(
-                out=h_grp[g][:, a * P : (a + 1) * P, :].rearrange("p (b i) t -> p b t i", i=4),
-                in0=s1_banks[i][:].rearrange("p (t b i) -> p b t i", t=4, i=4),
-                in1=occ_sb[:, a * P : (a + 1) * P].rearrange("p (b i) -> p b i", i=4).unsqueeze(2).to_broadcast([P, 32, 4, 4]),
-                op=MULT,
-            )
+        def weigh(g, a, on_vector=False):
+            wide = wide_pool.tile([P, W], BF16, name="h_wide")
+            out = wide[:].rearrange("p (u m e) -> p u m e", u=2, e=2)
+            in_ = s1_banks[g, a][:].rearrange("p (m u e) -> p u m e", u=2, e=2)
+            if on_vector:
+                nc.vector.tensor_scalar(out, in_, occ_f32[:, a : a + 1], None, MULT)
+            else:
+                nc.scalar.activation(out, in_, COPY, scale=occ_f32[:, a : a + 1])
+            h_wide[g, a] = wide
 
-        def quantise_half(i):
-            g, a = divmod(i, OT)
-            cols = slice(a * P, (a + 1) * P)
+        def turn_half(g, h):
+            xt = bank(2 * h)
+            for a2 in range(2):
+                words = h_wide[g, 2 * h + a2][:].bitcast(F32)
+                for u in range(2):
+                    col = 256 * a2 + P * u
+                    nc.tensor.transpose(xt[:, col : col + P], words[:, P * u : P * (u + 1)], ident[:])
+            h_turned[g, h] = xt
+
+        def untangle_half(g, h, on_vector=False):
+            grp = turn_pool.tile([P, 256, 4], BF16, name="h_grp", align_bytes=64)
+            untangle(grp[:], h_turned[g, h], on_vector)
+            h_grp[g, h] = grp
+
+        def quantise_half(g, h):
+            cols = slice(256 * h, 256 * (h + 1))
             nc.vector.quantize_mx(
-                out=h_codes[:, g, cols].bitcast(FP8X4),
-                scales=h_planes[:, g, cols],
-                in_=h_grp[g][:, cols, :].rearrange("p o j -> p (o j)"),
+                out=h_codes[g][:, cols].bitcast(FP8X4),
+                scales=h_planes[g][:, cols],
+                in_=h_grp[g, h][:].rearrange("p o j -> p (o j)"),
             )
 
-        def pass2(acc, g, a, n, start, stop, cols=slice(0, 512)):
-            if n == 0:
-                rhs, rhs_scale = c_codes[:, g, cols].bitcast(FP8X4), c_planes[:, g, cols]
-            else:
-                rhs = v_sb[:, g, (n - 1) * 1024 : n * 1024].bitcast(FP4X4)
-                rhs_scale = v_planes[:, g, (n - 1) * 512 : n * 512]
-            nc.tensor.matmul_mx(
-                out=acc,
-                lhsT=h_codes[:, g, a * P : (a + 1) * P].bitcast(FP8X4),
-                lhsT_scale=h_planes[:, g, a * P : (a + 1) * P],
-                rhs=rhs,
-                rhs_scale=rhs_scale,
-                start=start,
-                stop=stop,
-            )
+        accs = {}
 
-        early = [(a, 0) for a in range(3)] + [(a, 1) for a in range(3)]
-        early_acc = {}
+        def stage2(a, n, passes, where=None):
+            for g in passes:
+                if g == 0:
+                    accs[a, n] = bank(where)
+                if n == 0:
+                    rhs, rhs_scale = c_codes[g][:].bitcast(FP8X4), c_planes[g][:]
+                else:
+                    rhs = v_sb[:, g, (n - 1) * 2 * W : n * 2 * W].bitcast(FP4X4)
+                    rhs_scale = v_planes[:, g, (n - 1) * W : n * W]
+                nc.tensor.matmul_mx(
+                    out=accs[a, n][:],
+                    lhsT=h_codes[g][:, a * P : (a + 1) * P].bitcast(FP8X4),
+                    lhsT_scale=h_planes[g][:, a * P : (a + 1) * P],
+                    rhs=rhs,
+                    rhs_scale=rhs_scale,
+                    start=(g == 0),
+                    stop=(g == G - 1),
+                )
 
-        def stage2(i):
-            g, a = divmod(i, OT)
-            for e, (ea, en) in enumerate(early):
-                if ea == a:
-                    if g == 0:
-                        early_acc[e] = bank(2 + e)
-                    pass2(early_acc[e][:], g, ea, en, g == 0, g == G - 1)
+        oo_rows = f_oo.rearrange("(p a) n -> a p n", a=OT)
+        ov_rows = f_ov.rearrange("(p a) n -> a p n", a=OT)
 
-        flip = [0]
+        def store(a, n, on_vector, pieces=1):
+            res = out_pool.tile([P, W], F32, name="res")
+            width = W // pieces
+            for i in range(pieces):
+                cols = slice(i * width, (i + 1) * width)
+                if n == 0:
+                    out = res[:].rearrange("p (q b) -> p q b", b=OT)
+                    in_ = accs[a, n][:].rearrange("p (b q) -> p q b", b=OT)
+                    dst = oo_rows[a]
+                else:
+                    out, in_ = res[:, cols], accs[a, n][:, cols]
+                    dst = ov_rows[a][:, (n - 1) * W + i * width : (n - 1) * W + (i + 1) * width]
+                if on_vector:
+                    nc.vector.tensor_copy(out=out, in_=in_)
+                else:
+                    nc.scalar.copy(out, in_)
+                nc.sync.dma_start(out=dst, in_=res[:, cols])
 
-        def store(acc, a, n, cols=slice(0, 512)):
-            res = out_pool.tile([P, 512], F32, name="res")[:, cols]
-            acc = acc[:, cols]
-            if flip[0] % 2 == 0:
-                nc.vector.tensor_copy(out=res, in_=acc)
-            else:
-                nc.scalar.copy(res, acc)
-            flip[0] += 1
-            rows = slice(a * P, (a + 1) * P)
-            dst = f_oo[rows, cols] if n == 0 else f_ov[rows, (n - 1) * 512 : n * 512]
-            nc.sync.dma_start(out=dst, in_=res)
+        odd, even = (1, 3), (0, 2)
+        for k in range(2):
+            widen(k)
+            turn_c(k)
+        for k in range(G):
+            untangle_c(k)
+            interleave(k, False)
+            interleave(k, True)
+            if k + 2 < G:
+                widen(k + 2)
+                turn_c(k + 2)
+            quantise_c(k)
+            quantise_fock(k)
+            if k < G - 1:
+                stage1(k, odd + even)
+        nc.vector.tensor_copy(out=occ_f32[:], in_=occ_sb[:])
+        interleave(G, False)
+        interleave(G, True)
+        interleave(G + 1, False)
 
-        widen(0)
-        turn(0)
-        widen(1)
-        turn(1)
-        untangle(0)
-        widen(2)
-        turn(2)
-        untangle(1)
-        widen(3)
-        turn(3)
-        untangle(2)
-        interleave(0)
-        untangle(3)
-        for g in range(G):
-            quantise_c(g)
+        last = G - 1
+        for g in range(last):
+            s = G * (g + 1)
+            stage1(s - 1, odd + even)
+            if g > 0:
+                for a in range(OT):
+                    stage2(a, 0, [g - 1], 4 + a)
+            for a in odd + even:
+                weigh(g, a)
+            interleave(s + 1, True)
+            quantise_fock(s)
+            stage1(s, odd)
+            turn_half(g, 0)
+            turn_half(g, 1)
+            interleave(s + 2, False)
+            interleave(s + 2, True)
+            quantise_fock(s + 1)
+            untangle_half(g, 0)
+            untangle_half(g, 1)
+            stage1(s + 1, odd)
+            for a in even:
+                stage1(s, [a])
+                stage1(s + 1, [a])
+            interleave(s + 3, False)
+            interleave(s + 3, True)
+            quantise_fock(s + 2)
+            quantise_half(g, 0)
+            stage1(s + 2, odd + even)
+            interleave(s + 4, False)
+            interleave(s + 5, False)
+            interleave(s + 4, True)
+            quantise_half(g, 1)
+            quantise_fock(s + 3)
 
-        last = 4 * G
-        for s in range(1, last + 6):
-            if 0 <= s - 6 < last:
-                weigh(s - 6)
-            if s < last:
-                interleave(s)
-            if s - 1 < last:
-                quantise_fock(s - 1)
-            if 0 <= s - 6 < last:
-                quantise_half(s - 6)
-            if 0 <= s - 5 < last:
-                stage1(s - 5)
-            if 0 <= s - 7 < last:
-                stage2(s - 7)
-        late = [(a, n) for n in (1, 2, 3) for a in range(OT) if (a, n) not in early]
-        acc = bank(0)
-        a, n = late[0]
-        for g in range(G - 1):
-            pass2(acc[:], g, a, n, g == 0, False)
-        stage2(last - 1)
-        pass2(acc[:], G - 1, a, n, False, True)
-        for e, (ea, en) in enumerate(early):
-            store(early_acc[e], ea, en)
-        store(acc, a, n)
-        for j, (a, n) in enumerate(late[1:]):
-            acc = bank((j + 1) % 8)
-            for g in range(G):
-                pass2(acc[:], g, a, n, g == 0, g == G - 1)
-            store(acc, a, n)
-        for h in range(2):
-            cols = slice(256 * h, 256 * h + 256)
-            acc = bank((len(late) + h) % 8)
-            for g in range(G):
-                pass2(acc[:, cols], g, OT - 1, 0, g == 0, g == G - 1, cols)
-            store(acc, OT - 1, 0, cols)
+        stage1(STEPS - 1, odd + even)
+        for a in range(OT):
+            stage2(a, 0, [last - 1])
+        for i, a in enumerate(odd + even):
+            weigh(last, a, on_vector=(i % 2 == 1))
+        turn_half(last, 0)
+        turn_half(last, 1)
+        untangle_half(last, 0)
+        untangle_half(last, 1, on_vector=True)
+        quantise_half(last, 0)
+        quantise_half(last, 1)
+        for a, where in enumerate(odd):
+            stage2(a, 1, range(last), where)
+        done = [(a, 0) for a in range(OT)] + [(0, 1), (1, 1)]
+        for i, (a, n) in enumerate(done):
+            stage2(a, n, [last])
+            store(a, n, i % 2 == 0)
+        rest = [(a, n) for n in range(1, 4) for a in range(OT) if (a, n) not in done]
+        order = even + (4, 5, 6, 7) + odd
+        for i, (a, n) in enumerate(rest):
+            stage2(a, n, range(G), order[i % 8])
+            store(a, n, i % 2 == 0, 2 if i == len(rest) - 1 else 1)

@@ -22,10 +22,11 @@ OT = O // P
 B = 128
 STEPS = G * G
 
-SHARE_HEAD = 36
-SHARE = 42
-SHARE_LAST = 10
-WIDEN_S = 6
+SHARE_HEAD = 64
+SHARE_FREE = 54
+SHARE_BUSY = 26
+WIDEN_S = (2, 0, 0, 0)
+TURNED = ()
 
 FLOPS = 2 * O * N * N + 2 * O * N * (O + V)
 
@@ -48,6 +49,7 @@ def tile_fock_orbital_blocks_d4_kernel(tc, c_bytes, c_scale, fock, occ, v_words,
         ident = keep.tile([P, P], F32, name="ident")
         scale_sb = keep.tile([P, OT, N // B], F32, name="scale_sb")
         occ_sb = keep.tile([P, OT], BF16, name="occ_sb")
+        warm = keep.tile([P, 1], F32, name="warm")
         occ_f32 = keep.tile([P, OT], F32, name="occ_f32")
         c_raw = [keep.tile([P, OT, W], U8, name=f"c_raw{g}") for g in range(G)]
         c_codes = [keep.tile([P, O], U32, name=f"c_codes{g}", align_bytes=64) for g in range(G)]
@@ -70,18 +72,20 @@ def tile_fock_orbital_blocks_d4_kernel(tc, c_bytes, c_scale, fock, occ, v_words,
             )
             raws[s] = raw
 
-        for k in range(G + 1):
+        c_rows = c_bytes.rearrange("(p a) n -> p a n", a=OT)
+        for h in range(2):
+            nc.sync.dma_start(out=c_raw[0][:, 2 * h : 2 * h + 2, :], in_=c_rows[:, 2 * h : 2 * h + 2, 0:W])
+        for k in range(1, G + 1):
             if k < G:
-                nc.sync.dma_start(
-                    out=c_raw[k][:], in_=c_bytes[:, k * W : (k + 1) * W].rearrange("(p a) n -> p a n", a=OT)
-                )
-            if k > 0:
-                load_fock(k - 1)
+                nc.sync.dma_start(out=c_raw[k][:], in_=c_rows[:, :, k * W : (k + 1) * W])
+            load_fock(G * (k - 1) if k - 1 in TURNED else k - 1)
         make_identity(nc, ident[:])
+        nc.scalar.activation(warm[:], ident[:, 0:1], COPY, scale=ident[:, 0:1])
         nc.gpsimd.memset(v_planes[:].rearrange("p g n -> p (g n)").bitcast(U32), 0)
         nc.sync.dma_start(out=occ_sb[:], in_=occ.rearrange("(p a) -> p a", a=OT))
         for s in range(G, STEPS):
-            load_fock(s)
+            if s not in raws:
+                load_fock(s)
         for q in range(4):
             nc.sync.dma_start(
                 out=v_planes[32 * q : 32 * q + 4, :, :].bitcast(I32),
@@ -89,7 +93,7 @@ def tile_fock_orbital_blocks_d4_kernel(tc, c_bytes, c_scale, fock, occ, v_words,
             )
         nc.sync.dma_start(out=v_sb[:].bitcast(I32), in_=v_words.rearrange("g p n -> p g n").bitcast(I32))
 
-        c_wide, c_turned, c_grp = {}, {}, {}
+        c_wide, c_turned, c_grp, grps = {}, {}, {}, {}
 
         def widen(g):
             for a in range(OT):
@@ -98,22 +102,52 @@ def tile_fock_orbital_blocks_d4_kernel(tc, c_bytes, c_scale, fock, occ, v_words,
                     src = c_raw[g][:, a, b * B : (b + 1) * B].bitcast(FP8)
                     dst = wide[:, b * B : (b + 1) * B]
                     scale = scale_sb[:, a, 4 * g + b : 4 * g + b + 1]
-                    i = 4 * a + b
-                    if i * WIDEN_S // 16 != (i + 1) * WIDEN_S // 16:
+                    if a >= OT - WIDEN_S[g]:
                         nc.scalar.activation(dst, src, COPY, scale=scale)
                     else:
+                        dst = wide[:].rearrange("p (u m e) -> p m u e", u=2, e=2)[:, 32 * b : 32 * (b + 1)]
+                        src = src.rearrange("p (m u e) -> p m u e", u=2, e=2)
                         nc.vector.tensor_scalar(dst, src, scale, None, MULT)
                 c_wide[g, a] = wide
 
+        turns = []
+
+        def turn_banks():
+            first = 2 * len(turns) if len(turns) < 4 else 4 + 2 * (len(turns) % 2)
+            turns.append(first)
+            return first
+
         def turn_c(g):
+            first = turn_banks()
             for h in range(2):
-                xt = bank(4 + 2 * (g % 2) + h)
+                xt = bank(first + h)
                 for a2 in range(2):
-                    words = c_wide[g, 2 * h + a2][:].bitcast(F32)
+                    a = 2 * h + a2
+                    words = c_wide[g, a][:].bitcast(F32)
                     for u in range(2):
                         col = 256 * a2 + P * u
-                        nc.tensor.transpose(xt[:, col : col + P], words[:, u : 256 : 2], ident[:])
+                        in_ = words[:, u : 256 : 2] if a >= OT - WIDEN_S[g] else words[:, P * u : P * (u + 1)]
+                        nc.tensor.transpose(xt[:, col : col + P], in_, ident[:])
                 c_turned[g, h] = xt
+
+        f_turned = {}
+
+        def turn_fock(k):
+            first = turn_banks()
+            for h in range(2):
+                xt = bank(first + h)
+                for j2 in range(2):
+                    words = raws[G * k][:, 2 * h + j2, :].bitcast(F32)
+                    for u in range(2):
+                        col = 256 * j2 + P * u
+                        nc.tensor.transpose(xt[:, col : col + P], words[:, u : 256 : 2], ident[:])
+                f_turned[k, h] = xt
+
+        def untangle_fock(k):
+            grps[k] = grp_pool.tile([P, W, 4], BF16, name="grp", align_bytes=64)
+            words = grps[k][:].rearrange("p n j -> p (n j)").bitcast(F32).rearrange("p (m h w) -> p h m w", h=2, w=4)
+            for h in range(2):
+                nc.scalar.copy(words[:, h], f_turned[k, h][:].rearrange("p (w m) -> p m w", w=4))
 
         def untangle(dst, xt, on_vector):
             out = dst.rearrange("p r j -> p (r j)").bitcast(F32).rearrange("p (a r u) -> p a r u", a=2, u=2)
@@ -134,14 +168,14 @@ def tile_fock_orbital_blocks_d4_kernel(tc, c_bytes, c_scale, fock, occ, v_words,
                 out=c_codes[g][:].bitcast(FP8X4), scales=c_planes[g][:], in_=c_grp[g][:].rearrange("p o j -> p (o j)")
             )
 
-        grps, f_codes, f_planes = {}, {}, {}
+        f_codes, f_planes = {}, {}
 
         def interleave(s, on_vector):
             if s >= STEPS:
                 return
             if s not in grps:
                 grps[s] = grp_pool.tile([P, W, 4], BF16, name="grp", align_bytes=64)
-            cut = SHARE_HEAD if s < G else SHARE if s < STEPS - 1 else SHARE_LAST
+            cut = SHARE_HEAD if s < G else SHARE_FREE if s % G < 2 else SHARE_BUSY
             src = raws[s][:].rearrange("p j (c i) -> p c j i", i=4)
             dst = grps[s][:].rearrange("p (c i) j -> p c j i", i=4)
             if on_vector:
@@ -230,61 +264,88 @@ def tile_fock_orbital_blocks_d4_kernel(tc, c_bytes, c_scale, fock, occ, v_words,
         oo_rows = f_oo.rearrange("(p a) n -> a p n", a=OT)
         ov_rows = f_ov.rearrange("(p a) n -> a p n", a=OT)
 
-        def store(a, n, on_vector, pieces=1):
+        def empty(out, in_, on_vector):
+            if on_vector:
+                nc.vector.tensor_copy(out=out, in_=in_)
+            else:
+                nc.scalar.copy(out, in_)
+
+        def store(a, n, on_vector):
             res = out_pool.tile([P, W], F32, name="res")
-            width = W // pieces
-            for i in range(pieces):
-                cols = slice(i * width, (i + 1) * width)
-                if n == 0:
-                    out = res[:].rearrange("p (q b) -> p q b", b=OT)
-                    in_ = accs[a, n][:].rearrange("p (b q) -> p q b", b=OT)
-                    dst = oo_rows[a]
-                else:
-                    out, in_ = res[:, cols], accs[a, n][:, cols]
-                    dst = ov_rows[a][:, (n - 1) * W + i * width : (n - 1) * W + (i + 1) * width]
-                if on_vector:
-                    nc.vector.tensor_copy(out=out, in_=in_)
-                else:
-                    nc.scalar.copy(out, in_)
-                nc.sync.dma_start(out=dst, in_=res[:, cols])
+            if n == 0:
+                empty(
+                    res[:].rearrange("p (q b) -> p q b", b=OT),
+                    accs[a, n][:].rearrange("p (b q) -> p q b", b=OT),
+                    on_vector,
+                )
+                nc.sync.dma_start(out=oo_rows[a], in_=res[:])
+            else:
+                empty(res[:], accs[a, n][:], on_vector)
+                nc.sync.dma_start(out=ov_rows[a][:, (n - 1) * W : n * W], in_=res[:])
+
+        def last_piece(a, col, width, where, on_vector):
+            acc = bank(where)
+            for c in range(0, width, P):
+                for g in range(G):
+                    nc.tensor.matmul_mx(
+                        out=acc[:, c : c + P],
+                        lhsT=h_codes[g][:, a * P : (a + 1) * P].bitcast(FP8X4),
+                        lhsT_scale=h_planes[g][:, a * P : (a + 1) * P],
+                        rhs=v_sb[:, g, 2 * (col + c) : 2 * (col + c + P)].bitcast(FP4X4),
+                        rhs_scale=v_planes[:, g, col + c : col + c + P],
+                        start=(g == 0),
+                        stop=(g == G - 1),
+                    )
+            res = out_pool.tile([P, W], F32, name="res")
+            empty(res[:, :width], acc[:, :width], on_vector)
+            nc.sync.dma_start(out=ov_rows[a][:, col : col + width], in_=res[:, :width])
 
         odd, even = (1, 3), (0, 2)
         for k in range(2):
             widen(k)
             turn_c(k)
+        if 0 in TURNED:
+            turn_fock(0)
         for k in range(G):
             untangle_c(k)
-            interleave(k, False)
-            interleave(k, True)
+            if k in TURNED:
+                untangle_fock(k)
+            else:
+                interleave(k, False)
+                interleave(k, True)
+            if k + 1 in TURNED:
+                turn_fock(k + 1)
             if k + 2 < G:
                 widen(k + 2)
                 turn_c(k + 2)
+            if k == G - 1:
+                nc.vector.tensor_copy(out=occ_f32[:], in_=occ_sb[:])
             quantise_c(k)
             quantise_fock(k)
             if k < G - 1:
                 stage1(k, odd + even)
-        nc.vector.tensor_copy(out=occ_f32[:], in_=occ_sb[:])
         interleave(G, False)
-        interleave(G, True)
         interleave(G + 1, False)
 
         last = G - 1
         for g in range(last):
             s = G * (g + 1)
             stage1(s - 1, odd + even)
+            interleave(s, True)
             if g > 0:
+                quantise_half(g - 1, 1)
                 for a in range(OT):
                     stage2(a, 0, [g - 1], 4 + a)
             for a in odd + even:
                 weigh(g, a)
             interleave(s + 1, True)
             quantise_fock(s)
+            quantise_fock(s + 1)
             stage1(s, odd)
             turn_half(g, 0)
             turn_half(g, 1)
             interleave(s + 2, False)
             interleave(s + 2, True)
-            quantise_fock(s + 1)
             untangle_half(g, 0)
             untangle_half(g, 1)
             stage1(s + 1, odd)
@@ -298,10 +359,9 @@ def tile_fock_orbital_blocks_d4_kernel(tc, c_bytes, c_scale, fock, occ, v_words,
             stage1(s + 2, odd + even)
             interleave(s + 4, False)
             interleave(s + 5, False)
-            interleave(s + 4, True)
-            quantise_half(g, 1)
             quantise_fock(s + 3)
 
+        quantise_half(last - 1, 1)
         stage1(STEPS - 1, odd + even)
         for a in range(OT):
             stage2(a, 0, [last - 1])
@@ -321,6 +381,10 @@ def tile_fock_orbital_blocks_d4_kernel(tc, c_bytes, c_scale, fock, occ, v_words,
             store(a, n, i % 2 == 0)
         rest = [(a, n) for n in range(1, 4) for a in range(OT) if (a, n) not in done]
         order = even + (4, 5, 6, 7) + odd
-        for i, (a, n) in enumerate(rest):
+        for i, (a, n) in enumerate(rest[:-1]):
             stage2(a, n, range(G), order[i % 8])
-            store(a, n, i % 2 == 0, 2 if i == len(rest) - 1 else 1)
+            store(a, n, i % 2 == 0)
+        col = V - W
+        for i, width in enumerate((2 * P, P, P)):
+            last_piece(OT - 1, col, width, order[len(rest) % 8 + i], i % 2 == 1)
+            col = col + width

@@ -22,11 +22,13 @@ OT = O // P
 B = 128
 STEPS = G * G
 
-SHARE_HEAD = 64
+SHARE_HEAD = 60
 SHARE_FREE = 54
 SHARE_BUSY = 26
 WIDEN_S = (2, 0, 0, 0)
-TURNED = ()
+LOADS = (("c", 1), ("f", 0), ("c", 2), ("f", 4), ("c", 3), ("f", 2), ("f", 12))
+VW = (1,)
+TURNED = (0, 1, 3)
 
 FLOPS = 2 * O * N * N + 2 * O * N * (O + V)
 
@@ -75,13 +77,18 @@ def tile_fock_orbital_blocks_d4_kernel(tc, c_bytes, c_scale, fock, occ, v_words,
         c_rows = c_bytes.rearrange("(p a) n -> p a n", a=OT)
         for h in range(2):
             nc.sync.dma_start(out=c_raw[0][:, 2 * h : 2 * h + 2, :], in_=c_rows[:, 2 * h : 2 * h + 2, 0:W])
-        for k in range(1, G + 1):
-            if k < G:
+        for w in LOADS:
+            if w[0] == "c":
+                k = w[1]
                 nc.sync.dma_start(out=c_raw[k][:], in_=c_rows[:, :, k * W : (k + 1) * W])
-            load_fock(G * (k - 1) if k - 1 in TURNED else k - 1)
+            else:
+                load_fock(w[1])
         make_identity(nc, ident[:])
         nc.scalar.activation(warm[:], ident[:, 0:1], COPY, scale=ident[:, 0:1])
-        nc.gpsimd.memset(v_planes[:].rearrange("p g n -> p (g n)").bitcast(U32), 0)
+        idle = bank(7)
+        for i in range(4):
+            nc.tensor.matmul(idle[:, i * P : (i + 1) * P], lhsT=ident[:], rhs=ident[:], start=True, stop=True)
+        nc.vector.memset(v_planes[:].rearrange("p g n -> p (g n)").bitcast(U32), 0)
         nc.sync.dma_start(out=occ_sb[:], in_=occ.rearrange("(p a) -> p a", a=OT))
         for s in range(G, STEPS):
             if s not in raws:
@@ -102,7 +109,7 @@ def tile_fock_orbital_blocks_d4_kernel(tc, c_bytes, c_scale, fock, occ, v_words,
                     src = c_raw[g][:, a, b * B : (b + 1) * B].bitcast(FP8)
                     dst = wide[:, b * B : (b + 1) * B]
                     scale = scale_sb[:, a, 4 * g + b : 4 * g + b + 1]
-                    if a >= OT - WIDEN_S[g]:
+                    if g == 0 and a % 2 == 1:
                         nc.scalar.activation(dst, src, COPY, scale=scale)
                     else:
                         dst = wide[:].rearrange("p (u m e) -> p m u e", u=2, e=2)[:, 32 * b : 32 * (b + 1)]
@@ -110,15 +117,7 @@ def tile_fock_orbital_blocks_d4_kernel(tc, c_bytes, c_scale, fock, occ, v_words,
                         nc.vector.tensor_scalar(dst, src, scale, None, MULT)
                 c_wide[g, a] = wide
 
-        turns = []
-
-        def turn_banks():
-            first = 2 * len(turns) if len(turns) < 4 else 4 + 2 * (len(turns) % 2)
-            turns.append(first)
-            return first
-
-        def turn_c(g):
-            first = turn_banks()
+        def turn_c(g, first):
             for h in range(2):
                 xt = bank(first + h)
                 for a2 in range(2):
@@ -126,14 +125,13 @@ def tile_fock_orbital_blocks_d4_kernel(tc, c_bytes, c_scale, fock, occ, v_words,
                     words = c_wide[g, a][:].bitcast(F32)
                     for u in range(2):
                         col = 256 * a2 + P * u
-                        in_ = words[:, u : 256 : 2] if a >= OT - WIDEN_S[g] else words[:, P * u : P * (u + 1)]
+                        in_ = words[:, u : 256 : 2] if g == 0 and a % 2 == 1 else words[:, P * u : P * (u + 1)]
                         nc.tensor.transpose(xt[:, col : col + P], in_, ident[:])
                 c_turned[g, h] = xt
 
         f_turned = {}
 
-        def turn_fock(k):
-            first = turn_banks()
+        def turn_fock(k, first):
             for h in range(2):
                 xt = bank(first + h)
                 for j2 in range(2):
@@ -143,11 +141,11 @@ def tile_fock_orbital_blocks_d4_kernel(tc, c_bytes, c_scale, fock, occ, v_words,
                         nc.tensor.transpose(xt[:, col : col + P], words[:, u : 256 : 2], ident[:])
                 f_turned[k, h] = xt
 
-        def untangle_fock(k):
+        def untangle_fock(k, shared=False):
             grps[k] = grp_pool.tile([P, W, 4], BF16, name="grp", align_bytes=64)
             words = grps[k][:].rearrange("p n j -> p (n j)").bitcast(F32).rearrange("p (m h w) -> p h m w", h=2, w=4)
             for h in range(2):
-                nc.scalar.copy(words[:, h], f_turned[k, h][:].rearrange("p (w m) -> p m w", w=4))
+                empty(words[:, h], f_turned[k, h][:].rearrange("p (w m) -> p m w", w=4), shared and h == 1)
 
         def untangle(dst, xt, on_vector):
             out = dst.rearrange("p r j -> p (r j)").bitcast(F32).rearrange("p (a r u) -> p a r u", a=2, u=2)
@@ -298,32 +296,43 @@ def tile_fock_orbital_blocks_d4_kernel(tc, c_bytes, c_scale, fock, occ, v_words,
                     )
             res = out_pool.tile([P, W], F32, name="res")
             empty(res[:, :width], acc[:, :width], on_vector)
-            nc.sync.dma_start(out=ov_rows[a][:, col : col + width], in_=res[:, :width])
+            queue = nc.scalar if col + width == V else nc.sync
+            queue.dma_start(out=ov_rows[a][:, col : col + width], in_=res[:, :width])
 
         odd, even = (1, 3), (0, 2)
-        for k in range(2):
-            widen(k)
-            turn_c(k)
-        if 0 in TURNED:
-            turn_fock(0)
-        for k in range(G):
-            untangle_c(k)
-            if k in TURNED:
-                untangle_fock(k)
-            else:
-                interleave(k, False)
-                interleave(k, True)
-            if k + 1 in TURNED:
-                turn_fock(k + 1)
-            if k + 2 < G:
-                widen(k + 2)
-                turn_c(k + 2)
-            if k == G - 1:
-                nc.vector.tensor_copy(out=occ_f32[:], in_=occ_sb[:])
-            quantise_c(k)
-            quantise_fock(k)
-            if k < G - 1:
-                stage1(k, odd + even)
+        widen(0)
+        turn_c(0, 0)
+        widen(1)
+        turn_c(1, 2)
+        turn_fock(0, 4)
+        untangle_c(0)
+        untangle_c(1)
+        widen(2)
+        turn_c(2, 6)
+        untangle_fock(0)
+        quantise_c(0)
+        quantise_c(1)
+        turn_fock(1, 4)
+        untangle_c(2)
+        quantise_fock(0)
+        stage1(0, odd + even)
+        widen(3)
+        untangle_fock(1)
+        turn_c(3, 6)
+        turn_fock(3, 4)
+        interleave(2, False)
+        interleave(2, True)
+        quantise_fock(1)
+        stage1(1, odd + even)
+        quantise_c(2)
+        untangle_c(3)
+        quantise_fock(2)
+        stage1(2, odd + even)
+        nc.vector.tensor_copy(out=occ_f32[:], in_=occ_sb[:])
+        interleave(G, True)
+        untangle_fock(3)
+        quantise_c(3)
+        quantise_fock(3)
         interleave(G, False)
         interleave(G + 1, False)
 
@@ -331,15 +340,20 @@ def tile_fock_orbital_blocks_d4_kernel(tc, c_bytes, c_scale, fock, occ, v_words,
         for g in range(last):
             s = G * (g + 1)
             stage1(s - 1, odd + even)
-            interleave(s, True)
+            if g > 0:
+                interleave(s, True)
             if g > 0:
                 quantise_half(g - 1, 1)
                 for a in range(OT):
                     stage2(a, 0, [g - 1], 4 + a)
-            for a in odd + even:
-                weigh(g, a)
-            interleave(s + 1, True)
-            quantise_fock(s)
+            if g == 0:
+                interleave(s + 1, True)
+                quantise_fock(s)
+            for i, a in enumerate(odd + even):
+                weigh(g, a, g == 0 and i in VW)
+            if g > 0:
+                interleave(s + 1, True)
+                quantise_fock(s)
             quantise_fock(s + 1)
             stage1(s, odd)
             turn_half(g, 0)

@@ -22,13 +22,12 @@ OT = O // P
 B = 128
 STEPS = G * G
 
-SHARE_HEAD = 60
+SHARE_HEAD = 62
 SHARE_FREE = 54
 SHARE_BUSY = 26
-WIDEN_S = (2, 0, 0, 0)
-LOADS = (("c", 1), ("f", 0), ("c", 2), ("f", 4), ("c", 3), ("f", 2), ("f", 12))
-VW = (1,)
-TURNED = (0, 1, 3)
+VW = ()
+FIRST = (1, 8, 3)
+WS = 3
 
 FLOPS = 2 * O * N * N + 2 * O * N * (O + V)
 
@@ -49,11 +48,12 @@ def tile_fock_orbital_blocks_d4_kernel(tc, c_bytes, c_scale, fock, occ, v_words,
             return psum.tile([P, W], F32, name=f"bank{i}", tag=f"bank{i}")
 
         ident = keep.tile([P, P], F32, name="ident")
-        scale_sb = keep.tile([P, OT, N // B], F32, name="scale_sb")
+        scale_sb = keep.tile([P, OT * N // B], F32, name="scale_sb")
         occ_sb = keep.tile([P, OT], BF16, name="occ_sb")
         warm = keep.tile([P, 1], F32, name="warm")
         occ_f32 = keep.tile([P, OT], F32, name="occ_f32")
-        c_raw = [keep.tile([P, OT, W], U8, name=f"c_raw{g}") for g in range(G)]
+        c_raw = [keep.tile([P, N], U8, name=f"c_raw{a}") for a in range(OT)]
+        c_grp = [keep.tile([P, 2, O, 4], BF16, name=f"c_grp{h}", align_bytes=64) for h in range(2)]
         c_codes = [keep.tile([P, O], U32, name=f"c_codes{g}", align_bytes=64) for g in range(G)]
         c_planes = [keep.tile([P, O], U8, name=f"c_planes{g}", align_bytes=64) for g in range(G)]
         h_codes = [keep.tile([P, O], U32, name=f"h_codes{g}", align_bytes=64) for g in range(G)]
@@ -63,7 +63,7 @@ def tile_fock_orbital_blocks_d4_kernel(tc, c_bytes, c_scale, fock, occ, v_words,
 
         ctx.enter_context(tc.manual_schedule())
 
-        nc.scalar.dma_start(out=scale_sb[:], in_=c_scale.rearrange("(p a) b -> p a b", a=OT))
+        nc.scalar.dma_start(out=scale_sb[:], in_=c_scale.rearrange("(p a) b -> p (a b)", a=OT))
         raws = {}
 
         def load_fock(s):
@@ -74,20 +74,18 @@ def tile_fock_orbital_blocks_d4_kernel(tc, c_bytes, c_scale, fock, occ, v_words,
             )
             raws[s] = raw
 
-        c_rows = c_bytes.rearrange("(p a) n -> p a n", a=OT)
+        c_rows = c_bytes.rearrange("(p a) n -> a p n", a=OT)
         for h in range(2):
-            nc.sync.dma_start(out=c_raw[0][:, 2 * h : 2 * h + 2, :], in_=c_rows[:, 2 * h : 2 * h + 2, 0:W])
-        for w in LOADS:
-            if w[0] == "c":
-                k = w[1]
-                nc.sync.dma_start(out=c_raw[k][:], in_=c_rows[:, :, k * W : (k + 1) * W])
-            else:
-                load_fock(w[1])
+            cols = slice(h * N // 2, (h + 1) * N // 2)
+            nc.sync.dma_start(out=c_raw[0][:, cols], in_=c_rows[0][:, cols])
+        for a in range(1, OT):
+            if a == OT - 1:
+                load_fock(0)
+            nc.sync.dma_start(out=c_raw[a][:], in_=c_rows[a])
+        for s in FIRST:
+            load_fock(s)
         make_identity(nc, ident[:])
         nc.scalar.activation(warm[:], ident[:, 0:1], COPY, scale=ident[:, 0:1])
-        idle = bank(7)
-        for i in range(4):
-            nc.tensor.matmul(idle[:, i * P : (i + 1) * P], lhsT=ident[:], rhs=ident[:], start=True, stop=True)
         nc.vector.memset(v_planes[:].rearrange("p g n -> p (g n)").bitcast(U32), 0)
         nc.sync.dma_start(out=occ_sb[:], in_=occ.rearrange("(p a) -> p a", a=OT))
         for s in range(G, STEPS):
@@ -100,34 +98,37 @@ def tile_fock_orbital_blocks_d4_kernel(tc, c_bytes, c_scale, fock, occ, v_words,
             )
         nc.sync.dma_start(out=v_sb[:].bitcast(I32), in_=v_words.rearrange("g p n -> p g n").bitcast(I32))
 
-        c_wide, c_turned, c_grp, grps = {}, {}, {}, {}
+        c_wide, c_turned, grps = {}, {}, {}
 
-        def widen(g):
-            for a in range(OT):
+        def on_scalar(a, g):
+            return a == 0 and g >= WS
+
+        def widen(a):
+            for g in range(G):
                 wide = wide_pool.tile([P, W], BF16, name="c_wide")
                 for b in range(W // B):
-                    src = c_raw[g][:, a, b * B : (b + 1) * B].bitcast(FP8)
-                    dst = wide[:, b * B : (b + 1) * B]
-                    scale = scale_sb[:, a, 4 * g + b : 4 * g + b + 1]
-                    if g == 0 and a % 2 == 1:
-                        nc.scalar.activation(dst, src, COPY, scale=scale)
+                    src = c_raw[a][:, g * W + b * B : g * W + (b + 1) * B].bitcast(FP8)
+                    i = a * (N // B) + 4 * g + b
+                    scale = scale_sb[:, i : i + 1]
+                    if on_scalar(a, g):
+                        nc.scalar.activation(wide[:, b * B : (b + 1) * B], src, COPY, scale=scale)
                     else:
                         dst = wide[:].rearrange("p (u m e) -> p m u e", u=2, e=2)[:, 32 * b : 32 * (b + 1)]
                         src = src.rearrange("p (m u e) -> p m u e", u=2, e=2)
                         nc.vector.tensor_scalar(dst, src, scale, None, MULT)
-                c_wide[g, a] = wide
+                c_wide[a, g] = wide
 
-        def turn_c(g, first):
+        def turn_c(a):
             for h in range(2):
-                xt = bank(first + h)
-                for a2 in range(2):
-                    a = 2 * h + a2
-                    words = c_wide[g, a][:].bitcast(F32)
+                xt = bank(2 * a + h)
+                for g2 in range(2):
+                    g = 2 * h + g2
+                    words = c_wide[a, g][:].bitcast(F32)
                     for u in range(2):
-                        col = 256 * a2 + P * u
-                        in_ = words[:, u : 256 : 2] if g == 0 and a % 2 == 1 else words[:, P * u : P * (u + 1)]
+                        col = 256 * g2 + P * u
+                        in_ = words[:, u : 256 : 2] if on_scalar(a, g) else words[:, P * u : P * (u + 1)]
                         nc.tensor.transpose(xt[:, col : col + P], in_, ident[:])
-                c_turned[g, h] = xt
+                c_turned[a, h] = xt
 
         f_turned = {}
 
@@ -141,11 +142,11 @@ def tile_fock_orbital_blocks_d4_kernel(tc, c_bytes, c_scale, fock, occ, v_words,
                         nc.tensor.transpose(xt[:, col : col + P], words[:, u : 256 : 2], ident[:])
                 f_turned[k, h] = xt
 
-        def untangle_fock(k, shared=False):
+        def untangle_fock(k):
             grps[k] = grp_pool.tile([P, W, 4], BF16, name="grp", align_bytes=64)
             words = grps[k][:].rearrange("p n j -> p (n j)").bitcast(F32).rearrange("p (m h w) -> p h m w", h=2, w=4)
             for h in range(2):
-                empty(words[:, h], f_turned[k, h][:].rearrange("p (w m) -> p m w", w=4), shared and h == 1)
+                nc.scalar.copy(words[:, h], f_turned[k, h][:].rearrange("p (w m) -> p m w", w=4))
 
         def untangle(dst, xt, on_vector):
             out = dst.rearrange("p r j -> p (r j)").bitcast(F32).rearrange("p (a r u) -> p a r u", a=2, u=2)
@@ -155,15 +156,19 @@ def tile_fock_orbital_blocks_d4_kernel(tc, c_bytes, c_scale, fock, occ, v_words,
             else:
                 nc.scalar.copy(out, in_)
 
-        def untangle_c(g):
-            grp = turn_pool.tile([P, O, 4], BF16, name="c_grp", align_bytes=64)
+        def untangle_c(a):
             for h in range(2):
-                untangle(grp[:, 256 * h : 256 * (h + 1), :], c_turned[g, h], False)
-            c_grp[g] = grp
+                out = c_grp[h][:, :, a * P : (a + 1) * P, :].rearrange("p g r j -> p g (r j)").bitcast(F32)
+                nc.scalar.copy(
+                    out.rearrange("p g (r u) -> p g r u", u=2),
+                    c_turned[a, h][:].rearrange("p (g u r) -> p g r u", g=2, u=2),
+                )
 
         def quantise_c(g):
             nc.vector.quantize_mx(
-                out=c_codes[g][:].bitcast(FP8X4), scales=c_planes[g][:], in_=c_grp[g][:].rearrange("p o j -> p (o j)")
+                out=c_codes[g][:].bitcast(FP8X4),
+                scales=c_planes[g][:],
+                in_=c_grp[g // 2][:, g % 2].rearrange("p o j -> p (o j)"),
             )
 
         f_codes, f_planes = {}, {}
@@ -268,7 +273,7 @@ def tile_fock_orbital_blocks_d4_kernel(tc, c_bytes, c_scale, fock, occ, v_words,
             else:
                 nc.scalar.copy(out, in_)
 
-        def store(a, n, on_vector):
+        def store(a, n, on_vector, pieces=1):
             res = out_pool.tile([P, W], F32, name="res")
             if n == 0:
                 empty(
@@ -278,8 +283,11 @@ def tile_fock_orbital_blocks_d4_kernel(tc, c_bytes, c_scale, fock, occ, v_words,
                 )
                 nc.sync.dma_start(out=oo_rows[a], in_=res[:])
             else:
-                empty(res[:], accs[a, n][:], on_vector)
-                nc.sync.dma_start(out=ov_rows[a][:, (n - 1) * W : n * W], in_=res[:])
+                width = W // pieces
+                for c in range(0, W, width):
+                    col = (n - 1) * W + c
+                    empty(res[:, c : c + width], accs[a, n][:, c : c + width], on_vector)
+                    nc.sync.dma_start(out=ov_rows[a][:, col : col + width], in_=res[:, c : c + width])
 
         def last_piece(a, col, width, where, on_vector):
             acc = bank(where)
@@ -301,38 +309,41 @@ def tile_fock_orbital_blocks_d4_kernel(tc, c_bytes, c_scale, fock, occ, v_words,
 
         odd, even = (1, 3), (0, 2)
         widen(0)
-        turn_c(0, 0)
+        turn_c(0)
         widen(1)
-        turn_c(1, 2)
-        turn_fock(0, 4)
+        turn_c(1)
         untangle_c(0)
-        untangle_c(1)
         widen(2)
-        turn_c(2, 6)
-        untangle_fock(0)
-        quantise_c(0)
-        quantise_c(1)
-        turn_fock(1, 4)
-        untangle_c(2)
-        quantise_fock(0)
-        stage1(0, odd + even)
+        turn_c(2)
+        untangle_c(1)
         widen(3)
-        untangle_fock(1)
-        turn_c(3, 6)
-        turn_fock(3, 4)
-        interleave(2, False)
-        interleave(2, True)
+        turn_c(3)
+        idle = bank(0)
+        for i in range(2):
+            nc.tensor.matmul(idle[:, i * P : (i + 1) * P], lhsT=ident[:], rhs=ident[:], start=True, stop=True)
+        interleave(0, False)
+        untangle_c(2)
+        turn_fock(2, 4)
+        untangle_c(3)
+        interleave(0, True)
+        interleave(1, True)
+        quantise_fock(0)
+        quantise_c(0)
+        stage1(0, odd + even)
+        interleave(1, False)
+        untangle_fock(2)
+        quantise_c(1)
+        interleave(3, True)
         quantise_fock(1)
         stage1(1, odd + even)
+        interleave(3, False)
         quantise_c(2)
-        untangle_c(3)
         quantise_fock(2)
         stage1(2, odd + even)
         nc.vector.tensor_copy(out=occ_f32[:], in_=occ_sb[:])
-        interleave(G, True)
-        untangle_fock(3)
         quantise_c(3)
         quantise_fock(3)
+        interleave(G, True)
         interleave(G, False)
         interleave(G + 1, False)
 
@@ -397,7 +408,7 @@ def tile_fock_orbital_blocks_d4_kernel(tc, c_bytes, c_scale, fock, occ, v_words,
         order = even + (4, 5, 6, 7) + odd
         for i, (a, n) in enumerate(rest[:-1]):
             stage2(a, n, range(G), order[i % 8])
-            store(a, n, i % 2 == 0)
+            store(a, n, i % 2 == 0, 2 if i == len(rest) - 2 else 1)
         col = V - W
         for i, width in enumerate((2 * P, P, P)):
             last_piece(OT - 1, col, width, order[len(rest) % 8 + i], i % 2 == 1)

@@ -22,12 +22,20 @@ OT = O // P
 B = 128
 STEPS = G * G
 
-SHARE_HEAD = 62
-SHARE_FREE = 54
-SHARE_BUSY = 26
-VW = ()
+SHARE_HEAD = 56
+SHARE_FREE = 56
+SHARE_BUSY = 32
+TURNED = 3
+WARM = 1
 FIRST = (1, 8, 3)
 WS = 3
+SHARE_LEAD = 80
+SHARE_MID = 28
+WT = 2
+LEAD = 24
+CUT0 = 1024
+PRE = 0
+MID = 0
 
 FLOPS = 2 * O * N * N + 2 * O * N * (O + V)
 
@@ -48,6 +56,8 @@ def tile_fock_orbital_blocks_d4_kernel(tc, c_bytes, c_scale, fock, occ, v_words,
             return psum.tile([P, W], F32, name=f"bank{i}", tag=f"bank{i}")
 
         ident = keep.tile([P, P], F32, name="ident")
+        ident_bf = keep.tile([P, P], BF16, name="ident_bf")
+        occ_row = keep.tile([P, O], BF16, name="occ_row")
         scale_sb = keep.tile([P, OT * N // B], F32, name="scale_sb")
         occ_sb = keep.tile([P, OT], BF16, name="occ_sb")
         warm = keep.tile([P, 1], F32, name="warm")
@@ -75,19 +85,19 @@ def tile_fock_orbital_blocks_d4_kernel(tc, c_bytes, c_scale, fock, occ, v_words,
             raws[s] = raw
 
         c_rows = c_bytes.rearrange("(p a) n -> a p n", a=OT)
-        for h in range(2):
-            cols = slice(h * N // 2, (h + 1) * N // 2)
+        for cols in (slice(0, CUT0), slice(CUT0, N)):
             nc.sync.dma_start(out=c_raw[0][:, cols], in_=c_rows[0][:, cols])
         for a in range(1, OT):
             if a == OT - 1:
                 load_fock(0)
             nc.sync.dma_start(out=c_raw[a][:], in_=c_rows[a])
+        nc.sync.dma_start(out=occ_sb[:], in_=occ.rearrange("(p a) -> p a", a=OT))
         for s in FIRST:
             load_fock(s)
         make_identity(nc, ident[:])
+        make_identity(nc, ident_bf[:])
         nc.scalar.activation(warm[:], ident[:, 0:1], COPY, scale=ident[:, 0:1])
         nc.vector.memset(v_planes[:].rearrange("p g n -> p (g n)").bitcast(U32), 0)
-        nc.sync.dma_start(out=occ_sb[:], in_=occ.rearrange("(p a) -> p a", a=OT))
         for s in range(G, STEPS):
             if s not in raws:
                 load_fock(s)
@@ -101,7 +111,7 @@ def tile_fock_orbital_blocks_d4_kernel(tc, c_bytes, c_scale, fock, occ, v_words,
         c_wide, c_turned, grps = {}, {}, {}
 
         def on_scalar(a, g):
-            return a == 0 and g >= WS
+            return a < WT and g >= WS
 
         def widen(a):
             for g in range(G):
@@ -156,8 +166,8 @@ def tile_fock_orbital_blocks_d4_kernel(tc, c_bytes, c_scale, fock, occ, v_words,
             else:
                 nc.scalar.copy(out, in_)
 
-        def untangle_c(a):
-            for h in range(2):
+        def untangle_c(a, halves=range(2)):
+            for h in halves:
                 out = c_grp[h][:, :, a * P : (a + 1) * P, :].rearrange("p g r j -> p g (r j)").bitcast(F32)
                 nc.scalar.copy(
                     out.rearrange("p g (r u) -> p g r u", u=2),
@@ -173,17 +183,27 @@ def tile_fock_orbital_blocks_d4_kernel(tc, c_bytes, c_scale, fock, occ, v_words,
 
         f_codes, f_planes = {}, {}
 
-        def interleave(s, on_vector):
+        def interleave(s, on_vector, part=None):
             if s >= STEPS:
                 return
             if s not in grps:
                 grps[s] = grp_pool.tile([P, W, 4], BF16, name="grp", align_bytes=64)
-            cut = SHARE_HEAD if s < G else SHARE_FREE if s % G < 2 else SHARE_BUSY
-            src = raws[s][:].rearrange("p j (c i) -> p c j i", i=4)
-            dst = grps[s][:].rearrange("p (c i) j -> p c j i", i=4)
-            if on_vector:
-                nc.vector.tensor_copy(out=dst[:, cut:], in_=src[:, cut:])
+            cut = SHARE_HEAD if s < G else SHARE_LEAD if s < G + 2 else SHARE_BUSY if s % G >= 2 else SHARE_MID if s < 3 * G else SHARE_FREE
+            if s == G + 2:
+                cut = 0
+            if s < G * TURNED:
+                src = raws[s][:].rearrange("p j (c i) -> p c j i", i=4)
+                dst = grps[s][:].rearrange("p (c i) j -> p c j i", i=4)
             else:
+                cut = cut // 2
+                src = raws[s][:].rearrange("p j (c m t) -> p c t m j", m=2, t=4)
+                dst = grps[s][:].rearrange("p (t c m) j -> p c t m j", m=2, t=4)
+            runs = dst.shape[1]
+            mid = min(runs, cut + LEAD * runs // P)
+            lo, hi = {None: (cut, runs), 0: (cut, mid), 1: (mid, runs)}[part]
+            if on_vector and lo < hi:
+                nc.vector.tensor_copy(out=dst[:, lo:hi], in_=src[:, lo:hi])
+            elif not on_vector and cut > 0:
                 nc.scalar.copy(dst[:, :cut], src[:, :cut])
 
         def quantise_fock(s):
@@ -200,13 +220,16 @@ def tile_fock_orbital_blocks_d4_kernel(tc, c_bytes, c_scale, fock, occ, v_words,
             g, k = divmod(s, G)
             for a in tiles:
                 if k == 0:
-                    s1_banks[g, a] = bank(a)
+                    s1_banks[g, a] = bank(a if g == 0 else OT + a)
+                still, moving = (c_codes[k], c_planes[k]), (f_codes[s], f_planes[s])
+                if g >= TURNED:
+                    still, moving = moving, still
                 nc.tensor.matmul_mx(
                     out=s1_banks[g, a][:],
-                    lhsT=c_codes[k][:, a * P : (a + 1) * P].bitcast(FP8X4),
-                    lhsT_scale=c_planes[k][:, a * P : (a + 1) * P],
-                    rhs=f_codes[s][:].bitcast(FP8X4),
-                    rhs_scale=f_planes[s][:],
+                    lhsT=still[0][:, a * P : (a + 1) * P].bitcast(FP8X4),
+                    lhsT_scale=still[1][:, a * P : (a + 1) * P],
+                    rhs=moving[0][:].bitcast(FP8X4),
+                    rhs_scale=moving[1][:],
                     start=(k == 0),
                     stop=(k == G - 1),
                 )
@@ -221,8 +244,25 @@ def tile_fock_orbital_blocks_d4_kernel(tc, c_bytes, c_scale, fock, occ, v_words,
                 nc.scalar.activation(out, in_, COPY, scale=occ_f32[:, a : a + 1])
             h_wide[g, a] = wide
 
+        h_slots = {}
+
+        def weigh_slot(g, t, cols):
+            if g not in h_slots:
+                h_slots[g] = turn_pool.tile([P, 4, O], BF16, name="h_slots")
+            nc.vector.tensor_tensor(h_slots[g][:, t, cols], s1_banks[g, t][:, cols], occ_row[:, cols], MULT)
+
+        def interleave_half(g, h, on_vector, cut):
+            if (g, h) not in h_grp:
+                h_grp[g, h] = turn_pool.tile([P, 256, 4], BF16, name="h_grp", align_bytes=64)
+            src = h_slots[g][:, :, 256 * h : 256 * (h + 1)].rearrange("p j (c i) -> p c j i", i=4)
+            dst = h_grp[g, h][:].rearrange("p (c i) j -> p c j i", i=4)
+            if on_vector:
+                nc.vector.tensor_copy(out=dst[:, cut:], in_=src[:, cut:])
+            else:
+                nc.scalar.copy(dst[:, :cut], src[:, :cut])
+
         def turn_half(g, h):
-            xt = bank(2 * h)
+            xt = bank(2 * h if g == 0 else OT + 2 * h)
             for a2 in range(2):
                 words = h_wide[g, 2 * h + a2][:].bitcast(F32)
                 for u in range(2):
@@ -308,69 +348,111 @@ def tile_fock_orbital_blocks_d4_kernel(tc, c_bytes, c_scale, fock, occ, v_words,
             queue.dma_start(out=ov_rows[a][:, col : col + width], in_=res[:, :width])
 
         odd, even = (1, 3), (0, 2)
+
+        def heat(where, n):
+            if n:
+                idle = bank(where)
+                rhs = ident[:].unsqueeze(1).to_broadcast([P, n, P])
+                nc.tensor.matmul(idle[:, : n * P], lhsT=ident[:], rhs=rhs, start=True, stop=True)
+
+        heat(7, PRE)
         widen(0)
         turn_c(0)
+        heat(7, MID)
         widen(1)
         turn_c(1)
+        heat(7, MID)
         untangle_c(0)
         widen(2)
         turn_c(2)
+        heat(7, MID)
         untangle_c(1)
         widen(3)
         turn_c(3)
-        idle = bank(0)
-        for i in range(2):
-            nc.tensor.matmul(idle[:, i * P : (i + 1) * P], lhsT=ident[:], rhs=ident[:], start=True, stop=True)
+        heat(1, WARM)
+        spread = psum.tile([P, 2 * W], BF16, name="spread", tag="bank0")
+        for a in range(OT):
+            nc.tensor.matmul(
+                spread[:, a * P : (a + 1) * P],
+                lhsT=occ_sb[:, a : a + 1].to_broadcast([P, P]),
+                rhs=ident_bf[:],
+                start=True,
+                stop=True,
+            )
         interleave(0, False)
-        untangle_c(2)
+        for h in range(2):
+            untangle_c(2, [h])
+            untangle_c(3, [h])
         turn_fock(2, 4)
-        untangle_c(3)
+        nc.scalar.copy(occ_row[:], spread[:, :O])
         interleave(0, True)
         interleave(1, True)
         quantise_fock(0)
         quantise_c(0)
-        stage1(0, odd + even)
+        stage1(0, even + odd)
         interleave(1, False)
         untangle_fock(2)
         quantise_c(1)
         interleave(3, True)
         quantise_fock(1)
-        stage1(1, odd + even)
+        stage1(1, even + odd)
         interleave(3, False)
         quantise_c(2)
         quantise_fock(2)
-        stage1(2, odd + even)
-        nc.vector.tensor_copy(out=occ_f32[:], in_=occ_sb[:])
+        stage1(2, even + odd)
         quantise_c(3)
         quantise_fock(3)
-        interleave(G, True)
+        stage1(3, range(OT))
         interleave(G, False)
         interleave(G + 1, False)
+        interleave(G, True)
+        nc.vector.tensor_copy(out=occ_f32[:], in_=occ_sb[:])
+        interleave(G + 1, True, 0)
+        quantise_fock(G)
+        stage1(G, range(OT))
+        for a in range(OT):
+            weigh(0, a)
+        interleave(G + 1, True, 1)
+        interleave(G + 2, True, 0)
+        quantise_fock(G + 1)
+        stage1(G + 1, odd + even)
+        turn_half(0, 0)
+        turn_half(0, 1)
+        interleave(G + 2, False)
+        interleave(G + 3, False)
+        interleave(G + 2, True, 1)
+        interleave(G + 3, True, 0)
+        untangle_half(0, 0)
+        untangle_half(0, 1)
+        quantise_fock(G + 2)
+        stage1(G + 2, odd + even)
+        interleave(G + 3, True, 1)
+        interleave(2 * G, False)
+        interleave(2 * G + 1, False)
+        interleave(2 * G, True, 0)
+        quantise_fock(G + 3)
+        quantise_half(0, 0)
 
         last = G - 1
-        for g in range(last):
+        for g in range(1, last):
             s = G * (g + 1)
             stage1(s - 1, odd + even)
-            if g > 0:
-                interleave(s, True)
-            if g > 0:
-                quantise_half(g - 1, 1)
-                for a in range(OT):
-                    stage2(a, 0, [g - 1], 4 + a)
-            if g == 0:
-                interleave(s + 1, True)
-                quantise_fock(s)
-            for i, a in enumerate(odd + even):
-                weigh(g, a, g == 0 and i in VW)
-            if g > 0:
-                interleave(s + 1, True)
-                quantise_fock(s)
+            quantise_half(g - 1, 1)
+            for a in range(OT):
+                stage2(a, 0, [g - 1], a)
+            for a in odd + even:
+                weigh(g, a)
+            interleave(s, True, 1 if g == 1 else None)
+            interleave(s + 1, True, 0)
+            quantise_fock(s)
+            interleave(s + 1, True, 1)
+            interleave(s + 2, True, 0)
             quantise_fock(s + 1)
             stage1(s, odd)
             turn_half(g, 0)
             turn_half(g, 1)
             interleave(s + 2, False)
-            interleave(s + 2, True)
+            interleave(s + 2, True, 1)
             untangle_half(g, 0)
             untangle_half(g, 1)
             stage1(s + 1, odd)
@@ -378,38 +460,40 @@ def tile_fock_orbital_blocks_d4_kernel(tc, c_bytes, c_scale, fock, occ, v_words,
                 stage1(s, [a])
                 stage1(s + 1, [a])
             interleave(s + 3, False)
-            interleave(s + 3, True)
+            interleave(s + 3, True, 0)
             quantise_fock(s + 2)
+            interleave(s + 3, True, 1)
             quantise_half(g, 0)
             stage1(s + 2, odd + even)
             interleave(s + 4, False)
             interleave(s + 5, False)
             quantise_fock(s + 3)
 
+        halves = (slice(0, 256), slice(256, 512))
         quantise_half(last - 1, 1)
-        stage1(STEPS - 1, odd + even)
+        stage1(STEPS - 1, range(4))
         for a in range(OT):
             stage2(a, 0, [last - 1])
-        for i, a in enumerate(odd + even):
-            weigh(last, a, on_vector=(i % 2 == 1))
-        turn_half(last, 0)
-        turn_half(last, 1)
-        untangle_half(last, 0)
-        untangle_half(last, 1, on_vector=True)
+        for t in range(4):
+            weigh_slot(last, t, halves[0])
+        interleave_half(last, 0, False, 64)
+        for t in range(4):
+            weigh_slot(last, t, halves[1])
+        interleave_half(last, 1, True, 0)
         quantise_half(last, 0)
         quantise_half(last, 1)
-        for a, where in enumerate(odd):
-            stage2(a, 1, range(last), where)
-        done = [(a, 0) for a in range(OT)] + [(0, 1), (1, 1)]
+        for a in range(OT):
+            stage2(a, 1, range(last), OT + a)
+        done = [(a, n) for n in range(2) for a in range(OT)]
         for i, (a, n) in enumerate(done):
             stage2(a, n, [last])
             store(a, n, i % 2 == 0)
         rest = [(a, n) for n in range(1, 4) for a in range(OT) if (a, n) not in done]
-        order = even + (4, 5, 6, 7) + odd
+        order = range(8)
         for i, (a, n) in enumerate(rest[:-1]):
             stage2(a, n, range(G), order[i % 8])
             store(a, n, i % 2 == 0, 2 if i == len(rest) - 2 else 1)
         col = V - W
         for i, width in enumerate((2 * P, P, P)):
-            last_piece(OT - 1, col, width, order[len(rest) % 8 + i], i % 2 == 1)
+            last_piece(OT - 1, col, width, order[(len(rest) - 1 + i) % 8], i % 2 == 1)
             col = col + width

@@ -22,7 +22,7 @@ OT = O // P
 B = 128
 STEPS = G * G
 
-SHARE_HEAD = 56
+SHARE_HEAD = 52
 SHARE_FREE = 56
 SHARE_BUSY = 32
 TURNED = 3
@@ -31,9 +31,11 @@ FIRST = (1, 8, 3)
 WS = 3
 SHARE_LEAD = 80
 SHARE_MID = 28
-WT = 2
-LEAD = 24
-CUT0 = 1024
+SW = ((0, 3), (1, 3))
+F0AT = 4
+TAILCUT = 48
+LEAD = 28
+CUT0 = (1024,)
 PRE = 0
 MID = 0
 
@@ -60,7 +62,7 @@ def tile_fock_orbital_blocks_d4_kernel(tc, c_bytes, c_scale, fock, occ, v_words,
         occ_row = keep.tile([P, O], BF16, name="occ_row")
         scale_sb = keep.tile([P, OT * N // B], F32, name="scale_sb")
         occ_sb = keep.tile([P, OT], BF16, name="occ_sb")
-        warm = keep.tile([P, 1], F32, name="warm")
+        warm = keep.tile([P, P + 2], F32, name="warm")
         occ_f32 = keep.tile([P, OT], F32, name="occ_f32")
         c_raw = [keep.tile([P, N], U8, name=f"c_raw{a}") for a in range(OT)]
         c_grp = [keep.tile([P, 2, O, 4], BF16, name=f"c_grp{h}", align_bytes=64) for h in range(2)]
@@ -85,18 +87,21 @@ def tile_fock_orbital_blocks_d4_kernel(tc, c_bytes, c_scale, fock, occ, v_words,
             raws[s] = raw
 
         c_rows = c_bytes.rearrange("(p a) n -> a p n", a=OT)
-        for cols in (slice(0, CUT0), slice(CUT0, N)):
+        for cols in [slice(x, y) for x, y in zip((0,) + CUT0, CUT0 + (N,))]:
             nc.sync.dma_start(out=c_raw[0][:, cols], in_=c_rows[0][:, cols])
         for a in range(1, OT):
-            if a == OT - 1:
+            if a == F0AT:
                 load_fock(0)
             nc.sync.dma_start(out=c_raw[a][:], in_=c_rows[a])
+        if 0 not in raws:
+            load_fock(0)
         nc.sync.dma_start(out=occ_sb[:], in_=occ.rearrange("(p a) -> p a", a=OT))
         for s in FIRST:
             load_fock(s)
         make_identity(nc, ident[:])
         make_identity(nc, ident_bf[:])
-        nc.scalar.activation(warm[:], ident[:, 0:1], COPY, scale=ident[:, 0:1])
+        nc.vector.memset(warm[:], 0.0)
+        nc.scalar.activation(warm[:, P : P + 1], warm[:, 1:2], COPY, scale=warm[:, 1:2])
         nc.vector.memset(v_planes[:].rearrange("p g n -> p (g n)").bitcast(U32), 0)
         for s in range(G, STEPS):
             if s not in raws:
@@ -111,7 +116,7 @@ def tile_fock_orbital_blocks_d4_kernel(tc, c_bytes, c_scale, fock, occ, v_words,
         c_wide, c_turned, grps = {}, {}, {}
 
         def on_scalar(a, g):
-            return a < WT and g >= WS
+            return (a, g) in SW
 
         def widen(a):
             for g in range(G):
@@ -196,8 +201,8 @@ def tile_fock_orbital_blocks_d4_kernel(tc, c_bytes, c_scale, fock, occ, v_words,
                 dst = grps[s][:].rearrange("p (c i) j -> p c j i", i=4)
             else:
                 cut = cut // 2
-                src = raws[s][:].rearrange("p j (c m t) -> p c t m j", m=2, t=4)
-                dst = grps[s][:].rearrange("p (t c m) j -> p c t m j", m=2, t=4)
+                src = raws[s][:].rearrange("p j (c m t) -> p c t j m", m=2, t=4)
+                dst = grps[s][:].rearrange("p (t c m) j -> p c t j m", m=2, t=4)
             runs = dst.shape[1]
             mid = min(runs, cut + LEAD * runs // P)
             lo, hi = {None: (cut, runs), 0: (cut, mid), 1: (mid, runs)}[part]
@@ -352,8 +357,8 @@ def tile_fock_orbital_blocks_d4_kernel(tc, c_bytes, c_scale, fock, occ, v_words,
         def heat(where, n):
             if n:
                 idle = bank(where)
-                rhs = ident[:].unsqueeze(1).to_broadcast([P, n, P])
-                nc.tensor.matmul(idle[:, : n * P], lhsT=ident[:], rhs=rhs, start=True, stop=True)
+                rhs = warm[:, :P].unsqueeze(1).to_broadcast([P, n, P])
+                nc.tensor.matmul(idle[:, : n * P], lhsT=warm[:, :P], rhs=rhs, start=True, stop=True)
 
         heat(7, PRE)
         widen(0)
@@ -393,11 +398,11 @@ def tile_fock_orbital_blocks_d4_kernel(tc, c_bytes, c_scale, fock, occ, v_words,
         interleave(1, False)
         untangle_fock(2)
         quantise_c(1)
-        interleave(3, True)
+        quantise_c(2)
         quantise_fock(1)
         stage1(1, even + odd)
         interleave(3, False)
-        quantise_c(2)
+        interleave(3, True)
         quantise_fock(2)
         stage1(2, even + odd)
         quantise_c(3)
@@ -475,11 +480,10 @@ def tile_fock_orbital_blocks_d4_kernel(tc, c_bytes, c_scale, fock, occ, v_words,
         for a in range(OT):
             stage2(a, 0, [last - 1])
         for t in range(4):
-            weigh_slot(last, t, halves[0])
-        interleave_half(last, 0, False, 64)
-        for t in range(4):
-            weigh_slot(last, t, halves[1])
-        interleave_half(last, 1, True, 0)
+            weigh_slot(last, t, slice(0, O))
+        interleave_half(last, 1, False, TAILCUT)
+        interleave_half(last, 0, True, 0)
+        interleave_half(last, 1, True, TAILCUT)
         quantise_half(last, 0)
         quantise_half(last, 1)
         for a in range(OT):

@@ -33,7 +33,7 @@ SHARE_LEAD = 80
 SHARE_MID = 28
 SW = ((0, 3), (1, 3))
 F0AT = 4
-TAILCUT = 48
+TAILCUT = 96
 LEAD = 28
 CUT0 = (1024,)
 PRE = 0
@@ -70,7 +70,7 @@ def tile_fock_orbital_blocks_d4_kernel(tc, c_bytes, c_scale, fock, occ, v_words,
         c_planes = [keep.tile([P, O], U8, name=f"c_planes{g}", align_bytes=64) for g in range(G)]
         h_codes = [keep.tile([P, O], U32, name=f"h_codes{g}", align_bytes=64) for g in range(G)]
         h_planes = [keep.tile([P, O], U8, name=f"h_planes{g}", align_bytes=64) for g in range(G)]
-        v_sb = keep.tile([P, G, 2 * V], U8, name="v_sb", align_bytes=64)
+        v_sb = [keep.tile([P, G, 2 * W], U8, name=f"v_sb{n}", align_bytes=64) for n in range(V // W)]
         v_planes = keep.tile([P, G, V], U8, name="v_planes", align_bytes=64)
 
         ctx.enter_context(tc.manual_schedule())
@@ -111,7 +111,9 @@ def tile_fock_orbital_blocks_d4_kernel(tc, c_bytes, c_scale, fock, occ, v_words,
                 out=v_planes[32 * q : 32 * q + 4, :, :].bitcast(I32),
                 in_=v_scales[:, 4 * q : 4 * q + 4, :].rearrange("g r n -> r g n").bitcast(I32),
             )
-        nc.sync.dma_start(out=v_sb[:].bitcast(I32), in_=v_words.rearrange("g p n -> p g n").bitcast(I32))
+        v_rows = v_words.rearrange("g p n -> p g n")
+        for n in range(V // W):
+            nc.sync.dma_start(out=v_sb[n][:].bitcast(I32), in_=v_rows[:, :, n * 2 * W : (n + 1) * 2 * W].bitcast(I32))
 
         c_wide, c_turned, grps = {}, {}, {}
 
@@ -197,8 +199,9 @@ def tile_fock_orbital_blocks_d4_kernel(tc, c_bytes, c_scale, fock, occ, v_words,
             if s == G + 2:
                 cut = 0
             if s < G * TURNED:
-                src = raws[s][:].rearrange("p j (c i) -> p c j i", i=4)
-                dst = grps[s][:].rearrange("p (c i) j -> p c j i", i=4)
+                cut = cut * 2
+                src = raws[s][:].rearrange("p j (c i) -> p c j i", i=2)
+                dst = grps[s][:].rearrange("p (c i) j -> p c j i", i=2)
             else:
                 cut = cut // 2
                 src = raws[s][:].rearrange("p j (c m t) -> p c t j m", m=2, t=4)
@@ -259,8 +262,8 @@ def tile_fock_orbital_blocks_d4_kernel(tc, c_bytes, c_scale, fock, occ, v_words,
         def interleave_half(g, h, on_vector, cut):
             if (g, h) not in h_grp:
                 h_grp[g, h] = turn_pool.tile([P, 256, 4], BF16, name="h_grp", align_bytes=64)
-            src = h_slots[g][:, :, 256 * h : 256 * (h + 1)].rearrange("p j (c i) -> p c j i", i=4)
-            dst = h_grp[g, h][:].rearrange("p (c i) j -> p c j i", i=4)
+            src = h_slots[g][:, :, 256 * h : 256 * (h + 1)].rearrange("p j (c i) -> p c j i", i=2)
+            dst = h_grp[g, h][:].rearrange("p (c i) j -> p c j i", i=2)
             if on_vector:
                 nc.vector.tensor_copy(out=dst[:, cut:], in_=src[:, cut:])
             else:
@@ -297,7 +300,7 @@ def tile_fock_orbital_blocks_d4_kernel(tc, c_bytes, c_scale, fock, occ, v_words,
                 if n == 0:
                     rhs, rhs_scale = c_codes[g][:].bitcast(FP8X4), c_planes[g][:]
                 else:
-                    rhs = v_sb[:, g, (n - 1) * 2 * W : n * 2 * W].bitcast(FP4X4)
+                    rhs = v_sb[n - 1][:, g, :].bitcast(FP4X4)
                     rhs_scale = v_planes[:, g, (n - 1) * W : n * W]
                 nc.tensor.matmul_mx(
                     out=accs[a, n][:],
@@ -342,7 +345,7 @@ def tile_fock_orbital_blocks_d4_kernel(tc, c_bytes, c_scale, fock, occ, v_words,
                         out=acc[:, c : c + P],
                         lhsT=h_codes[g][:, a * P : (a + 1) * P].bitcast(FP8X4),
                         lhsT_scale=h_planes[g][:, a * P : (a + 1) * P],
-                        rhs=v_sb[:, g, 2 * (col + c) : 2 * (col + c + P)].bitcast(FP4X4),
+                        rhs=v_sb[col // W][:, g, 2 * (col % W + c) : 2 * (col % W + c + P)].bitcast(FP4X4),
                         rhs_scale=v_planes[:, g, col + c : col + c + P],
                         start=(g == 0),
                         stop=(g == G - 1),

@@ -18,26 +18,22 @@ P = 128
 N, O, V = 2048, 512, 1536
 W = 512
 G = N // W
+LAST = G - 1
 OT = O // P
 B = 128
-STEPS = G * G
+PIECES = G * G
+BANKS = 8
+HALF = O // 2
 
-SHARE_HEAD = 52
-SHARE_FREE = 56
-SHARE_BUSY = 32
-TURNED = 3
-WARM = 1
-FIRST = (1, 8, 3)
-WS = 3
-SHARE_LEAD = 80
-SHARE_MID = 28
-SW = ((0, 3), (1, 3))
-F0AT = 4
-TAILCUT = 96
-LEAD = 28
-CUT0 = (1024,)
-PRE = 0
-MID = 0
+DMA_ALIGN = 256
+
+MIRRORED, MIRROR_SOURCE = 2, 2 * G
+
+SHARE_USUAL = 192
+SHARE_AHEAD = 320
+SHARE_BUSY = 112
+LEAD = 112
+TAIL_SHARE = 192
 
 FLOPS = 2 * O * N * N + 2 * O * N * (O + V)
 
@@ -46,12 +42,12 @@ def tile_fock_orbital_blocks_d4_kernel(tc, c_bytes, c_scale, fock, occ, v_words,
     nc = tc.nc
     with ExitStack() as ctx:
         keep = ctx.enter_context(tc.tile_pool(name="keep", bufs=1))
-        raw_pool = ctx.enter_context(tc.tile_pool(name="raw", bufs=STEPS))
+        raw_pool = ctx.enter_context(tc.tile_pool(name="raw", bufs=PIECES))
         grp_pool = ctx.enter_context(tc.tile_pool(name="grp", bufs=6))
         code_pool = ctx.enter_context(tc.tile_pool(name="code", bufs=6))
         wide_pool = ctx.enter_context(tc.tile_pool(name="wide", bufs=8))
         turn_pool = ctx.enter_context(tc.tile_pool(name="turn", bufs=2))
-        out_pool = ctx.enter_context(tc.tile_pool(name="outs", bufs=8))
+        out_pool = ctx.enter_context(tc.tile_pool(name="outs", bufs=BANKS))
         psum = ctx.enter_context(tc.psum_pool(name="psum", bufs=1))
 
         def bank(i):
@@ -62,16 +58,17 @@ def tile_fock_orbital_blocks_d4_kernel(tc, c_bytes, c_scale, fock, occ, v_words,
         occ_row = keep.tile([P, O], BF16, name="occ_row")
         scale_sb = keep.tile([P, OT * N // B], F32, name="scale_sb")
         occ_sb = keep.tile([P, OT], BF16, name="occ_sb")
-        warm = keep.tile([P, P + 2], F32, name="warm")
+        warm = keep.tile([P, 2], F32, name="warm")
         occ_f32 = keep.tile([P, OT], F32, name="occ_f32")
-        c_raw = [keep.tile([P, N], U8, name=f"c_raw{a}") for a in range(OT)]
+        c_raw = [keep.tile([P, N], U8, name=f"c_raw{a}", align_bytes=DMA_ALIGN) for a in range(OT)]
         c_grp = [keep.tile([P, 2, O, 4], BF16, name=f"c_grp{h}", align_bytes=64) for h in range(2)]
         c_codes = [keep.tile([P, O], U32, name=f"c_codes{g}", align_bytes=64) for g in range(G)]
-        c_planes = [keep.tile([P, O], U8, name=f"c_planes{g}", align_bytes=64) for g in range(G)]
+        c_scales = [keep.tile([P, O], U8, name=f"c_scales{g}", align_bytes=64) for g in range(G)]
         h_codes = [keep.tile([P, O], U32, name=f"h_codes{g}", align_bytes=64) for g in range(G)]
-        h_planes = [keep.tile([P, O], U8, name=f"h_planes{g}", align_bytes=64) for g in range(G)]
-        v_sb = [keep.tile([P, G, 2 * W], U8, name=f"v_sb{n}", align_bytes=64) for n in range(V // W)]
-        v_planes = keep.tile([P, G, V], U8, name="v_planes", align_bytes=64)
+        h_scales = [keep.tile([P, O], U8, name=f"h_scales{g}", align_bytes=64) for g in range(G)]
+        h_slots = keep.tile([P, 4, O], BF16, name="h_slots")
+        v_sb = [keep.tile([P, G, 2 * W], U8, name=f"v_sb{n}", align_bytes=DMA_ALIGN) for n in range(V // W)]
+        v_scale_sb = keep.tile([P, G, V], U8, name="v_scale_sb", align_bytes=64)
 
         ctx.enter_context(tc.manual_schedule())
 
@@ -80,52 +77,49 @@ def tile_fock_orbital_blocks_d4_kernel(tc, c_bytes, c_scale, fock, occ, v_words,
 
         def load_fock(s):
             g, k = divmod(s, G)
-            raw = raw_pool.tile([P, 4, W], BF16, name="raw")
+            raw = raw_pool.tile([P, 4, W], BF16, name="raw", align_bytes=DMA_ALIGN)
             nc.sync.dma_start(
-                out=raw[:], in_=fock[k * W : (k + 1) * W, g * W : (g + 1) * W].rearrange("(p j) n -> p j n", j=4)
+                out=raw[:], in_=fock[k * W : (k + 1) * W, g * W : (g + 1) * W].rearrange("(p t) n -> p t n", t=4)
             )
             raws[s] = raw
 
         c_rows = c_bytes.rearrange("(p a) n -> a p n", a=OT)
-        for cols in [slice(x, y) for x, y in zip((0,) + CUT0, CUT0 + (N,))]:
+        for cols in (slice(0, N // 2), slice(N // 2, N)):
             nc.sync.dma_start(out=c_raw[0][:, cols], in_=c_rows[0][:, cols])
         for a in range(1, OT):
-            if a == F0AT:
-                load_fock(0)
             nc.sync.dma_start(out=c_raw[a][:], in_=c_rows[a])
-        if 0 not in raws:
-            load_fock(0)
+        load_fock(0)
         nc.sync.dma_start(out=occ_sb[:], in_=occ.rearrange("(p a) -> p a", a=OT))
-        for s in FIRST:
-            load_fock(s)
+        for s in range(1, G):
+            load_fock(MIRROR_SOURCE if s == MIRRORED else s)
         make_identity(nc, ident[:])
         make_identity(nc, ident_bf[:])
         nc.vector.memset(warm[:], 0.0)
-        nc.scalar.activation(warm[:, P : P + 1], warm[:, 1:2], COPY, scale=warm[:, 1:2])
-        nc.vector.memset(v_planes[:].rearrange("p g n -> p (g n)").bitcast(U32), 0)
-        for s in range(G, STEPS):
-            if s not in raws:
+        nc.scalar.activation(warm[:, 0:1], warm[:, 1:2], COPY, scale=warm[:, 1:2])
+        nc.vector.memset(v_scale_sb[:].rearrange("p g n -> p (g n)").bitcast(U32), 0)
+        for s in range(G, PIECES):
+            if s != MIRROR_SOURCE:
                 load_fock(s)
         for q in range(4):
             nc.sync.dma_start(
-                out=v_planes[32 * q : 32 * q + 4, :, :].bitcast(I32),
+                out=v_scale_sb[32 * q : 32 * q + 4, :, :].bitcast(I32),
                 in_=v_scales[:, 4 * q : 4 * q + 4, :].rearrange("g r n -> r g n").bitcast(I32),
             )
         v_rows = v_words.rearrange("g p n -> p g n")
         for n in range(V // W):
             nc.sync.dma_start(out=v_sb[n][:].bitcast(I32), in_=v_rows[:, :, n * 2 * W : (n + 1) * 2 * W].bitcast(I32))
 
-        c_wide, c_turned, grps = {}, {}, {}
+        c_wide, c_turned = {}, {}
 
         def on_scalar(a, g):
-            return (a, g) in SW
+            return (a == 0 and g % 2 == 1) or (a == 1 and g == LAST)
 
         def widen(a):
             for g in range(G):
                 wide = wide_pool.tile([P, W], BF16, name="c_wide")
                 for b in range(W // B):
                     src = c_raw[a][:, g * W + b * B : g * W + (b + 1) * B].bitcast(FP8)
-                    i = a * (N // B) + 4 * g + b
+                    i = a * (N // B) + (W // B) * g + b
                     scale = scale_sb[:, i : i + 1]
                     if on_scalar(a, g):
                         nc.scalar.activation(wide[:, b * B : (b + 1) * B], src, COPY, scale=scale)
@@ -142,242 +136,224 @@ def tile_fock_orbital_blocks_d4_kernel(tc, c_bytes, c_scale, fock, occ, v_words,
                     g = 2 * h + g2
                     words = c_wide[a, g][:].bitcast(F32)
                     for u in range(2):
-                        col = 256 * g2 + P * u
-                        in_ = words[:, u : 256 : 2] if on_scalar(a, g) else words[:, P * u : P * (u + 1)]
+                        col = 2 * P * g2 + P * u
+                        in_ = words[:, u : 2 * P : 2] if on_scalar(a, g) else words[:, P * u : P * (u + 1)]
                         nc.tensor.transpose(xt[:, col : col + P], in_, ident[:])
                 c_turned[a, h] = xt
 
-        f_turned = {}
-
-        def turn_fock(k, first):
-            for h in range(2):
-                xt = bank(first + h)
-                for j2 in range(2):
-                    words = raws[G * k][:, 2 * h + j2, :].bitcast(F32)
-                    for u in range(2):
-                        col = 256 * j2 + P * u
-                        nc.tensor.transpose(xt[:, col : col + P], words[:, u : 256 : 2], ident[:])
-                f_turned[k, h] = xt
-
-        def untangle_fock(k):
-            grps[k] = grp_pool.tile([P, W, 4], BF16, name="grp", align_bytes=64)
-            words = grps[k][:].rearrange("p n j -> p (n j)").bitcast(F32).rearrange("p (m h w) -> p h m w", h=2, w=4)
-            for h in range(2):
-                nc.scalar.copy(words[:, h], f_turned[k, h][:].rearrange("p (w m) -> p m w", w=4))
-
-        def untangle(dst, xt, on_vector):
-            out = dst.rearrange("p r j -> p (r j)").bitcast(F32).rearrange("p (a r u) -> p a r u", a=2, u=2)
-            in_ = xt[:].rearrange("p (a u r) -> p a r u", a=2, u=2)
-            if on_vector:
-                nc.vector.tensor_copy(out=out, in_=in_)
-            else:
-                nc.scalar.copy(out, in_)
-
-        def untangle_c(a, halves=range(2)):
-            for h in halves:
-                out = c_grp[h][:, :, a * P : (a + 1) * P, :].rearrange("p g r j -> p g (r j)").bitcast(F32)
-                nc.scalar.copy(
-                    out.rearrange("p g (r u) -> p g r u", u=2),
-                    c_turned[a, h][:].rearrange("p (g u r) -> p g r u", g=2, u=2),
-                )
+        def untangle_c(a, h):
+            out = c_grp[h][:, :, a * P : (a + 1) * P, :].rearrange("p g r t -> p g (r t)").bitcast(F32)
+            nc.scalar.copy(
+                out.rearrange("p g (r u) -> p g r u", u=2),
+                c_turned[a, h][:].rearrange("p (g u r) -> p g r u", g=2, u=2),
+            )
 
         def quantise_c(g):
             nc.vector.quantize_mx(
                 out=c_codes[g][:].bitcast(FP8X4),
-                scales=c_planes[g][:],
-                in_=c_grp[g // 2][:, g % 2].rearrange("p o j -> p (o j)"),
+                scales=c_scales[g][:],
+                in_=c_grp[g // 2][:, g % 2].rearrange("p o t -> p (o t)"),
             )
 
-        f_codes, f_planes = {}, {}
+        grps, f_codes, f_scales, mirror_banks = {}, {}, {}, {}
 
-        def interleave(s, on_vector, part=None):
-            if s >= STEPS:
-                return
+        def turn_mirror(first_bank):
+            for h in range(2):
+                xt = bank(first_bank + h)
+                for j2 in range(2):
+                    words = raws[MIRROR_SOURCE][:, 2 * h + j2, :].bitcast(F32)
+                    for u in range(2):
+                        col = 2 * P * j2 + P * u
+                        nc.tensor.transpose(xt[:, col : col + P], words[:, u : 2 * P : 2], ident[:])
+                mirror_banks[h] = xt
+
+        def untangle_mirror():
+            grp = grp_pool.tile([P, W, 4], BF16, name="grp", align_bytes=64)
+            words = grp[:].rearrange("p n t -> p (n t)").bitcast(F32).rearrange("p (m h w) -> p h m w", h=2, w=4)
+            for h in range(2):
+                nc.scalar.copy(words[:, h], mirror_banks[h][:].rearrange("p (w m) -> p m w", w=4))
+            grps[MIRRORED] = grp
+
+        def scalar_share(s):
+            g, k = divmod(s, G)
+            if g == 0 or (g == LAST and k < 2):
+                return SHARE_USUAL
+            if g == 1 and k < 2:
+                return SHARE_AHEAD
+            return 0 if s == G + 2 else SHARE_BUSY
+
+        def interleave(s, lo, hi, engine_copy):
             if s not in grps:
                 grps[s] = grp_pool.tile([P, W, 4], BF16, name="grp", align_bytes=64)
-            cut = SHARE_HEAD if s < G else SHARE_LEAD if s < G + 2 else SHARE_BUSY if s % G >= 2 else SHARE_MID if s < 3 * G else SHARE_FREE
-            if s == G + 2:
-                cut = 0
-            if s < G * TURNED:
-                cut = cut * 2
-                src = raws[s][:].rearrange("p j (c i) -> p c j i", i=2)
-                dst = grps[s][:].rearrange("p (c i) j -> p c j i", i=2)
+            if s < G * LAST:
+                step = 2
+                src = raws[s][:].rearrange("p t (c i) -> p c t i", i=step)
+                dst = grps[s][:].rearrange("p (c i) t -> p c t i", i=step)
             else:
-                cut = cut // 2
-                src = raws[s][:].rearrange("p j (c m t) -> p c t j m", m=2, t=4)
-                dst = grps[s][:].rearrange("p (t c m) j -> p c t j m", m=2, t=4)
-            runs = dst.shape[1]
-            mid = min(runs, cut + LEAD * runs // P)
-            lo, hi = {None: (cut, runs), 0: (cut, mid), 1: (mid, runs)}[part]
-            if on_vector and lo < hi:
-                nc.vector.tensor_copy(out=dst[:, lo:hi], in_=src[:, lo:hi])
-            elif not on_vector and cut > 0:
-                nc.scalar.copy(dst[:, :cut], src[:, :cut])
+                step = 8
+                src = raws[s][:].rearrange("p t (c i j) -> p c j t i", i=2, j=4)
+                dst = grps[s][:].rearrange("p (j c i) t -> p c j t i", i=2, j=4)
+            engine_copy(dst[:, lo // step : hi // step], src[:, lo // step : hi // step])
+
+        def vector_copy(out, in_):
+            nc.vector.tensor_copy(out=out, in_=in_)
+
+        def scalar_part(s):
+            interleave(s, 0, scalar_share(s), nc.scalar.copy)
+
+        def vector_part(s):
+            interleave(s, scalar_share(s), W, vector_copy)
+
+        def vector_lead(s):
+            interleave(s, scalar_share(s), scalar_share(s) + LEAD, vector_copy)
+
+        def vector_rest(s):
+            interleave(s, scalar_share(s) + LEAD, W, vector_copy)
 
         def quantise_fock(s):
             codes = code_pool.tile([P, W], U32, name="f_codes", align_bytes=64)
-            planes = code_pool.tile([P, W], U8, name="f_planes", align_bytes=64)
+            scales = code_pool.tile([P, W], U8, name="f_scales", align_bytes=64)
             nc.vector.quantize_mx(
-                out=codes[:].bitcast(FP8X4), scales=planes[:], in_=grps[s][:].rearrange("p n j -> p (n j)")
+                out=codes[:].bitcast(FP8X4), scales=scales[:], in_=grps[s][:].rearrange("p n t -> p (n t)")
             )
-            f_codes[s], f_planes[s] = codes, planes
+            f_codes[s], f_scales[s] = codes, scales
 
         s1_banks, h_wide, h_turned, h_grp = {}, {}, {}, {}
 
-        def stage1(s, tiles):
+        def group_bank(g, i):
+            return bank(i if g == 0 else OT + i)
+
+        def stage1(s, slices):
             g, k = divmod(s, G)
-            for a in tiles:
+            still, moving = (c_codes[k], c_scales[k]), (f_codes[s], f_scales[s])
+            if g == LAST:
+                still, moving = moving, still
+            for i in slices:
                 if k == 0:
-                    s1_banks[g, a] = bank(a if g == 0 else OT + a)
-                still, moving = (c_codes[k], c_planes[k]), (f_codes[s], f_planes[s])
-                if g >= TURNED:
-                    still, moving = moving, still
+                    s1_banks[g, i] = group_bank(g, i)
                 nc.tensor.matmul_mx(
-                    out=s1_banks[g, a][:],
-                    lhsT=still[0][:, a * P : (a + 1) * P].bitcast(FP8X4),
-                    lhsT_scale=still[1][:, a * P : (a + 1) * P],
+                    out=s1_banks[g, i][:],
+                    lhsT=still[0][:, i * P : (i + 1) * P].bitcast(FP8X4),
+                    lhsT_scale=still[1][:, i * P : (i + 1) * P],
                     rhs=moving[0][:].bitcast(FP8X4),
                     rhs_scale=moving[1][:],
                     start=(k == 0),
-                    stop=(k == G - 1),
+                    stop=(k == LAST),
                 )
 
-        def weigh(g, a, on_vector=False):
+        def weigh(g, a):
             wide = wide_pool.tile([P, W], BF16, name="h_wide")
             out = wide[:].rearrange("p (u m e) -> p u m e", u=2, e=2)
             in_ = s1_banks[g, a][:].rearrange("p (m u e) -> p u m e", u=2, e=2)
-            if on_vector:
-                nc.vector.tensor_scalar(out, in_, occ_f32[:, a : a + 1], None, MULT)
-            else:
-                nc.scalar.activation(out, in_, COPY, scale=occ_f32[:, a : a + 1])
+            nc.scalar.activation(out, in_, COPY, scale=occ_f32[:, a : a + 1])
             h_wide[g, a] = wide
 
-        h_slots = {}
+        def turn_half(g):
+            for h in range(2):
+                xt = group_bank(g, 2 * h)
+                for a2 in range(2):
+                    words = h_wide[g, 2 * h + a2][:].bitcast(F32)
+                    for u in range(2):
+                        col = 2 * P * a2 + P * u
+                        nc.tensor.transpose(xt[:, col : col + P], words[:, P * u : P * (u + 1)], ident[:])
+                h_turned[g, h] = xt
 
-        def weigh_slot(g, t, cols):
-            if g not in h_slots:
-                h_slots[g] = turn_pool.tile([P, 4, O], BF16, name="h_slots")
-            nc.vector.tensor_tensor(h_slots[g][:, t, cols], s1_banks[g, t][:, cols], occ_row[:, cols], MULT)
+        def untangle_half(g):
+            for h in range(2):
+                grp = turn_pool.tile([P, HALF, 4], BF16, name="h_grp", align_bytes=64)
+                out = grp[:].rearrange("p r t -> p (r t)").bitcast(F32).rearrange("p (a r u) -> p a r u", a=2, u=2)
+                nc.scalar.copy(out, h_turned[g, h][:].rearrange("p (a u r) -> p a r u", a=2, u=2))
+                h_grp[g, h] = grp
 
-        def interleave_half(g, h, on_vector, cut):
-            if (g, h) not in h_grp:
-                h_grp[g, h] = turn_pool.tile([P, 256, 4], BF16, name="h_grp", align_bytes=64)
-            src = h_slots[g][:, :, 256 * h : 256 * (h + 1)].rearrange("p j (c i) -> p c j i", i=2)
-            dst = h_grp[g, h][:].rearrange("p (c i) j -> p c j i", i=2)
-            if on_vector:
-                nc.vector.tensor_copy(out=dst[:, cut:], in_=src[:, cut:])
-            else:
-                nc.scalar.copy(dst[:, :cut], src[:, :cut])
+        def weigh_slot(t):
+            nc.vector.tensor_tensor(h_slots[:, t, :], s1_banks[LAST, t][:], occ_row[:], MULT)
 
-        def turn_half(g, h):
-            xt = bank(2 * h if g == 0 else OT + 2 * h)
-            for a2 in range(2):
-                words = h_wide[g, 2 * h + a2][:].bitcast(F32)
-                for u in range(2):
-                    col = 256 * a2 + P * u
-                    nc.tensor.transpose(xt[:, col : col + P], words[:, P * u : P * (u + 1)], ident[:])
-            h_turned[g, h] = xt
-
-        def untangle_half(g, h, on_vector=False):
-            grp = turn_pool.tile([P, 256, 4], BF16, name="h_grp", align_bytes=64)
-            untangle(grp[:], h_turned[g, h], on_vector)
-            h_grp[g, h] = grp
+        def interleave_last_half(h, lo, hi, engine_copy):
+            if (LAST, h) not in h_grp:
+                h_grp[LAST, h] = turn_pool.tile([P, HALF, 4], BF16, name="h_grp", align_bytes=64)
+            src = h_slots[:, :, HALF * h : HALF * (h + 1)].rearrange("p t (c i) -> p c t i", i=2)
+            dst = h_grp[LAST, h][:].rearrange("p (c i) t -> p c t i", i=2)
+            engine_copy(dst[:, lo // 2 : hi // 2], src[:, lo // 2 : hi // 2])
 
         def quantise_half(g, h):
-            cols = slice(256 * h, 256 * (h + 1))
+            cols = slice(HALF * h, HALF * (h + 1))
             nc.vector.quantize_mx(
                 out=h_codes[g][:, cols].bitcast(FP8X4),
-                scales=h_planes[g][:, cols],
-                in_=h_grp[g, h][:].rearrange("p o j -> p (o j)"),
+                scales=h_scales[g][:, cols],
+                in_=h_grp[g, h][:].rearrange("p o t -> p (o t)"),
             )
 
         accs = {}
 
-        def stage2(a, n, passes, where=None):
+        def stage2(a, n, passes):
             for g in passes:
-                if g == 0:
-                    accs[a, n] = bank(where)
                 if n == 0:
-                    rhs, rhs_scale = c_codes[g][:].bitcast(FP8X4), c_planes[g][:]
+                    rhs, rhs_scale = c_codes[g][:].bitcast(FP8X4), c_scales[g][:]
                 else:
                     rhs = v_sb[n - 1][:, g, :].bitcast(FP4X4)
-                    rhs_scale = v_planes[:, g, (n - 1) * W : n * W]
+                    rhs_scale = v_scale_sb[:, g, (n - 1) * W : n * W]
                 nc.tensor.matmul_mx(
                     out=accs[a, n][:],
                     lhsT=h_codes[g][:, a * P : (a + 1) * P].bitcast(FP8X4),
-                    lhsT_scale=h_planes[g][:, a * P : (a + 1) * P],
+                    lhsT_scale=h_scales[g][:, a * P : (a + 1) * P],
                     rhs=rhs,
                     rhs_scale=rhs_scale,
                     start=(g == 0),
-                    stop=(g == G - 1),
+                    stop=(g == LAST),
                 )
+
+        def f_oo_pass(g):
+            for a in range(OT):
+                if g == 0:
+                    accs[a, 0] = bank(a)
+                stage2(a, 0, [g])
 
         oo_rows = f_oo.rearrange("(p a) n -> a p n", a=OT)
         ov_rows = f_ov.rearrange("(p a) n -> a p n", a=OT)
+        in_turn = (vector_copy, nc.scalar.copy)
 
-        def empty(out, in_, on_vector):
-            if on_vector:
-                nc.vector.tensor_copy(out=out, in_=in_)
-            else:
-                nc.scalar.copy(out, in_)
-
-        def store(a, n, on_vector, pieces=1):
-            res = out_pool.tile([P, W], F32, name="res")
+        def store(a, n, engine_copy, parts):
+            res = out_pool.tile([P, W], F32, name="res", align_bytes=DMA_ALIGN)
             if n == 0:
-                empty(
-                    res[:].rearrange("p (q b) -> p q b", b=OT),
-                    accs[a, n][:].rearrange("p (b q) -> p q b", b=OT),
-                    on_vector,
+                engine_copy(
+                    res[:].rearrange("p (q b) -> p q b", b=OT), accs[a, n][:].rearrange("p (b q) -> p q b", b=OT)
                 )
                 nc.sync.dma_start(out=oo_rows[a], in_=res[:])
             else:
-                width = W // pieces
+                width = W // parts
                 for c in range(0, W, width):
                     col = (n - 1) * W + c
-                    empty(res[:, c : c + width], accs[a, n][:, c : c + width], on_vector)
+                    engine_copy(res[:, c : c + width], accs[a, n][:, c : c + width])
                     nc.sync.dma_start(out=ov_rows[a][:, col : col + width], in_=res[:, c : c + width])
 
-        def last_piece(a, col, width, where, on_vector):
+        def narrow_part(a, first, width, where, engine_copy):
             acc = bank(where)
-            for c in range(0, width, P):
+            for c in range(first, first + width, P):
                 for g in range(G):
                     nc.tensor.matmul_mx(
-                        out=acc[:, c : c + P],
+                        out=acc[:, c - first : c - first + P],
                         lhsT=h_codes[g][:, a * P : (a + 1) * P].bitcast(FP8X4),
-                        lhsT_scale=h_planes[g][:, a * P : (a + 1) * P],
-                        rhs=v_sb[col // W][:, g, 2 * (col % W + c) : 2 * (col % W + c + P)].bitcast(FP4X4),
-                        rhs_scale=v_planes[:, g, col + c : col + c + P],
+                        lhsT_scale=h_scales[g][:, a * P : (a + 1) * P],
+                        rhs=v_sb[-1][:, g, 2 * c : 2 * (c + P)].bitcast(FP4X4),
+                        rhs_scale=v_scale_sb[:, g, V - W + c : V - W + c + P],
                         start=(g == 0),
-                        stop=(g == G - 1),
+                        stop=(g == LAST),
                     )
-            res = out_pool.tile([P, W], F32, name="res")
-            empty(res[:, :width], acc[:, :width], on_vector)
-            queue = nc.scalar if col + width == V else nc.sync
-            queue.dma_start(out=ov_rows[a][:, col : col + width], in_=res[:, :width])
+            res = out_pool.tile([P, W], F32, name="res", align_bytes=DMA_ALIGN)
+            engine_copy(res[:, :width], acc[:, :width])
+            queue = nc.scalar if first + width == W else nc.sync
+            queue.dma_start(out=ov_rows[a][:, V - W + first : V - W + first + width], in_=res[:, :width])
 
         odd, even = (1, 3), (0, 2)
 
-        def heat(where, n):
-            if n:
-                idle = bank(where)
-                rhs = warm[:, :P].unsqueeze(1).to_broadcast([P, n, P])
-                nc.tensor.matmul(idle[:, : n * P], lhsT=warm[:, :P], rhs=rhs, start=True, stop=True)
-
-        heat(7, PRE)
-        widen(0)
-        turn_c(0)
-        heat(7, MID)
-        widen(1)
-        turn_c(1)
-        heat(7, MID)
-        untangle_c(0)
-        widen(2)
-        turn_c(2)
-        heat(7, MID)
-        untangle_c(1)
-        widen(3)
-        turn_c(3)
-        heat(1, WARM)
+        for a in range(OT):
+            widen(a)
+            turn_c(a)
+            if a in (1, 2):
+                for h in range(2):
+                    untangle_c(a - 1, h)
+        idle = bank(1)
+        nc.tensor.matmul(idle[:, :P], lhsT=ident[:], rhs=ident[:], start=True, stop=True)
         spread = psum.tile([P, 2 * W], BF16, name="spread", tag="bank0")
         for a in range(OT):
             nc.tensor.matmul(
@@ -387,120 +363,118 @@ def tile_fock_orbital_blocks_d4_kernel(tc, c_bytes, c_scale, fock, occ, v_words,
                 start=True,
                 stop=True,
             )
-        interleave(0, False)
+        scalar_part(0)
         for h in range(2):
-            untangle_c(2, [h])
-            untangle_c(3, [h])
-        turn_fock(2, 4)
+            untangle_c(2, h)
+            untangle_c(3, h)
+        turn_mirror(OT)
         nc.scalar.copy(occ_row[:], spread[:, :O])
-        interleave(0, True)
-        interleave(1, True)
+        vector_part(0)
+        vector_part(1)
         quantise_fock(0)
         quantise_c(0)
         stage1(0, even + odd)
-        interleave(1, False)
-        untangle_fock(2)
+        scalar_part(1)
+        untangle_mirror()
         quantise_c(1)
         quantise_c(2)
         quantise_fock(1)
         stage1(1, even + odd)
-        interleave(3, False)
-        interleave(3, True)
+        scalar_part(3)
+        vector_part(3)
         quantise_fock(2)
         stage1(2, even + odd)
         quantise_c(3)
         quantise_fock(3)
         stage1(3, range(OT))
-        interleave(G, False)
-        interleave(G + 1, False)
-        interleave(G, True)
+
+        s = G
+        scalar_part(s)
+        scalar_part(s + 1)
+        vector_part(s)
         nc.vector.tensor_copy(out=occ_f32[:], in_=occ_sb[:])
-        interleave(G + 1, True, 0)
-        quantise_fock(G)
-        stage1(G, range(OT))
+        vector_lead(s + 1)
+        quantise_fock(s)
+        stage1(s, range(OT))
         for a in range(OT):
             weigh(0, a)
-        interleave(G + 1, True, 1)
-        interleave(G + 2, True, 0)
-        quantise_fock(G + 1)
-        stage1(G + 1, odd + even)
-        turn_half(0, 0)
-        turn_half(0, 1)
-        interleave(G + 2, False)
-        interleave(G + 3, False)
-        interleave(G + 2, True, 1)
-        interleave(G + 3, True, 0)
-        untangle_half(0, 0)
-        untangle_half(0, 1)
-        quantise_fock(G + 2)
-        stage1(G + 2, odd + even)
-        interleave(G + 3, True, 1)
-        interleave(2 * G, False)
-        interleave(2 * G + 1, False)
-        interleave(2 * G, True, 0)
-        quantise_fock(G + 3)
+        vector_rest(s + 1)
+        vector_lead(s + 2)
+        quantise_fock(s + 1)
+        stage1(s + 1, odd + even)
+        turn_half(0)
+        scalar_part(s + 3)
+        vector_rest(s + 2)
+        vector_lead(s + 3)
+        untangle_half(0)
+        quantise_fock(s + 2)
+        stage1(s + 2, odd + even)
+        vector_rest(s + 3)
+        scalar_part(s + 4)
+        scalar_part(s + 5)
+        vector_lead(s + 4)
+        quantise_fock(s + 3)
         quantise_half(0, 0)
 
-        last = G - 1
-        for g in range(1, last):
+        for g in range(1, LAST):
             s = G * (g + 1)
             stage1(s - 1, odd + even)
             quantise_half(g - 1, 1)
-            for a in range(OT):
-                stage2(a, 0, [g - 1], a)
+            f_oo_pass(g - 1)
             for a in odd + even:
                 weigh(g, a)
-            interleave(s, True, 1 if g == 1 else None)
-            interleave(s + 1, True, 0)
+            if g == 1:
+                vector_rest(s)
+            else:
+                vector_part(s)
+            vector_lead(s + 1)
             quantise_fock(s)
-            interleave(s + 1, True, 1)
-            interleave(s + 2, True, 0)
+            vector_rest(s + 1)
+            vector_lead(s + 2)
             quantise_fock(s + 1)
             stage1(s, odd)
-            turn_half(g, 0)
-            turn_half(g, 1)
-            interleave(s + 2, False)
-            interleave(s + 2, True, 1)
-            untangle_half(g, 0)
-            untangle_half(g, 1)
+            turn_half(g)
+            scalar_part(s + 2)
+            vector_rest(s + 2)
+            untangle_half(g)
             stage1(s + 1, odd)
             for a in even:
                 stage1(s, [a])
                 stage1(s + 1, [a])
-            interleave(s + 3, False)
-            interleave(s + 3, True, 0)
+            scalar_part(s + 3)
+            vector_lead(s + 3)
             quantise_fock(s + 2)
-            interleave(s + 3, True, 1)
+            vector_rest(s + 3)
             quantise_half(g, 0)
             stage1(s + 2, odd + even)
-            interleave(s + 4, False)
-            interleave(s + 5, False)
+            if g + 1 < LAST:
+                scalar_part(s + 4)
+                scalar_part(s + 5)
             quantise_fock(s + 3)
 
-        halves = (slice(0, 256), slice(256, 512))
-        quantise_half(last - 1, 1)
-        stage1(STEPS - 1, range(4))
-        for a in range(OT):
-            stage2(a, 0, [last - 1])
+        quantise_half(LAST - 1, 1)
+        stage1(PIECES - 1, range(4))
+        f_oo_pass(LAST - 1)
         for t in range(4):
-            weigh_slot(last, t, slice(0, O))
-        interleave_half(last, 1, False, TAILCUT)
-        interleave_half(last, 0, True, 0)
-        interleave_half(last, 1, True, TAILCUT)
-        quantise_half(last, 0)
-        quantise_half(last, 1)
+            weigh_slot(t)
+        interleave_last_half(1, 0, TAIL_SHARE, nc.scalar.copy)
+        interleave_last_half(0, 0, HALF, vector_copy)
+        interleave_last_half(1, TAIL_SHARE, HALF, vector_copy)
+        quantise_half(LAST, 0)
+        quantise_half(LAST, 1)
         for a in range(OT):
-            stage2(a, 1, range(last), OT + a)
-        done = [(a, n) for n in range(2) for a in range(OT)]
-        for i, (a, n) in enumerate(done):
-            stage2(a, n, [last])
-            store(a, n, i % 2 == 0)
-        rest = [(a, n) for n in range(1, 4) for a in range(OT) if (a, n) not in done]
-        order = range(8)
-        for i, (a, n) in enumerate(rest[:-1]):
-            stage2(a, n, range(G), order[i % 8])
-            store(a, n, i % 2 == 0, 2 if i == len(rest) - 2 else 1)
-        col = V - W
+            accs[a, 1] = bank(OT + a)
+            stage2(a, 1, range(LAST))
+        begun = [(a, n) for n in range(2) for a in range(OT)]
+        for i, (a, n) in enumerate(begun):
+            stage2(a, n, [LAST])
+            store(a, n, in_turn[i % 2], 1)
+        whole = [(a, n) for n in range(2, 4) for a in range(OT)][:-1]
+        for i, (a, n) in enumerate(whole):
+            accs[a, n] = bank(i)
+            stage2(a, n, range(G))
+            store(a, n, in_turn[i % 2], 2 if i == len(whole) - 1 else 1)
+        first = 0
         for i, width in enumerate((2 * P, P, P)):
-            last_piece(OT - 1, col, width, order[(len(rest) - 1 + i) % 8], i % 2 == 1)
-            col = col + width
+            narrow_part(OT - 1, first, width, (len(whole) + i) % BANKS, in_turn[(i + 1) % 2])
+            first = first + width

@@ -13,6 +13,7 @@ FP8X4 = mybir.dt.float8_e4m3fn_x4
 FP4X4 = mybir.dt.float4_e2m1fn_x4
 COPY = mybir.ActivationFunctionType.Copy
 MULT = mybir.AluOpType.mult
+ADD = mybir.AluOpType.add
 
 P = 128
 N, O, V = 2048, 512, 1536
@@ -27,13 +28,14 @@ HALF = O // 2
 
 DMA_ALIGN = 256
 
-MIRRORED, MIRROR_SOURCE = 2, 2 * G
+MIRRORED = (1, 2)
 
-SHARE_USUAL = 192
-SHARE_AHEAD = 320
-SHARE_BUSY = 112
-LEAD = 112
+SHARE = (0, 0, 0, 192, 192, 320, 224, 448, 320, 512, 224, 320, 256, 512, 224, 320)
+SHARE_POOL = 288
+S_WIDE = ((0, 1), (1, 1), (2, 1), (0, 3))
 TAIL_SHARE = 192
+
+AHEAD = 192
 
 FLOPS = 2 * O * N * N + 2 * O * N * (O + V)
 
@@ -43,9 +45,9 @@ def tile_fock_orbital_blocks_d4_kernel(tc, c_bytes, c_scale, fock, occ, v_words,
     with ExitStack() as ctx:
         keep = ctx.enter_context(tc.tile_pool(name="keep", bufs=1))
         raw_pool = ctx.enter_context(tc.tile_pool(name="raw", bufs=PIECES))
-        grp_pool = ctx.enter_context(tc.tile_pool(name="grp", bufs=6))
+        grp_pool = ctx.enter_context(tc.tile_pool(name="grp", bufs=4))
         code_pool = ctx.enter_context(tc.tile_pool(name="code", bufs=6))
-        wide_pool = ctx.enter_context(tc.tile_pool(name="wide", bufs=8))
+        wide_pool = ctx.enter_context(tc.tile_pool(name="wide", bufs=OT * G))
         turn_pool = ctx.enter_context(tc.tile_pool(name="turn", bufs=2))
         out_pool = ctx.enter_context(tc.tile_pool(name="outs", bufs=BANKS))
         psum = ctx.enter_context(tc.psum_pool(name="psum", bufs=1))
@@ -59,8 +61,11 @@ def tile_fock_orbital_blocks_d4_kernel(tc, c_bytes, c_scale, fock, occ, v_words,
         scale_sb = keep.tile([P, OT * N // B], F32, name="scale_sb")
         occ_sb = keep.tile([P, OT], BF16, name="occ_sb")
         warm = keep.tile([P, 2], F32, name="warm")
-        occ_f32 = keep.tile([P, OT], F32, name="occ_f32")
-        c_raw = [keep.tile([P, N], U8, name=f"c_raw{a}", align_bytes=DMA_ALIGN) for a in range(OT)]
+        c_raw = {
+            (a, h): keep.tile([P, N // 2], U8, name=f"c_raw{a}{h}", align_bytes=DMA_ALIGN)
+            for a in range(OT)
+            for h in range(2)
+        }
         c_grp = [keep.tile([P, 2, O, 4], BF16, name=f"c_grp{h}", align_bytes=64) for h in range(2)]
         c_codes = [keep.tile([P, O], U32, name=f"c_codes{g}", align_bytes=64) for g in range(G)]
         c_scales = [keep.tile([P, O], U8, name=f"c_scales{g}", align_bytes=64) for g in range(G)]
@@ -84,21 +89,25 @@ def tile_fock_orbital_blocks_d4_kernel(tc, c_bytes, c_scale, fock, occ, v_words,
             raws[s] = raw
 
         c_rows = c_bytes.rearrange("(p a) n -> a p n", a=OT)
-        for cols in (slice(0, N // 2), slice(N // 2, N)):
-            nc.sync.dma_start(out=c_raw[0][:, cols], in_=c_rows[0][:, cols])
-        for a in range(1, OT):
-            nc.sync.dma_start(out=c_raw[a][:], in_=c_rows[a])
+
+        def load_c(h):
+            for a in range(OT):
+                nc.sync.dma_start(out=c_raw[a, h][:], in_=c_rows[a][:, h * N // 2 : (h + 1) * N // 2])
+
+        load_c(0)
+        load_c(1)
         load_fock(0)
+        load_fock(G)
         nc.sync.dma_start(out=occ_sb[:], in_=occ.rearrange("(p a) -> p a", a=OT))
-        for s in range(1, G):
-            load_fock(MIRROR_SOURCE if s == MIRRORED else s)
+        load_fock(2 * G)
+        load_fock(3)
         make_identity(nc, ident[:])
         make_identity(nc, ident_bf[:])
         nc.vector.memset(warm[:], 0.0)
         nc.scalar.activation(warm[:, 0:1], warm[:, 1:2], COPY, scale=warm[:, 1:2])
         nc.vector.memset(v_scale_sb[:].rearrange("p g n -> p (g n)").bitcast(U32), 0)
         for s in range(G, PIECES):
-            if s != MIRROR_SOURCE:
+            if s not in (G, 2 * G):
                 load_fock(s)
         for q in range(4):
             nc.sync.dma_start(
@@ -111,35 +120,26 @@ def tile_fock_orbital_blocks_d4_kernel(tc, c_bytes, c_scale, fock, occ, v_words,
 
         c_wide, c_turned = {}, {}
 
-        def on_scalar(a, g):
-            return (a == 0 and g % 2 == 1) or (a == 1 and g == LAST)
+        def widen(a, g):
+            wide = wide_pool.tile([P, W], BF16, name="c_wide")
+            for b in range(W // B):
+                src = c_raw[a, g // 2][:, (g % 2) * W + b * B : (g % 2) * W + (b + 1) * B].bitcast(FP8)
+                i = a * (N // B) + (W // B) * g + b
+                scale = scale_sb[:, i : i + 1]
+                if (a, g) in S_WIDE:
+                    nc.scalar.activation(wide[:, b * B : (b + 1) * B], src, COPY, scale=scale)
+                else:
+                    nc.vector.tensor_scalar(wide[:, b * B : (b + 1) * B], src, scale, None, MULT)
+            c_wide[a, g] = wide
 
-        def widen(a):
-            for g in range(G):
-                wide = wide_pool.tile([P, W], BF16, name="c_wide")
-                for b in range(W // B):
-                    src = c_raw[a][:, g * W + b * B : g * W + (b + 1) * B].bitcast(FP8)
-                    i = a * (N // B) + (W // B) * g + b
-                    scale = scale_sb[:, i : i + 1]
-                    if on_scalar(a, g):
-                        nc.scalar.activation(wide[:, b * B : (b + 1) * B], src, COPY, scale=scale)
-                    else:
-                        dst = wide[:].rearrange("p (u m e) -> p m u e", u=2, e=2)[:, 32 * b : 32 * (b + 1)]
-                        src = src.rearrange("p (m u e) -> p m u e", u=2, e=2)
-                        nc.vector.tensor_scalar(dst, src, scale, None, MULT)
-                c_wide[a, g] = wide
-
-        def turn_c(a):
-            for h in range(2):
-                xt = bank(2 * a + h)
-                for g2 in range(2):
-                    g = 2 * h + g2
-                    words = c_wide[a, g][:].bitcast(F32)
-                    for u in range(2):
-                        col = 2 * P * g2 + P * u
-                        in_ = words[:, u : 2 * P : 2] if on_scalar(a, g) else words[:, P * u : P * (u + 1)]
-                        nc.tensor.transpose(xt[:, col : col + P], in_, ident[:])
-                c_turned[a, h] = xt
+        def turn_c(a, h, where):
+            xt = bank(where)
+            for g2 in range(2):
+                words = c_wide[a, 2 * h + g2][:].bitcast(F32)
+                for u in range(2):
+                    col = 2 * P * g2 + P * u
+                    nc.tensor.transpose(xt[:, col : col + P], words[:, u : 2 * P : 2], ident[:])
+            c_turned[a, h] = xt
 
         def untangle_c(a, h):
             out = c_grp[h][:, :, a * P : (a + 1) * P, :].rearrange("p g r t -> p g (r t)").bitcast(F32)
@@ -157,58 +157,62 @@ def tile_fock_orbital_blocks_d4_kernel(tc, c_bytes, c_scale, fock, occ, v_words,
 
         grps, f_codes, f_scales, mirror_banks = {}, {}, {}, {}
 
-        def turn_mirror(first_bank):
+        def new_grp(s):
+            if s in (5, 6, 8, 10, 12, 14):
+                grps[s] = grp_pool.tile([P, W, 4], BF16, name=f"grp_pair{s // G}", align_bytes=64, bufs=1)
+            else:
+                grps[s] = grp_pool.tile([P, W, 4], BF16, name="grp", align_bytes=64)
+
+        def turn_mirror(s, first_bank):
+            g, k = divmod(s, G)
             for h in range(2):
                 xt = bank(first_bank + h)
                 for j2 in range(2):
-                    words = raws[MIRROR_SOURCE][:, 2 * h + j2, :].bitcast(F32)
+                    words = raws[G * k + g][:, 2 * h + j2, :].bitcast(F32)
                     for u in range(2):
                         col = 2 * P * j2 + P * u
                         nc.tensor.transpose(xt[:, col : col + P], words[:, u : 2 * P : 2], ident[:])
-                mirror_banks[h] = xt
+                mirror_banks[s, h] = xt
 
-        def untangle_mirror():
-            grp = grp_pool.tile([P, W, 4], BF16, name="grp", align_bytes=64)
-            words = grp[:].rearrange("p n t -> p (n t)").bitcast(F32).rearrange("p (m h w) -> p h m w", h=2, w=4)
+        def untangle_mirror(s):
+            new_grp(s)
+            words = grps[s][:].rearrange("p n t -> p (n t)").bitcast(F32)
+            words = words.rearrange("p (h j m u) -> p h j m u", h=2, j=2, u=2)
             for h in range(2):
-                nc.scalar.copy(words[:, h], mirror_banks[h][:].rearrange("p (w m) -> p m w", w=4))
-            grps[MIRRORED] = grp
+                nc.scalar.copy(words[:, h], mirror_banks[s, h][:].rearrange("p (j u m) -> p j m u", j=2, u=2))
 
-        def scalar_share(s):
-            g, k = divmod(s, G)
-            if g == 0 or (g == LAST and k < 2):
-                return SHARE_USUAL
-            if g == 1 and k < 2:
-                return SHARE_AHEAD
-            return 0 if s == G + 2 else SHARE_BUSY
+        def pool_share(s):
+            return SHARE_POOL if s > G and s % G == 2 else 0
 
         def interleave(s, lo, hi, engine_copy):
+            if lo == hi:
+                return
             if s not in grps:
-                grps[s] = grp_pool.tile([P, W, 4], BF16, name="grp", align_bytes=64)
-            if s < G * LAST:
-                step = 2
-                src = raws[s][:].rearrange("p t (c i) -> p c t i", i=step)
-                dst = grps[s][:].rearrange("p (c i) t -> p c t i", i=step)
-            else:
-                step = 8
-                src = raws[s][:].rearrange("p t (c i j) -> p c j t i", i=2, j=4)
-                dst = grps[s][:].rearrange("p (j c i) t -> p c j t i", i=2, j=4)
-            engine_copy(dst[:, lo // step : hi // step], src[:, lo // step : hi // step])
+                new_grp(s)
+            src = raws[s][:].rearrange("p t (c i j) -> p c j t i", i=2, j=4)
+            dst = grps[s][:].rearrange("p (j c i) t -> p c j t i", i=2, j=4)
+            engine_copy(dst[:, lo // 8 : hi // 8], src[:, lo // 8 : hi // 8])
 
         def vector_copy(out, in_):
             nc.vector.tensor_copy(out=out, in_=in_)
 
         def scalar_part(s):
-            interleave(s, 0, scalar_share(s), nc.scalar.copy)
+            if s not in MIRRORED:
+                interleave(s, 0, SHARE[s], nc.scalar.copy)
 
         def vector_part(s):
-            interleave(s, scalar_share(s), W, vector_copy)
+            if s not in MIRRORED:
+                interleave(s, SHARE[s], W - pool_share(s), vector_copy)
 
-        def vector_lead(s):
-            interleave(s, scalar_share(s), scalar_share(s) + LEAD, vector_copy)
-
-        def vector_rest(s):
-            interleave(s, scalar_share(s) + LEAD, W, vector_copy)
+        def pool_part(s):
+            lo = W - pool_share(s)
+            if lo == W:
+                return
+            if s not in grps:
+                new_grp(s)
+            src = raws[s][:].rearrange("p t (m j) -> p j m t", j=4)
+            dst = grps[s][:].rearrange("p (j m) t -> p j m t", j=4)
+            nc.gpsimd.tensor_scalar(dst[:, :, lo // 4 :], src[:, :, lo // 4 :], 1.0, 0.0, MULT, ADD)
 
         def quantise_fock(s):
             codes = code_pool.tile([P, W], U32, name="f_codes", align_bytes=64)
@@ -218,52 +222,42 @@ def tile_fock_orbital_blocks_d4_kernel(tc, c_bytes, c_scale, fock, occ, v_words,
             )
             f_codes[s], f_scales[s] = codes, scales
 
-        s1_banks, h_wide, h_turned, h_grp = {}, {}, {}, {}
+        s1_banks, h_grp = {}, {}
 
         def group_bank(g, i):
             return bank(i if g == 0 else OT + i)
 
-        def stage1(s, slices):
+        def stage1(s):
             g, k = divmod(s, G)
-            still, moving = (c_codes[k], c_scales[k]), (f_codes[s], f_scales[s])
-            if g == LAST:
-                still, moving = moving, still
-            for i in slices:
+            for i in range(OT):
                 if k == 0:
                     s1_banks[g, i] = group_bank(g, i)
-                nc.tensor.matmul_mx(
-                    out=s1_banks[g, i][:],
-                    lhsT=still[0][:, i * P : (i + 1) * P].bitcast(FP8X4),
-                    lhsT_scale=still[1][:, i * P : (i + 1) * P],
-                    rhs=moving[0][:].bitcast(FP8X4),
-                    rhs_scale=moving[1][:],
-                    start=(k == 0),
-                    stop=(k == LAST),
-                )
+                if g == LAST:
+                    steps = [(i, slice(0, O), slice(0, W), k == 0, k == LAST)]
+                else:
+                    steps = [
+                        (j, slice(i * P, (i + 1) * P), slice(j * P, (j + 1) * P), k == 0 and j == 0, k == LAST and j == 3)
+                        for j in range(4)
+                    ]
+                for j, orbitals, cols, start, stop in steps:
+                    nc.tensor.matmul_mx(
+                        out=s1_banks[g, i][:, cols],
+                        lhsT=f_codes[s][:, j * P : (j + 1) * P].bitcast(FP8X4),
+                        lhsT_scale=f_scales[s][:, j * P : (j + 1) * P],
+                        rhs=c_codes[k][:, orbitals].bitcast(FP8X4),
+                        rhs_scale=c_scales[k][:, orbitals],
+                        start=start,
+                        stop=stop,
+                    )
 
         def weigh(g, a):
-            wide = wide_pool.tile([P, W], BF16, name="h_wide")
-            out = wide[:].rearrange("p (u m e) -> p u m e", u=2, e=2)
-            in_ = s1_banks[g, a][:].rearrange("p (m u e) -> p u m e", u=2, e=2)
-            nc.scalar.activation(out, in_, COPY, scale=occ_f32[:, a : a + 1])
-            h_wide[g, a] = wide
-
-        def turn_half(g):
-            for h in range(2):
-                xt = group_bank(g, 2 * h)
-                for a2 in range(2):
-                    words = h_wide[g, 2 * h + a2][:].bitcast(F32)
-                    for u in range(2):
-                        col = 2 * P * a2 + P * u
-                        nc.tensor.transpose(xt[:, col : col + P], words[:, P * u : P * (u + 1)], ident[:])
-                h_turned[g, h] = xt
-
-        def untangle_half(g):
-            for h in range(2):
-                grp = turn_pool.tile([P, HALF, 4], BF16, name="h_grp", align_bytes=64)
-                out = grp[:].rearrange("p r t -> p (r t)").bitcast(F32).rearrange("p (a r u) -> p a r u", a=2, u=2)
-                nc.scalar.copy(out, h_turned[g, h][:].rearrange("p (a u r) -> p a r u", a=2, u=2))
-                h_grp[g, h] = grp
+            h, a2 = divmod(a, 2)
+            if a2 == 0:
+                h_grp[g, h] = turn_pool.tile([P, HALF, 4], BF16, name="h_grp", align_bytes=64)
+            out = h_grp[g, h][:, a2 * P : (a2 + 1) * P, :].rearrange("p (c i) t -> p c t i", i=2)
+            sums = s1_banks[g, a][:].rearrange("p (t c i) -> p c t i", t=4, i=2)
+            weights = occ_row[:, a * P : (a + 1) * P].rearrange("p (c o i) -> p c o i", o=1, i=2)
+            nc.vector.tensor_tensor(out, sums, weights.to_broadcast([P, P // 2, 4, 2]), MULT)
 
         def weigh_slot(t):
             nc.vector.tensor_tensor(h_slots[:, t, :], s1_banks[LAST, t][:], occ_row[:], MULT)
@@ -302,8 +296,8 @@ def tile_fock_orbital_blocks_d4_kernel(tc, c_bytes, c_scale, fock, occ, v_words,
                     stop=(g == LAST),
                 )
 
-        def f_oo_pass(g):
-            for a in range(OT):
+        def f_oo_pass(g, tiles):
+            for a in tiles:
                 if g == 0:
                     accs[a, 0] = bank(a)
                 stage2(a, 0, [g])
@@ -344,17 +338,32 @@ def tile_fock_orbital_blocks_d4_kernel(tc, c_bytes, c_scale, fock, occ, v_words,
             queue = nc.scalar if first + width == W else nc.sync
             queue.dma_start(out=ov_rows[a][:, V - W + first : V - W + first + width], in_=res[:, :width])
 
-        odd, even = (1, 3), (0, 2)
-
         for a in range(OT):
-            widen(a)
-            turn_c(a)
-            if a in (1, 2):
-                for h in range(2):
-                    untangle_c(a - 1, h)
-        idle = bank(1)
-        nc.tensor.matmul(idle[:, :P], lhsT=ident[:], rhs=ident[:], start=True, stop=True)
-        spread = psum.tile([P, 2 * W], BF16, name="spread", tag="bank0")
+            widen(a, 0)
+            widen(a, 1)
+            turn_c(a, 0, a)
+        for a in range(OT):
+            widen(a, 2)
+            widen(a, 3)
+            turn_c(a, 1, OT + a)
+        for h in range(2):
+            for a in range(OT):
+                untangle_c(a, h)
+        turn_mirror(1, OT)
+        untangle_mirror(1)
+        turn_mirror(2, OT + 2)
+        untangle_mirror(2)
+        vector_part(0)
+        quantise_c(0)
+        quantise_fock(0)
+        stage1(0)
+        quantise_c(1)
+        quantise_c(2)
+        scalar_part(3)
+        vector_part(3)
+        quantise_fock(1)
+        stage1(1)
+        spread = psum.tile([P, 2 * W], BF16, name="spread", tag="bank4")
         for a in range(OT):
             nc.tensor.matmul(
                 spread[:, a * P : (a + 1) * P],
@@ -363,98 +372,57 @@ def tile_fock_orbital_blocks_d4_kernel(tc, c_bytes, c_scale, fock, occ, v_words,
                 start=True,
                 stop=True,
             )
-        scalar_part(0)
-        for h in range(2):
-            untangle_c(2, h)
-            untangle_c(3, h)
-        turn_mirror(OT)
-        nc.scalar.copy(occ_row[:], spread[:, :O])
-        vector_part(0)
-        vector_part(1)
-        quantise_fock(0)
-        quantise_c(0)
-        stage1(0, even + odd)
-        scalar_part(1)
-        untangle_mirror()
-        quantise_c(1)
-        quantise_c(2)
-        quantise_fock(1)
-        stage1(1, even + odd)
-        scalar_part(3)
-        vector_part(3)
-        quantise_fock(2)
-        stage1(2, even + odd)
         quantise_c(3)
+        quantise_fock(2)
+        stage1(2)
+        scalar_part(4)
+        vector_part(4)
         quantise_fock(3)
-        stage1(3, range(OT))
+        scalar_part(5)
+        vector_part(5)
+        nc.scalar.copy(occ_row[:], spread[:, :O])
+        quantise_fock(4)
+        quantise_fock(5)
 
-        s = G
-        scalar_part(s)
-        scalar_part(s + 1)
-        vector_part(s)
-        nc.vector.tensor_copy(out=occ_f32[:], in_=occ_sb[:])
-        vector_lead(s + 1)
-        quantise_fock(s)
-        stage1(s, range(OT))
-        for a in range(OT):
-            weigh(0, a)
-        vector_rest(s + 1)
-        vector_lead(s + 2)
-        quantise_fock(s + 1)
-        stage1(s + 1, odd + even)
-        turn_half(0)
-        scalar_part(s + 3)
-        vector_rest(s + 2)
-        vector_lead(s + 3)
-        untangle_half(0)
-        quantise_fock(s + 2)
-        stage1(s + 2, odd + even)
-        vector_rest(s + 3)
-        scalar_part(s + 4)
-        scalar_part(s + 5)
-        vector_lead(s + 4)
-        quantise_fock(s + 3)
-        quantise_half(0, 0)
-
-        for g in range(1, LAST):
+        for g in range(LAST):
             s = G * (g + 1)
-            stage1(s - 1, odd + even)
-            quantise_half(g - 1, 1)
-            f_oo_pass(g - 1)
-            for a in odd + even:
+            stage1(s - 1)
+            if g > 0:
+                f_oo_pass(g - 1, range(OT))
+            pool_part(s + 2)
+            if g > 0:
+                scalar_part(s + 1)
+            for a in range(OT):
                 weigh(g, a)
-            if g == 1:
-                vector_rest(s)
-            else:
-                vector_part(s)
-            vector_lead(s + 1)
-            quantise_fock(s)
-            vector_rest(s + 1)
-            vector_lead(s + 2)
-            quantise_fock(s + 1)
-            stage1(s, odd)
-            turn_half(g)
+            stage1(s)
+            if g == 0:
+                interleave(s + 3, 0, AHEAD, nc.scalar.copy)
             scalar_part(s + 2)
-            vector_rest(s + 2)
-            untangle_half(g)
-            stage1(s + 1, odd)
-            for a in even:
-                stage1(s, [a])
-                stage1(s + 1, [a])
-            scalar_part(s + 3)
-            vector_lead(s + 3)
+            vector_part(s + 2)
+            if g > 0:
+                quantise_fock(s + 1)
+            stage1(s + 1)
+            interleave(s + 3, AHEAD if g == 0 else 0, SHARE[s + 3], nc.scalar.copy)
+            if g > 0:
+                quantise_half(g, 0)
             quantise_fock(s + 2)
-            vector_rest(s + 3)
-            quantise_half(g, 0)
-            stage1(s + 2, odd + even)
+            if g == 0:
+                quantise_half(g, 0)
+            stage1(s + 2)
+            vector_part(s + 3)
             if g + 1 < LAST:
                 scalar_part(s + 4)
-                scalar_part(s + 5)
-            quantise_fock(s + 3)
+                vector_part(s + 4)
+                quantise_fock(s + 3)
+                quantise_half(g, 1)
+                quantise_fock(s + 4)
+            else:
+                quantise_half(g, 1)
+                quantise_fock(s + 3)
 
-        quantise_half(LAST - 1, 1)
-        stage1(PIECES - 1, range(4))
-        f_oo_pass(LAST - 1)
+        f_oo_pass(LAST - 1, range(2))
+        stage1(PIECES - 1)
+        f_oo_pass(LAST - 1, range(2, OT))
         for t in range(4):
             weigh_slot(t)
         interleave_last_half(1, 0, TAIL_SHARE, nc.scalar.copy)

@@ -30,8 +30,10 @@ DMA_ALIGN = 256
 
 MIRRORED = (1, 2)
 
-SHARE = (0, 0, 0, 192, 192, 320, 224, 448, 320, 512, 224, 320, 256, 512, 224, 320)
-SHARE_POOL = 288
+SHARE_POOL = 224
+SHARE_HEAD = 192
+SHARE_FIRST = 256
+SHARE_LAST = 320
 S_WIDE = ((0, 1), (1, 1), (2, 1), (0, 3))
 TAIL_SHARE = 192
 
@@ -181,6 +183,13 @@ def tile_fock_orbital_blocks_d4_kernel(tc, c_bytes, c_scale, fock, occ, v_words,
             for h in range(2):
                 nc.scalar.copy(words[:, h], mirror_banks[s, h][:].rearrange("p (j u m) -> p j m u", j=2, u=2))
 
+        def scalar_share(s):
+            if s <= G:
+                return SHARE_HEAD if s > 0 else 0
+            if s == G + 1:
+                return SHARE_LAST
+            return (SHARE_FIRST, W, W - SHARE_POOL, SHARE_LAST)[s % G]
+
         def pool_share(s):
             return SHARE_POOL if s > G and s % G == 2 else 0
 
@@ -198,11 +207,11 @@ def tile_fock_orbital_blocks_d4_kernel(tc, c_bytes, c_scale, fock, occ, v_words,
 
         def scalar_part(s):
             if s not in MIRRORED:
-                interleave(s, 0, SHARE[s], nc.scalar.copy)
+                interleave(s, 0, scalar_share(s), nc.scalar.copy)
 
         def vector_part(s):
             if s not in MIRRORED:
-                interleave(s, SHARE[s], W - pool_share(s), vector_copy)
+                interleave(s, scalar_share(s), W - pool_share(s), vector_copy)
 
         def pool_part(s):
             lo = W - pool_share(s)
@@ -210,9 +219,9 @@ def tile_fock_orbital_blocks_d4_kernel(tc, c_bytes, c_scale, fock, occ, v_words,
                 return
             if s not in grps:
                 new_grp(s)
-            src = raws[s][:].rearrange("p t (m j) -> p j m t", j=4)
-            dst = grps[s][:].rearrange("p (j m) t -> p j m t", j=4)
-            nc.gpsimd.tensor_scalar(dst[:, :, lo // 4 :], src[:, :, lo // 4 :], 1.0, 0.0, MULT, ADD)
+            src = raws[s][:].rearrange("p t (m j) -> p m j t", j=4)
+            dst = grps[s][:].rearrange("p (j m) t -> p m j t", j=4)
+            nc.gpsimd.tensor_scalar(dst[:, lo // 4 :], src[:, lo // 4 :], 1.0, 0.0, MULT, ADD)
 
         def quantise_fock(s):
             codes = code_pool.tile([P, W], U32, name="f_codes", align_bytes=64)
@@ -402,7 +411,7 @@ def tile_fock_orbital_blocks_d4_kernel(tc, c_bytes, c_scale, fock, occ, v_words,
             if g > 0:
                 quantise_fock(s + 1)
             stage1(s + 1)
-            interleave(s + 3, AHEAD if g == 0 else 0, SHARE[s + 3], nc.scalar.copy)
+            interleave(s + 3, AHEAD if g == 0 else 0, scalar_share(s + 3), nc.scalar.copy)
             if g > 0:
                 quantise_half(g, 0)
             quantise_fock(s + 2)

@@ -39,6 +39,9 @@ TAIL_SHARE = 192
 
 AHEAD = 192
 
+WARM_C = {(0, 0): (256, 256, 256), (3, 0): (256,), (2, 1): (256,)}
+WARM_M = {(2, 0): (256,)}
+
 FLOPS = 2 * O * N * N + 2 * O * N * (O + V)
 
 
@@ -62,7 +65,8 @@ def tile_fock_orbital_blocks_d4_kernel(tc, c_bytes, c_scale, fock, occ, v_words,
         occ_row = keep.tile([P, O], BF16, name="occ_row")
         scale_sb = keep.tile([P, OT * N // B], F32, name="scale_sb")
         occ_sb = keep.tile([P, OT], BF16, name="occ_sb")
-        warm = keep.tile([P, 2], F32, name="warm")
+        warm = keep.tile([P, P], F32, name="warm")
+        warm_out = keep.tile([P, 1], F32, name="warm_out")
         c_raw = {
             (a, h): keep.tile([P, N // 2], U8, name=f"c_raw{a}{h}", align_bytes=DMA_ALIGN)
             for a in range(OT)
@@ -103,10 +107,10 @@ def tile_fock_orbital_blocks_d4_kernel(tc, c_bytes, c_scale, fock, occ, v_words,
         nc.sync.dma_start(out=occ_sb[:], in_=occ.rearrange("(p a) -> p a", a=OT))
         load_fock(2 * G)
         load_fock(3)
+        nc.vector.memset(warm[:], 0.0)
         make_identity(nc, ident[:])
         make_identity(nc, ident_bf[:])
-        nc.vector.memset(warm[:], 0.0)
-        nc.scalar.activation(warm[:, 0:1], warm[:, 1:2], COPY, scale=warm[:, 1:2])
+        nc.scalar.activation(warm_out[:], warm[:, 0:1], COPY, scale=warm[:, 1:2])
         nc.vector.memset(v_scale_sb[:].rearrange("p g n -> p (g n)").bitcast(U32), 0)
         for s in range(G, PIECES):
             if s not in (G, 2 * G):
@@ -131,16 +135,25 @@ def tile_fock_orbital_blocks_d4_kernel(tc, c_bytes, c_scale, fock, occ, v_words,
                 if (a, g) in S_WIDE:
                     nc.scalar.activation(wide[:, b * B : (b + 1) * B], src, COPY, scale=scale)
                 else:
-                    nc.vector.tensor_scalar(wide[:, b * B : (b + 1) * B], src, scale, None, MULT)
+                    dst = wide[:].rearrange("p (u m e) -> p m u e", u=2, e=2)[:, 32 * b : 32 * (b + 1)]
+                    src = src.rearrange("p (m u e) -> p m u e", u=2, e=2)
+                    nc.vector.tensor_scalar(dst, src, scale, None, MULT)
             c_wide[a, g] = wide
+
+        def warm_up(xt, width):
+            moving = warm[:].rearrange("p (o n) -> p o n", o=1).to_broadcast([P, width // P, P])
+            nc.tensor.matmul(xt[:, :width], lhsT=warm[:], rhs=moving, start=True, stop=True)
 
         def turn_c(a, h, where):
             xt = bank(where)
+            for width in WARM_C.get((a, h), ()):
+                warm_up(xt, width)
             for g2 in range(2):
                 words = c_wide[a, 2 * h + g2][:].bitcast(F32)
                 for u in range(2):
                     col = 2 * P * g2 + P * u
-                    nc.tensor.transpose(xt[:, col : col + P], words[:, u : 2 * P : 2], ident[:])
+                    in_ = words[:, u : 2 * P : 2] if (a, 2 * h + g2) in S_WIDE else words[:, P * u : P * (u + 1)]
+                    nc.tensor.transpose(xt[:, col : col + P], in_, ident[:])
             c_turned[a, h] = xt
 
         def untangle_c(a, h):
@@ -169,6 +182,8 @@ def tile_fock_orbital_blocks_d4_kernel(tc, c_bytes, c_scale, fock, occ, v_words,
             g, k = divmod(s, G)
             for h in range(2):
                 xt = bank(first_bank + h)
+                for width in WARM_M.get((s, h), ()):
+                    warm_up(xt, width)
                 for j2 in range(2):
                     words = raws[G * k + g][:, 2 * h + j2, :].bitcast(F32)
                     for u in range(2):

@@ -30,17 +30,19 @@ DMA_ALIGN = 256
 
 MIRRORED = (1, 2)
 
-SHARE_POOL = 224
-SHARE_HEAD = 192
-SHARE_FIRST = 256
-SHARE_LAST = 320
+SHARE_POOL = 256
+SHARE_USUAL = 320
+SHARE_HEAD = 160
+SHARE_SEVEN = 448
+HALF_SHARE = {2: 160, 3: 192}
 S_WIDE = ((0, 1), (1, 1), (2, 1), (0, 3))
-TAIL_SHARE = 192
 
-AHEAD = 192
+WARM_WIDTH = 256
+WARM_C = {(0, 0): 3, (2, 0): 1, (1, 1): 1}
+WARM_M = {(1, 1): 1}
 
-WARM_C = {(0, 0): (256, 256, 256), (3, 0): (256,), (2, 1): (256,)}
-WARM_M = {(2, 0): (256,)}
+WIDE = (2, 3)
+RUNS = (((0, 1), (2, 3)), ((0, 1, 2, 3),), ((0, 1, 2, 3),), ((0,), (1,), (2, 3)))
 
 FLOPS = 2 * O * N * N + 2 * O * N * (O + V)
 
@@ -50,7 +52,7 @@ def tile_fock_orbital_blocks_d4_kernel(tc, c_bytes, c_scale, fock, occ, v_words,
     with ExitStack() as ctx:
         keep = ctx.enter_context(tc.tile_pool(name="keep", bufs=1))
         raw_pool = ctx.enter_context(tc.tile_pool(name="raw", bufs=PIECES))
-        grp_pool = ctx.enter_context(tc.tile_pool(name="grp", bufs=4))
+        grp_pool = ctx.enter_context(tc.tile_pool(name="grp", bufs=5))
         code_pool = ctx.enter_context(tc.tile_pool(name="code", bufs=6))
         wide_pool = ctx.enter_context(tc.tile_pool(name="wide", bufs=OT * G))
         turn_pool = ctx.enter_context(tc.tile_pool(name="turn", bufs=2))
@@ -77,7 +79,6 @@ def tile_fock_orbital_blocks_d4_kernel(tc, c_bytes, c_scale, fock, occ, v_words,
         c_scales = [keep.tile([P, O], U8, name=f"c_scales{g}", align_bytes=64) for g in range(G)]
         h_codes = [keep.tile([P, O], U32, name=f"h_codes{g}", align_bytes=64) for g in range(G)]
         h_scales = [keep.tile([P, O], U8, name=f"h_scales{g}", align_bytes=64) for g in range(G)]
-        h_slots = keep.tile([P, 4, O], BF16, name="h_slots")
         v_sb = [keep.tile([P, G, 2 * W], U8, name=f"v_sb{n}", align_bytes=DMA_ALIGN) for n in range(V // W)]
         v_scale_sb = keep.tile([P, G, V], U8, name="v_scale_sb", align_bytes=64)
 
@@ -140,14 +141,14 @@ def tile_fock_orbital_blocks_d4_kernel(tc, c_bytes, c_scale, fock, occ, v_words,
                     nc.vector.tensor_scalar(dst, src, scale, None, MULT)
             c_wide[a, g] = wide
 
-        def warm_up(xt, width):
-            moving = warm[:].rearrange("p (o n) -> p o n", o=1).to_broadcast([P, width // P, P])
-            nc.tensor.matmul(xt[:, :width], lhsT=warm[:], rhs=moving, start=True, stop=True)
+        def warm_up(xt, count):
+            moving = warm[:].rearrange("p (o n) -> p o n", o=1).to_broadcast([P, WARM_WIDTH // P, P])
+            for i in range(count):
+                nc.tensor.matmul(xt[:, :WARM_WIDTH], lhsT=warm[:], rhs=moving, start=True, stop=True)
 
         def turn_c(a, h, where):
             xt = bank(where)
-            for width in WARM_C.get((a, h), ()):
-                warm_up(xt, width)
+            warm_up(xt, WARM_C.get((a, h), 0))
             for g2 in range(2):
                 words = c_wide[a, 2 * h + g2][:].bitcast(F32)
                 for u in range(2):
@@ -182,8 +183,7 @@ def tile_fock_orbital_blocks_d4_kernel(tc, c_bytes, c_scale, fock, occ, v_words,
             g, k = divmod(s, G)
             for h in range(2):
                 xt = bank(first_bank + h)
-                for width in WARM_M.get((s, h), ()):
-                    warm_up(xt, width)
+                warm_up(xt, WARM_M.get((s, h), 0))
                 for j2 in range(2):
                     words = raws[G * k + g][:, 2 * h + j2, :].bitcast(F32)
                     for u in range(2):
@@ -199,11 +199,15 @@ def tile_fock_orbital_blocks_d4_kernel(tc, c_bytes, c_scale, fock, occ, v_words,
                 nc.scalar.copy(words[:, h], mirror_banks[s, h][:].rearrange("p (j u m) -> p j m u", j=2, u=2))
 
         def scalar_share(s):
+            if s == 0:
+                return 0
             if s <= G:
-                return SHARE_HEAD if s > 0 else 0
-            if s == G + 1:
-                return SHARE_LAST
-            return (SHARE_FIRST, W, W - SHARE_POOL, SHARE_LAST)[s % G]
+                return SHARE_HEAD
+            if s == 2 * G - 1:
+                return SHARE_SEVEN
+            if s % G == 2:
+                return W - SHARE_POOL
+            return W if s > 2 * G and s % G == 1 else SHARE_USUAL
 
         def pool_share(s):
             return SHARE_POOL if s > G and s % G == 2 else 0
@@ -253,26 +257,29 @@ def tile_fock_orbital_blocks_d4_kernel(tc, c_bytes, c_scale, fock, occ, v_words,
 
         def stage1(s):
             g, k = divmod(s, G)
-            for i in range(OT):
-                if k == 0:
+            if k == 0:
+                for i in range(OT):
                     s1_banks[g, i] = group_bank(g, i)
-                if g == LAST:
-                    steps = [(i, slice(0, O), slice(0, W), k == 0, k == LAST)]
-                else:
-                    steps = [
-                        (j, slice(i * P, (i + 1) * P), slice(j * P, (j + 1) * P), k == 0 and j == 0, k == LAST and j == 3)
-                        for j in range(4)
-                    ]
-                for j, orbitals, cols, start, stop in steps:
-                    nc.tensor.matmul_mx(
-                        out=s1_banks[g, i][:, cols],
-                        lhsT=f_codes[s][:, j * P : (j + 1) * P].bitcast(FP8X4),
-                        lhsT_scale=f_scales[s][:, j * P : (j + 1) * P],
-                        rhs=c_codes[k][:, orbitals].bitcast(FP8X4),
-                        rhs_scale=c_scales[k][:, orbitals],
-                        start=start,
-                        stop=stop,
-                    )
+            if g in WIDE:
+                steps = [(j, j, slice(0, O), slice(0, W), k == 0, k == LAST) for j in range(4)]
+            else:
+                runs = RUNS[k]
+                steps = [
+                    (a, j, slice(a * P, (a + 1) * P), slice(j * P, (j + 1) * P), k == 0 and j == 0, k == LAST and j == 3)
+                    for tiles in runs
+                    for j in range(4)
+                    for a in tiles
+                ]
+            for i, j, orbitals, cols, start, stop in steps:
+                nc.tensor.matmul_mx(
+                    out=s1_banks[g, i][:, cols],
+                    lhsT=f_codes[s][:, j * P : (j + 1) * P].bitcast(FP8X4),
+                    lhsT_scale=f_scales[s][:, j * P : (j + 1) * P],
+                    rhs=c_codes[k][:, orbitals].bitcast(FP8X4),
+                    rhs_scale=c_scales[k][:, orbitals],
+                    start=start,
+                    stop=stop,
+                )
 
         def weigh(g, a):
             h, a2 = divmod(a, 2)
@@ -283,14 +290,20 @@ def tile_fock_orbital_blocks_d4_kernel(tc, c_bytes, c_scale, fock, occ, v_words,
             weights = occ_row[:, a * P : (a + 1) * P].rearrange("p (c o i) -> p c o i", o=1, i=2)
             nc.vector.tensor_tensor(out, sums, weights.to_broadcast([P, P // 2, 4, 2]), MULT)
 
-        def weigh_slot(t):
-            nc.vector.tensor_tensor(h_slots[:, t, :], s1_banks[LAST, t][:], occ_row[:], MULT)
+        h_slots = {}
 
-        def interleave_last_half(h, lo, hi, engine_copy):
-            if (LAST, h) not in h_grp:
-                h_grp[LAST, h] = turn_pool.tile([P, HALF, 4], BF16, name="h_grp", align_bytes=64)
-            src = h_slots[:, :, HALF * h : HALF * (h + 1)].rearrange("p t (c i) -> p c t i", i=2)
-            dst = h_grp[LAST, h][:].rearrange("p (c i) t -> p c t i", i=2)
+        def weigh_slot(g, t):
+            if t == 0:
+                h_slots[g] = turn_pool.tile([P, 4, O], BF16, name="h_slots")
+            nc.vector.tensor_tensor(h_slots[g][:, t, :], s1_banks[g, t][:], occ_row[:], MULT)
+
+        def interleave_half(g, h, lo, hi, engine_copy):
+            if lo == hi:
+                return
+            if (g, h) not in h_grp:
+                h_grp[g, h] = turn_pool.tile([P, HALF, 4], BF16, name="h_grp", align_bytes=64)
+            src = h_slots[g][:, :, HALF * h : HALF * (h + 1)].rearrange("p t (c i) -> p c t i", i=2)
+            dst = h_grp[g, h][:].rearrange("p (c i) t -> p c t i", i=2)
             engine_copy(dst[:, lo // 2 : hi // 2], src[:, lo // 2 : hi // 2])
 
         def quantise_half(g, h):
@@ -417,41 +430,49 @@ def tile_fock_orbital_blocks_d4_kernel(tc, c_bytes, c_scale, fock, occ, v_words,
             if g > 0:
                 scalar_part(s + 1)
             for a in range(OT):
-                weigh(g, a)
+                if g in WIDE:
+                    weigh_slot(g, a)
+                else:
+                    weigh(g, a)
             stage1(s)
             if g == 0:
-                interleave(s + 3, 0, AHEAD, nc.scalar.copy)
+                interleave(s + 3, 0, SHARE_USUAL, nc.scalar.copy)
             scalar_part(s + 2)
             vector_part(s + 2)
             if g > 0:
                 quantise_fock(s + 1)
             stage1(s + 1)
-            interleave(s + 3, AHEAD if g == 0 else 0, scalar_share(s + 3), nc.scalar.copy)
-            if g > 0:
+            interleave(s + 3, SHARE_USUAL if g == 0 else 0, scalar_share(s + 3), nc.scalar.copy)
+            if g == 1:
                 quantise_half(g, 0)
+            if g == 2:
+                vector_part(s + 3)
             quantise_fock(s + 2)
             if g == 0:
                 quantise_half(g, 0)
             stage1(s + 2)
-            vector_part(s + 3)
             if g + 1 < LAST:
+                vector_part(s + 3)
                 scalar_part(s + 4)
                 vector_part(s + 4)
                 quantise_fock(s + 3)
                 quantise_half(g, 1)
                 quantise_fock(s + 4)
-            else:
-                quantise_half(g, 1)
-                quantise_fock(s + 3)
 
-        f_oo_pass(LAST - 1, range(2))
+        g = LAST - 1
+        interleave_half(g, 1, 0, HALF_SHARE[g], nc.scalar.copy)
+        interleave_half(g, 0, 0, HALF, vector_copy)
+        quantise_fock(PIECES - 1)
         stage1(PIECES - 1)
-        f_oo_pass(LAST - 1, range(2, OT))
+        quantise_half(g, 0)
+        interleave_half(g, 1, HALF_SHARE[g], HALF, vector_copy)
+        quantise_half(g, 1)
+        f_oo_pass(g, range(OT))
         for t in range(4):
-            weigh_slot(t)
-        interleave_last_half(1, 0, TAIL_SHARE, nc.scalar.copy)
-        interleave_last_half(0, 0, HALF, vector_copy)
-        interleave_last_half(1, TAIL_SHARE, HALF, vector_copy)
+            weigh_slot(LAST, t)
+        interleave_half(LAST, 1, 0, HALF_SHARE[LAST], nc.scalar.copy)
+        interleave_half(LAST, 0, 0, HALF, vector_copy)
+        interleave_half(LAST, 1, HALF_SHARE[LAST], HALF, vector_copy)
         quantise_half(LAST, 0)
         quantise_half(LAST, 1)
         for a in range(OT):

@@ -37,10 +37,6 @@ SHARE_SEVEN = 448
 HALF_SHARE = {2: 160, 3: 192}
 S_WIDE = ((0, 1), (1, 1), (2, 1), (0, 3))
 
-WARM_WIDTH = 256
-WARM_C = {(0, 0): 3, (2, 0): 1, (1, 1): 1}
-WARM_M = {(1, 1): 1}
-
 WIDE = (2, 3)
 RUNS = (((0, 1), (2, 3)), ((0, 1, 2, 3),), ((0, 1, 2, 3),), ((0,), (1,), (2, 3)))
 
@@ -141,14 +137,8 @@ def tile_fock_orbital_blocks_d4_kernel(tc, c_bytes, c_scale, fock, occ, v_words,
                     nc.vector.tensor_scalar(dst, src, scale, None, MULT)
             c_wide[a, g] = wide
 
-        def warm_up(xt, count):
-            moving = warm[:].rearrange("p (o n) -> p o n", o=1).to_broadcast([P, WARM_WIDTH // P, P])
-            for i in range(count):
-                nc.tensor.matmul(xt[:, :WARM_WIDTH], lhsT=warm[:], rhs=moving, start=True, stop=True)
-
         def turn_c(a, h, where):
             xt = bank(where)
-            warm_up(xt, WARM_C.get((a, h), 0))
             for g2 in range(2):
                 words = c_wide[a, 2 * h + g2][:].bitcast(F32)
                 for u in range(2):
@@ -183,7 +173,6 @@ def tile_fock_orbital_blocks_d4_kernel(tc, c_bytes, c_scale, fock, occ, v_words,
             g, k = divmod(s, G)
             for h in range(2):
                 xt = bank(first_bank + h)
-                warm_up(xt, WARM_M.get((s, h), 0))
                 for j2 in range(2):
                     words = raws[G * k + g][:, 2 * h + j2, :].bitcast(F32)
                     for u in range(2):

@@ -28,8 +28,6 @@ HALF = O // 2
 
 DMA_ALIGN = 256
 
-MIRRORED = (1, 2)
-
 SHARE_POOL = 256
 SHARE_USUAL = 320
 SHARE_HEAD = 160
@@ -51,7 +49,7 @@ def tile_fock_orbital_blocks_d4_kernel(tc, c_bytes, c_scale, fock, occ, v_words,
         grp_pool = ctx.enter_context(tc.tile_pool(name="grp", bufs=5))
         code_pool = ctx.enter_context(tc.tile_pool(name="code", bufs=6))
         wide_pool = ctx.enter_context(tc.tile_pool(name="wide", bufs=OT * G))
-        turn_pool = ctx.enter_context(tc.tile_pool(name="turn", bufs=2))
+        half_pool = ctx.enter_context(tc.tile_pool(name="half", bufs=2))
         out_pool = ctx.enter_context(tc.tile_pool(name="outs", bufs=BANKS))
         psum = ctx.enter_context(tc.psum_pool(name="psum", bufs=1))
 
@@ -63,8 +61,7 @@ def tile_fock_orbital_blocks_d4_kernel(tc, c_bytes, c_scale, fock, occ, v_words,
         occ_row = keep.tile([P, O], BF16, name="occ_row")
         scale_sb = keep.tile([P, OT * N // B], F32, name="scale_sb")
         occ_sb = keep.tile([P, OT], BF16, name="occ_sb")
-        warm = keep.tile([P, P], F32, name="warm")
-        warm_out = keep.tile([P, 1], F32, name="warm_out")
+        warm = keep.tile([P, 2], F32, name="warm")
         c_raw = {
             (a, h): keep.tile([P, N // 2], U8, name=f"c_raw{a}{h}", align_bytes=DMA_ALIGN)
             for a in range(OT)
@@ -107,10 +104,10 @@ def tile_fock_orbital_blocks_d4_kernel(tc, c_bytes, c_scale, fock, occ, v_words,
         nc.vector.memset(warm[:], 0.0)
         make_identity(nc, ident[:])
         make_identity(nc, ident_bf[:])
-        nc.scalar.activation(warm_out[:], warm[:, 0:1], COPY, scale=warm[:, 1:2])
+        nc.scalar.activation(warm[:, 0:1], warm[:, 1:2], COPY, scale=warm[:, 1:2])
         nc.vector.memset(v_scale_sb[:].rearrange("p g n -> p (g n)").bitcast(U32), 0)
-        for s in range(G, PIECES):
-            if s not in (G, 2 * G):
+        for s in range(G + 1, PIECES):
+            if s != 2 * G:
                 load_fock(s)
         for q in range(4):
             nc.sync.dma_start(
@@ -214,19 +211,14 @@ def tile_fock_orbital_blocks_d4_kernel(tc, c_bytes, c_scale, fock, occ, v_words,
             nc.vector.tensor_copy(out=out, in_=in_)
 
         def scalar_part(s):
-            if s not in MIRRORED:
-                interleave(s, 0, scalar_share(s), nc.scalar.copy)
+            interleave(s, 0, scalar_share(s), nc.scalar.copy)
 
         def vector_part(s):
-            if s not in MIRRORED:
-                interleave(s, scalar_share(s), W - pool_share(s), vector_copy)
+            interleave(s, scalar_share(s), W - pool_share(s), vector_copy)
 
         def pool_part(s):
             lo = W - pool_share(s)
-            if lo == W:
-                return
-            if s not in grps:
-                new_grp(s)
+            new_grp(s)
             src = raws[s][:].rearrange("p t (m j) -> p m j t", j=4)
             dst = grps[s][:].rearrange("p (j m) t -> p m j t", j=4)
             nc.gpsimd.tensor_scalar(dst[:, lo // 4 :], src[:, lo // 4 :], 1.0, 0.0, MULT, ADD)
@@ -244,6 +236,9 @@ def tile_fock_orbital_blocks_d4_kernel(tc, c_bytes, c_scale, fock, occ, v_words,
         def group_bank(g, i):
             return bank(i if g == 0 else OT + i)
 
+        def block(i):
+            return slice(i * P, (i + 1) * P)
+
         def stage1(s):
             g, k = divmod(s, G)
             if k == 0:
@@ -252,10 +247,9 @@ def tile_fock_orbital_blocks_d4_kernel(tc, c_bytes, c_scale, fock, occ, v_words,
             if g in WIDE:
                 steps = [(j, j, slice(0, O), slice(0, W), k == 0, k == LAST) for j in range(4)]
             else:
-                runs = RUNS[k]
                 steps = [
-                    (a, j, slice(a * P, (a + 1) * P), slice(j * P, (j + 1) * P), k == 0 and j == 0, k == LAST and j == 3)
-                    for tiles in runs
+                    (a, j, block(a), block(j), k == 0 and j == 0, k == LAST and j == 3)
+                    for tiles in RUNS[k]
                     for j in range(4)
                     for a in tiles
                 ]
@@ -273,7 +267,7 @@ def tile_fock_orbital_blocks_d4_kernel(tc, c_bytes, c_scale, fock, occ, v_words,
         def weigh(g, a):
             h, a2 = divmod(a, 2)
             if a2 == 0:
-                h_grp[g, h] = turn_pool.tile([P, HALF, 4], BF16, name="h_grp", align_bytes=64)
+                h_grp[g, h] = half_pool.tile([P, HALF, 4], BF16, name="h_grp", align_bytes=64)
             out = h_grp[g, h][:, a2 * P : (a2 + 1) * P, :].rearrange("p (c i) t -> p c t i", i=2)
             sums = s1_banks[g, a][:].rearrange("p (t c i) -> p c t i", t=4, i=2)
             weights = occ_row[:, a * P : (a + 1) * P].rearrange("p (c o i) -> p c o i", o=1, i=2)
@@ -283,14 +277,12 @@ def tile_fock_orbital_blocks_d4_kernel(tc, c_bytes, c_scale, fock, occ, v_words,
 
         def weigh_slot(g, t):
             if t == 0:
-                h_slots[g] = turn_pool.tile([P, 4, O], BF16, name="h_slots")
+                h_slots[g] = half_pool.tile([P, 4, O], BF16, name="h_slots")
             nc.vector.tensor_tensor(h_slots[g][:, t, :], s1_banks[g, t][:], occ_row[:], MULT)
 
         def interleave_half(g, h, lo, hi, engine_copy):
-            if lo == hi:
-                return
             if (g, h) not in h_grp:
-                h_grp[g, h] = turn_pool.tile([P, HALF, 4], BF16, name="h_grp", align_bytes=64)
+                h_grp[g, h] = half_pool.tile([P, HALF, 4], BF16, name="h_grp", align_bytes=64)
             src = h_slots[g][:, :, HALF * h : HALF * (h + 1)].rearrange("p t (c i) -> p c t i", i=2)
             dst = h_grp[g, h][:].rearrange("p (c i) t -> p c t i", i=2)
             engine_copy(dst[:, lo // 2 : hi // 2], src[:, lo // 2 : hi // 2])
@@ -322,8 +314,8 @@ def tile_fock_orbital_blocks_d4_kernel(tc, c_bytes, c_scale, fock, occ, v_words,
                     stop=(g == LAST),
                 )
 
-        def f_oo_pass(g, tiles):
-            for a in tiles:
+        def f_oo_pass(g):
+            for a in range(OT):
                 if g == 0:
                     accs[a, 0] = bank(a)
                 stage2(a, 0, [g])
@@ -410,53 +402,60 @@ def tile_fock_orbital_blocks_d4_kernel(tc, c_bytes, c_scale, fock, occ, v_words,
         quantise_fock(4)
         quantise_fock(5)
 
-        for g in range(LAST):
-            s = G * (g + 1)
-            stage1(s - 1)
-            if g > 0:
-                f_oo_pass(g - 1, range(OT))
-            pool_part(s + 2)
-            if g > 0:
-                scalar_part(s + 1)
-            for a in range(OT):
-                if g in WIDE:
-                    weigh_slot(g, a)
-                else:
-                    weigh(g, a)
-            stage1(s)
-            if g == 0:
-                interleave(s + 3, 0, SHARE_USUAL, nc.scalar.copy)
-            scalar_part(s + 2)
-            vector_part(s + 2)
-            if g > 0:
-                quantise_fock(s + 1)
-            stage1(s + 1)
-            interleave(s + 3, SHARE_USUAL if g == 0 else 0, scalar_share(s + 3), nc.scalar.copy)
-            if g == 1:
-                quantise_half(g, 0)
-            if g == 2:
-                vector_part(s + 3)
-            quantise_fock(s + 2)
-            if g == 0:
-                quantise_half(g, 0)
-            stage1(s + 2)
-            if g + 1 < LAST:
-                vector_part(s + 3)
-                scalar_part(s + 4)
-                vector_part(s + 4)
-                quantise_fock(s + 3)
-                quantise_half(g, 1)
-                quantise_fock(s + 4)
+        stage1(3)
+        pool_part(6)
+        for a in range(OT):
+            weigh(0, a)
+        stage1(4)
+        interleave(7, 0, SHARE_USUAL, nc.scalar.copy)
+        scalar_part(6)
+        stage1(5)
+        interleave(7, SHARE_USUAL, SHARE_SEVEN, nc.scalar.copy)
+        quantise_fock(6)
+        quantise_half(0, 0)
 
-        g = LAST - 1
-        interleave_half(g, 1, 0, HALF_SHARE[g], nc.scalar.copy)
-        interleave_half(g, 0, 0, HALF, vector_copy)
-        quantise_fock(PIECES - 1)
-        stage1(PIECES - 1)
-        quantise_half(g, 0)
-        interleave_half(g, 1, HALF_SHARE[g], HALF, vector_copy)
-        quantise_half(g, 1)
-        f_oo_pass(g, range(OT))
+        def finish_group(g):
+            s = G * g
+            stage1(s + 2)
+            vector_part(s + 3)
+            scalar_part(s + 4)
+            vector_part(s + 4)
+            quantise_fock(s + 3)
+            quantise_half(g - 1, 1)
+            quantise_fock(s + 4)
+
+        def open_group(g, weigh_bank):
+            s = G * g
+            stage1(s - 1)
+            f_oo_pass(g - 2)
+            pool_part(s + 2)
+            scalar_part(s + 1)
+            for i in range(4):
+                weigh_bank(g - 1, i)
+            stage1(s)
+            scalar_part(s + 2)
+            quantise_fock(s + 1)
+            stage1(s + 1)
+            scalar_part(s + 3)
+
+        finish_group(1)
+        open_group(2, weigh)
+        quantise_half(1, 0)
+        quantise_fock(10)
+        finish_group(2)
+        open_group(3, weigh_slot)
+        vector_part(15)
+        quantise_fock(14)
+        stage1(14)
+
+        interleave_half(2, 1, 0, HALF_SHARE[2], nc.scalar.copy)
+        interleave_half(2, 0, 0, HALF, vector_copy)
+        quantise_fock(15)
+        stage1(15)
+        quantise_half(2, 0)
+        interleave_half(2, 1, HALF_SHARE[2], HALF, vector_copy)
+        quantise_half(2, 1)
+        f_oo_pass(2)
         for t in range(4):
             weigh_slot(LAST, t)
         interleave_half(LAST, 1, 0, HALF_SHARE[LAST], nc.scalar.copy)

from contextlib import ExitStack

import concourse.mybir as mybir
from concourse.masks import make_identity

F32 = mybir.dt.float32
BF16 = mybir.dt.bfloat16
I32 = mybir.dt.int32
U32 = mybir.dt.uint32
U8 = mybir.dt.uint8
FP8 = mybir.dt.float8_e4m3fn
FP8X4 = mybir.dt.float8_e4m3fn_x4
FP4X4 = mybir.dt.float4_e2m1fn_x4
COPY = mybir.ActivationFunctionType.Copy
MULT = mybir.AluOpType.mult
ADD = mybir.AluOpType.add

P = 128
N, O, V = 2048, 512, 1536
W = 512
G = N // W
LAST = G - 1
OT = O // P
B = 128
PIECES = G * G
BANKS = 8
HALF = O // 2

DMA_ALIGN = 256

SHARE_POOL = 256
SHARE_USUAL = 320
SHARE_HEAD = 160
SHARE_SEVEN = 448
HALF_SHARE = {2: 160, 3: 192}
S_WIDE = ((0, 1), (1, 1), (2, 1), (0, 3))

WIDE = (2, 3)
RUNS = (((0, 1), (2, 3)), ((0, 1, 2, 3),), ((0, 1, 2, 3),), ((0,), (1,), (2, 3)))

FLOPS = 2 * O * N * N + 2 * O * N * (O + V)


def tile_fock_orbital_blocks_d4_kernel(tc, c_bytes, c_scale, fock, occ, v_words, v_scales, f_oo, f_ov):
    nc = tc.nc
    with ExitStack() as ctx:
        keep = ctx.enter_context(tc.tile_pool(name="keep", bufs=1))
        raw_pool = ctx.enter_context(tc.tile_pool(name="raw", bufs=PIECES))
        grp_pool = ctx.enter_context(tc.tile_pool(name="grp", bufs=5))
        code_pool = ctx.enter_context(tc.tile_pool(name="code", bufs=6))
        wide_pool = ctx.enter_context(tc.tile_pool(name="wide", bufs=OT * G))
        half_pool = ctx.enter_context(tc.tile_pool(name="half", bufs=2))
        out_pool = ctx.enter_context(tc.tile_pool(name="outs", bufs=BANKS))
        psum = ctx.enter_context(tc.psum_pool(name="psum", bufs=1))

        def bank(i):
            return psum.tile([P, W], F32, name=f"bank{i}", tag=f"bank{i}")

        ident = keep.tile([P, P], F32, name="ident")
        ident_bf = keep.tile([P, P], BF16, name="ident_bf")
        occ_row = keep.tile([P, O], BF16, name="occ_row")
        scale_sb = keep.tile([P, OT * N // B], F32, name="scale_sb")
        occ_sb = keep.tile([P, OT], BF16, name="occ_sb")
        warm = keep.tile([P, 2], F32, name="warm")
        c_raw = {
            (a, h): keep.tile([P, N // 2], U8, name=f"c_raw{a}{h}", align_bytes=DMA_ALIGN)
            for a in range(OT)
            for h in range(2)
        }
        c_grp = [keep.tile([P, 2, O, 4], BF16, name=f"c_grp{h}", align_bytes=64) for h in range(2)]
        c_codes = [keep.tile([P, O], U32, name=f"c_codes{g}", align_bytes=64) for g in range(G)]
        c_scales = [keep.tile([P, O], U8, name=f"c_scales{g}", align_bytes=64) for g in range(G)]
        h_codes = [keep.tile([P, O], U32, name=f"h_codes{g}", align_bytes=64) for g in range(G)]
        h_scales = [keep.tile([P, O], U8, name=f"h_scales{g}", align_bytes=64) for g in range(G)]
        v_sb = [keep.tile([P, G, 2 * W], U8, name=f"v_sb{n}", align_bytes=DMA_ALIGN) for n in range(V // W)]
        v_scale_sb = keep.tile([P, G, V], U8, name="v_scale_sb", align_bytes=64)

        ctx.enter_context(tc.manual_schedule())

        nc.scalar.dma_start(out=scale_sb[:], in_=c_scale.rearrange("(p a) b -> p (a b)", a=OT))
        raws = {}

        def load_fock(s):
            g, k = divmod(s, G)
            raw = raw_pool.tile([P, 4, W], BF16, name="raw", align_bytes=DMA_ALIGN)
            nc.sync.dma_start(
                out=raw[:], in_=fock[k * W : (k + 1) * W, g * W : (g + 1) * W].rearrange("(p t) n -> p t n", t=4)
            )
            raws[s] = raw

        c_rows = c_bytes.rearrange("(p a) n -> a p n", a=OT)

        def load_c(h):
            for a in range(OT):
                nc.sync.dma_start(out=c_raw[a, h][:], in_=c_rows[a][:, h * N // 2 : (h + 1) * N // 2])

        load_c(0)
        load_c(1)
        load_fock(0)
        load_fock(G)
        nc.sync.dma_start(out=occ_sb[:], in_=occ.rearrange("(p a) -> p a", a=OT))
        load_fock(2 * G)
        load_fock(3)
        nc.vector.memset(warm[:], 0.0)
        make_identity(nc, ident[:])
        make_identity(nc, ident_bf[:])
        nc.scalar.activation(warm[:, 0:1], warm[:, 1:2], COPY, scale=warm[:, 1:2])
        nc.vector.memset(v_scale_sb[:].rearrange("p g n -> p (g n)").bitcast(U32), 0)
        for s in range(G + 1, PIECES):
            if s != 2 * G:
                load_fock(s)
        for q in range(4):
            nc.sync.dma_start(
                out=v_scale_sb[32 * q : 32 * q + 4, :, :].bitcast(I32),
                in_=v_scales[:, 4 * q : 4 * q + 4, :].rearrange("g r n -> r g n").bitcast(I32),
            )
        v_rows = v_words.rearrange("g p n -> p g n")
        for n in range(V // W):
            nc.sync.dma_start(out=v_sb[n][:].bitcast(I32), in_=v_rows[:, :, n * 2 * W : (n + 1) * 2 * W].bitcast(I32))

        c_wide, c_turned = {}, {}

        def widen(a, g):
            wide = wide_pool.tile([P, W], BF16, name="c_wide")
            for b in range(W // B):
                src = c_raw[a, g // 2][:, (g % 2) * W + b * B : (g % 2) * W + (b + 1) * B].bitcast(FP8)
                i = a * (N // B) + (W // B) * g + b
                scale = scale_sb[:, i : i + 1]
                if (a, g) in S_WIDE:
                    nc.scalar.activation(wide[:, b * B : (b + 1) * B], src, COPY, scale=scale)
                else:
                    dst = wide[:].rearrange("p (u m e) -> p m u e", u=2, e=2)[:, 32 * b : 32 * (b + 1)]
                    src = src.rearrange("p (m u e) -> p m u e", u=2, e=2)
                    nc.vector.tensor_scalar(dst, src, scale, None, MULT)
            c_wide[a, g] = wide

        def turn_c(a, h, where):
            xt = bank(where)
            for g2 in range(2):
                words = c_wide[a, 2 * h + g2][:].bitcast(F32)
                for u in range(2):
                    col = 2 * P * g2 + P * u
                    in_ = words[:, u : 2 * P : 2] if (a, 2 * h + g2) in S_WIDE else words[:, P * u : P * (u + 1)]
                    nc.tensor.transpose(xt[:, col : col + P], in_, ident[:])
            c_turned[a, h] = xt

        def untangle_c(a, h):
            out = c_grp[h][:, :, a * P : (a + 1) * P, :].rearrange("p g r t -> p g (r t)").bitcast(F32)
            nc.scalar.copy(
                out.rearrange("p g (r u) -> p g r u", u=2),
                c_turned[a, h][:].rearrange("p (g u r) -> p g r u", g=2, u=2),
            )

        def quantise_c(g):
            nc.vector.quantize_mx(
                out=c_codes[g][:].bitcast(FP8X4),
                scales=c_scales[g][:],
                in_=c_grp[g // 2][:, g % 2].rearrange("p o t -> p (o t)"),
            )

        grps, f_codes, f_scales, mirror_banks = {}, {}, {}, {}

        def new_grp(s):
            if s in (5, 6, 8, 10, 12, 14):
                grps[s] = grp_pool.tile([P, W, 4], BF16, name=f"grp_pair{s // G}", align_bytes=64, bufs=1)
            else:
                grps[s] = grp_pool.tile([P, W, 4], BF16, name="grp", align_bytes=64)

        def turn_mirror(s, first_bank):
            g, k = divmod(s, G)
            for h in range(2):
                xt = bank(first_bank + h)
                for j2 in range(2):
                    words = raws[G * k + g][:, 2 * h + j2, :].bitcast(F32)
                    for u in range(2):
                        col = 2 * P * j2 + P * u
                        nc.tensor.transpose(xt[:, col : col + P], words[:, u : 2 * P : 2], ident[:])
                mirror_banks[s, h] = xt

        def untangle_mirror(s):
            new_grp(s)
            words = grps[s][:].rearrange("p n t -> p (n t)").bitcast(F32)
            words = words.rearrange("p (h j m u) -> p h j m u", h=2, j=2, u=2)
            for h in range(2):
                nc.scalar.copy(words[:, h], mirror_banks[s, h][:].rearrange("p (j u m) -> p j m u", j=2, u=2))

        def scalar_share(s):
            if s == 0:
                return 0
            if s <= G:
                return SHARE_HEAD
            if s == 2 * G - 1:
                return SHARE_SEVEN
            if s % G == 2:
                return W - SHARE_POOL
            return W if s > 2 * G and s % G == 1 else SHARE_USUAL

        def pool_share(s):
            return SHARE_POOL if s > G and s % G == 2 else 0

        def interleave(s, lo, hi, engine_copy):
            if lo == hi:
                return
            if s not in grps:
                new_grp(s)
            src = raws[s][:].rearrange("p t (c i j) -> p c j t i", i=2, j=4)
            dst = grps[s][:].rearrange("p (j c i) t -> p c j t i", i=2, j=4)
            engine_copy(dst[:, lo // 8 : hi // 8], src[:, lo // 8 : hi // 8])

        def vector_copy(out, in_):
            nc.vector.tensor_copy(out=out, in_=in_)

        def scalar_part(s):
            interleave(s, 0, scalar_share(s), nc.scalar.copy)

        def vector_part(s):
            interleave(s, scalar_share(s), W - pool_share(s), vector_copy)

        def pool_part(s):
            lo = W - pool_share(s)
            new_grp(s)
            src = raws[s][:].rearrange("p t (m j) -> p m j t", j=4)
            dst = grps[s][:].rearrange("p (j m) t -> p m j t", j=4)
            nc.gpsimd.tensor_scalar(dst[:, lo // 4 :], src[:, lo // 4 :], 1.0, 0.0, MULT, ADD)

        def quantise_fock(s):
            codes = code_pool.tile([P, W], U32, name="f_codes", align_bytes=64)
            scales = code_pool.tile([P, W], U8, name="f_scales", align_bytes=64)
            nc.vector.quantize_mx(
                out=codes[:].bitcast(FP8X4), scales=scales[:], in_=grps[s][:].rearrange("p n t -> p (n t)")
            )
            f_codes[s], f_scales[s] = codes, scales

        s1_banks, h_grp = {}, {}

        def group_bank(g, i):
            return bank(i if g == 0 else OT + i)

        def block(i):
            return slice(i * P, (i + 1) * P)

        def stage1(s):
            g, k = divmod(s, G)
            if k == 0:
                for i in range(OT):
                    s1_banks[g, i] = group_bank(g, i)
            if g in WIDE:
                steps = [(j, j, slice(0, O), slice(0, W), k == 0, k == LAST) for j in range(4)]
            else:
                steps = [
                    (a, j, block(a), block(j), k == 0 and j == 0, k == LAST and j == 3)
                    for tiles in RUNS[k]
                    for j in range(4)
                    for a in tiles
                ]
            for i, j, orbitals, cols, start, stop in steps:
                nc.tensor.matmul_mx(
                    out=s1_banks[g, i][:, cols],
                    lhsT=f_codes[s][:, j * P : (j + 1) * P].bitcast(FP8X4),
                    lhsT_scale=f_scales[s][:, j * P : (j + 1) * P],
                    rhs=c_codes[k][:, orbitals].bitcast(FP8X4),
                    rhs_scale=c_scales[k][:, orbitals],
                    start=start,
                    stop=stop,
                )

        def weigh(g, a):
            h, a2 = divmod(a, 2)
            if a2 == 0:
                h_grp[g, h] = half_pool.tile([P, HALF, 4], BF16, name="h_grp", align_bytes=64)
            out = h_grp[g, h][:, a2 * P : (a2 + 1) * P, :].rearrange("p (c i) t -> p c t i", i=2)
            sums = s1_banks[g, a][:].rearrange("p (t c i) -> p c t i", t=4, i=2)
            weights = occ_row[:, a * P : (a + 1) * P].rearrange("p (c o i) -> p c o i", o=1, i=2)
            nc.vector.tensor_tensor(out, sums, weights.to_broadcast([P, P // 2, 4, 2]), MULT)

        h_slots = {}

        def weigh_slot(g, t):
            if t == 0:
                h_slots[g] = half_pool.tile([P, 4, O], BF16, name="h_slots")
            nc.vector.tensor_tensor(h_slots[g][:, t, :], s1_banks[g, t][:], occ_row[:], MULT)

        def interleave_half(g, h, lo, hi, engine_copy):
            if (g, h) not in h_grp:
                h_grp[g, h] = half_pool.tile([P, HALF, 4], BF16, name="h_grp", align_bytes=64)
            src = h_slots[g][:, :, HALF * h : HALF * (h + 1)].rearrange("p t (c i) -> p c t i", i=2)
            dst = h_grp[g, h][:].rearrange("p (c i) t -> p c t i", i=2)
            engine_copy(dst[:, lo // 2 : hi // 2], src[:, lo // 2 : hi // 2])

        def quantise_half(g, h):
            cols = slice(HALF * h, HALF * (h + 1))
            nc.vector.quantize_mx(
                out=h_codes[g][:, cols].bitcast(FP8X4),
                scales=h_scales[g][:, cols],
                in_=h_grp[g, h][:].rearrange("p o t -> p (o t)"),
            )

        accs = {}

        def stage2(a, n, passes):
            for g in passes:
                if n == 0:
                    rhs, rhs_scale = c_codes[g][:].bitcast(FP8X4), c_scales[g][:]
                else:
                    rhs = v_sb[n - 1][:, g, :].bitcast(FP4X4)
                    rhs_scale = v_scale_sb[:, g, (n - 1) * W : n * W]
                nc.tensor.matmul_mx(
                    out=accs[a, n][:],
                    lhsT=h_codes[g][:, a * P : (a + 1) * P].bitcast(FP8X4),
                    lhsT_scale=h_scales[g][:, a * P : (a + 1) * P],
                    rhs=rhs,
                    rhs_scale=rhs_scale,
                    start=(g == 0),
                    stop=(g == LAST),
                )

        def f_oo_pass(g):
            for a in range(OT):
                if g == 0:
                    accs[a, 0] = bank(a)
                stage2(a, 0, [g])

        oo_rows = f_oo.rearrange("(p a) n -> a p n", a=OT)
        ov_rows = f_ov.rearrange("(p a) n -> a p n", a=OT)
        in_turn = (vector_copy, nc.scalar.copy)

        def store(a, n, engine_copy, parts):
            res = out_pool.tile([P, W], F32, name="res", align_bytes=DMA_ALIGN)
            if n == 0:
                engine_copy(
                    res[:].rearrange("p (q b) -> p q b", b=OT), accs[a, n][:].rearrange("p (b q) -> p q b", b=OT)
                )
                nc.sync.dma_start(out=oo_rows[a], in_=res[:])
            else:
                width = W // parts
                for c in range(0, W, width):
                    col = (n - 1) * W + c
                    engine_copy(res[:, c : c + width], accs[a, n][:, c : c + width])
                    nc.sync.dma_start(out=ov_rows[a][:, col : col + width], in_=res[:, c : c + width])

        def narrow_part(a, first, width, where, engine_copy):
            acc = bank(where)
            for c in range(first, first + width, P):
                for g in range(G):
                    nc.tensor.matmul_mx(
                        out=acc[:, c - first : c - first + P],
                        lhsT=h_codes[g][:, a * P : (a + 1) * P].bitcast(FP8X4),
                        lhsT_scale=h_scales[g][:, a * P : (a + 1) * P],
                        rhs=v_sb[-1][:, g, 2 * c : 2 * (c + P)].bitcast(FP4X4),
                        rhs_scale=v_scale_sb[:, g, V - W + c : V - W + c + P],
                        start=(g == 0),
                        stop=(g == LAST),
                    )
            res = out_pool.tile([P, W], F32, name="res", align_bytes=DMA_ALIGN)
            engine_copy(res[:, :width], acc[:, :width])
            queue = nc.scalar if first + width == W else nc.sync
            queue.dma_start(out=ov_rows[a][:, V - W + first : V - W + first + width], in_=res[:, :width])

        for a in range(OT):
            widen(a, 0)
            widen(a, 1)
            turn_c(a, 0, a)
        for a in range(OT):
            widen(a, 2)
            widen(a, 3)
            turn_c(a, 1, OT + a)
        for h in range(2):
            for a in range(OT):
                untangle_c(a, h)
        turn_mirror(1, OT)
        untangle_mirror(1)
        turn_mirror(2, OT + 2)
        untangle_mirror(2)
        vector_part(0)
        quantise_c(0)
        quantise_fock(0)
        stage1(0)
        quantise_c(1)
        quantise_c(2)
        scalar_part(3)
        vector_part(3)
        quantise_fock(1)
        stage1(1)
        spread = psum.tile([P, 2 * W], BF16, name="spread", tag="bank4")
        for a in range(OT):
            nc.tensor.matmul(
                spread[:, a * P : (a + 1) * P],
                lhsT=occ_sb[:, a : a + 1].to_broadcast([P, P]),
                rhs=ident_bf[:],
                start=True,
                stop=True,
            )
        quantise_c(3)
        quantise_fock(2)
        stage1(2)
        scalar_part(4)
        vector_part(4)
        quantise_fock(3)
        scalar_part(5)
        vector_part(5)
        nc.scalar.copy(occ_row[:], spread[:, :O])
        quantise_fock(4)
        quantise_fock(5)

        stage1(3)
        pool_part(6)
        for a in range(OT):
            weigh(0, a)
        stage1(4)
        interleave(7, 0, SHARE_USUAL, nc.scalar.copy)
        scalar_part(6)
        stage1(5)
        interleave(7, SHARE_USUAL, SHARE_SEVEN, nc.scalar.copy)
        quantise_fock(6)
        quantise_half(0, 0)

        def finish_group(g):
            s = G * g
            stage1(s + 2)
            vector_part(s + 3)
            scalar_part(s + 4)
            vector_part(s + 4)
            quantise_fock(s + 3)
            quantise_half(g - 1, 1)
            quantise_fock(s + 4)

        def open_group(g, weigh_bank):
            s = G * g
            stage1(s - 1)
            f_oo_pass(g - 2)
            pool_part(s + 2)
            scalar_part(s + 1)
            for i in range(4):
                weigh_bank(g - 1, i)
            stage1(s)
            scalar_part(s + 2)
            quantise_fock(s + 1)
            stage1(s + 1)
            scalar_part(s + 3)

        finish_group(1)
        open_group(2, weigh)
        quantise_half(1, 0)
        quantise_fock(10)
        finish_group(2)
        open_group(3, weigh_slot)
        vector_part(15)
        quantise_fock(14)
        stage1(14)

        interleave_half(2, 1, 0, HALF_SHARE[2], nc.scalar.copy)
        interleave_half(2, 0, 0, HALF, vector_copy)
        quantise_fock(15)
        stage1(15)
        quantise_half(2, 0)
        interleave_half(2, 1, HALF_SHARE[2], HALF, vector_copy)
        quantise_half(2, 1)
        f_oo_pass(2)
        for t in range(4):
            weigh_slot(LAST, t)
        interleave_half(LAST, 1, 0, HALF_SHARE[LAST], nc.scalar.copy)
        interleave_half(LAST, 0, 0, HALF, vector_copy)
        interleave_half(LAST, 1, HALF_SHARE[LAST], HALF, vector_copy)
        quantise_half(LAST, 0)
        quantise_half(LAST, 1)
        for a in range(OT):
            accs[a, 1] = bank(OT + a)
            stage2(a, 1, range(LAST))
        begun = [(a, n) for n in range(2) for a in range(OT)]
        for i, (a, n) in enumerate(begun):
            stage2(a, n, [LAST])
            store(a, n, in_turn[i % 2], 1)
        whole = [(a, n) for n in range(2, 4) for a in range(OT)][:-1]
        for i, (a, n) in enumerate(whole):
            accs[a, n] = bank(i)
            stage2(a, n, range(G))
            store(a, n, in_turn[i % 2], 2 if i == len(whole) - 1 else 1)
        first = 0
        for i, width in enumerate((2 * P, P, P)):
            narrow_part(OT - 1, first, width, (len(whole) + i) % BANKS, in_turn[(i + 1) % 2])
            first = first + width
